import numpy as np
import ml_dtypes


def mxq(x, axis, fmt="e4m3"):
    dtype, down = {"e4m3": (ml_dtypes.float8_e4m3fn, 7), "e5m2": (ml_dtypes.float8_e5m2, 14)}[fmt]
    v = np.moveaxis(np.asarray(x, np.float32).astype(ml_dtypes.bfloat16).astype(np.float64), axis, -1)
    blocks = v.reshape(v.shape[:-1] + (-1, 32))
    amax = np.abs(blocks).max(-1, keepdims=True)
    byte = np.maximum(np.where(amax > 0, np.frexp(amax)[1] - 1 + 127, 0) - down, 1)
    scale = np.exp2(byte - 127.0)
    codes = (blocks / scale).astype(np.float32).astype(dtype).astype(np.float64)
    return np.moveaxis((codes * scale).reshape(v.shape), -1, axis)


WIDE = False


def mx_kscale(k):
    if not WIDE:
        return np.ones(k)
    levels = np.array([24, -24, 12, -12, 0])
    if k % 512:
        return np.exp2(np.random.permutation(np.resize(levels, k // 32))).repeat(32)
    a = np.empty((k // 512, 16))
    for p in range(k // 512):
        a[p, :8] = np.random.permutation(np.resize(levels, 8))
        for g in range(8):
            far = levels[np.abs(levels - a[p, g]) >= 10]
            a[p, g + 8] = far[np.random.randint(len(far))]
    return np.exp2(a.ravel()).repeat(32)


def f64(x):
    return np.asarray(x).astype(np.float64)


def striped(idx):
    return np.tile(idx.reshape(-1, 16).T, (8, 1)).astype(np.uint16)


def unstriped(offs):
    return offs[:16].T.reshape(-1).astype(np.int64)


E2M1 = np.array([0.0, 0.5, 1.0, 1.5, 2.0, 3.0, 4.0, 6.0, -0.0, -0.5, -1.0, -1.5, -2.0, -3.0, -4.0, -6.0])


def pack_weight(w, fmt):
    k, n = w.shape
    w = f64(np.asarray(w, np.float32).astype(ml_dtypes.bfloat16)).reshape(k // 32, 32, n)
    amax = np.abs(w).max(1)
    if fmt == "e4m3":
        byte = np.frexp(amax)[1] - 1 + 127 - 7
    else:
        mant, ex = np.frexp(amax / 6.0)
        byte = np.where(mant > 0.5, ex, ex - 1) + 127
    byte = np.clip(np.where(amax > 0, byte, 1), 1, 254)
    scaled = (w * np.exp2(127.0 - byte)[:, None, :]).reshape(k, n).astype(np.float32)
    by_word = np.ascontiguousarray(scaled.reshape(k // 512, 128, 4, n).transpose(0, 1, 3, 2))
    if fmt == "e4m3":
        words = by_word.astype(ml_dtypes.float8_e4m3fn).view(np.uint8)
    else:
        c = by_word.astype(ml_dtypes.float4_e2m1fn).view(np.uint8) & 0xF
        words = (c[..., 0::2] | (c[..., 1::2] << 4)).reshape(k // 512, 128, 2 * n)
    return np.ascontiguousarray(words), np.ascontiguousarray(byte.astype(np.uint8).reshape(k // 512, 16, n))


def unpack_weight(words, scales, fmt):
    g, _, n = scales.shape
    words = np.ascontiguousarray(words).reshape(g, 128, n, -1)
    if fmt == "e4m3":
        vals = words.view(ml_dtypes.float8_e4m3fn).astype(np.float64)
    else:
        nib = np.empty((g, 128, n, 4), np.uint8)
        nib[..., 0::2] = words & 0xF
        nib[..., 1::2] = words >> 4
        vals = E2M1[nib]
    vals = vals * np.repeat(np.exp2(scales.astype(np.float64) - 127.0), 8, axis=1)[..., None]
    return vals.transpose(0, 1, 3, 2).reshape(g * 512, n)


def pack_table4(v):
    words, scales = pack_weight(v, "e2m1")
    g, t = words.shape[0] // 2, v.shape[1]
    return np.ascontiguousarray(words.reshape(g, 2, 128, t, 2).transpose(0, 2, 3, 1, 4).reshape(g, 128, t, 4)), scales


def unpack_table4(words, scales):
    g, _, t, _ = words.shape
    return unpack_weight(words.reshape(g, 128, t, 2, 2).transpose(0, 3, 1, 2, 4).reshape(2 * g, 128, 2 * t), scales, "e2m1")


def planes(y):
    n, m = y.shape
    v = y.astype(np.float32).astype(ml_dtypes.bfloat16).astype(np.float64).reshape(n // 32, 32, m)
    top = np.abs(v).max(1)
    byte = np.clip(np.where(top > 0, np.frexp(top)[1] - 1 + 127 - 7, 1), 1, 254)
    codes = (v * np.exp2(127.0 - byte)[:, None, :]).reshape(n, m).astype(np.float32).astype(ml_dtypes.float8_e4m3fn).view(np.uint8)
    words = codes.reshape(n // 512, 128, 4, m).transpose(0, 1, 3, 2)
    return np.ascontiguousarray(words), np.ascontiguousarray(byte.astype(np.uint8).reshape(n // 512, 16, m))


def silu(f):
    return f / (1.0 + np.exp(-np.maximum(f, -700.0)))


def sigm(f):
    return 1.0 / (1.0 + np.exp(-np.maximum(f, -700.0)))


K, L, N, T, J = 512, 1024, 512, 2048, 1024


def setup_inputs():
    n = np.random.standard_normal
    s = mx_kscale(K)[:, None]
    s2 = mx_kscale(L)[:, None]
    p_tab = pack_weight(n((K, T)) * s, "e4m3")
    p_tab2 = pack_table4(n((L, T)) * s2)
    p_wv = pack_weight(n((K, N)) / np.sqrt(K) / s, "e4m3")
    p_wt = pack_weight(n((L, N)) / np.sqrt(L) / s2, "e4m3")
    return {
        "tab_words": p_tab[0],
        "tab_scales": p_tab[1],
        "tab2_words": p_tab2[0],
        "tab2_scales": p_tab2[1],
        "zv": (n((K, N)) / np.sqrt(K) / s).astype(np.float32),
        "zt": (n((L, N)) / np.sqrt(L) / s2).astype(np.float32),
        "b": (0.3 * n(N)).astype(np.float32),
        "wv_words": p_wv[0],
        "wv_scales": p_wv[1],
        "wt_words": p_wt[0],
        "wt_scales": p_wt[1],
        "wgo": np.tile(np.random.uniform(0.5, 2.0, J), (128, 1)).astype(np.float32),
        "offs": striped(np.random.permutation(T)[:J]),
        "offs2": striped(np.random.permutation(T)[:J]),
    }


def reference(tab_words, tab_scales, tab2_words, tab2_scales, zv, zt, b, wv_words, wv_scales, wt_words, wt_scales, wgo, offs, offs2):
    idx = unstriped(offs)
    idx2 = unstriped(offs2)
    tab_ = unpack_weight(tab_words, tab_scales, "e4m3")[:, idx]
    tab2_ = unpack_table4(tab2_words, tab2_scales)[:, idx2]
    zv_ = mxq(f64(zv), 0, "e4m3")
    zt_ = mxq(f64(zt), 0, "e4m3")
    z = zv_.T @ tab_ + zt_.T @ tab2_
    gate = sigm(z + f64(b)[:, None])
    wv_ = unpack_weight(wv_words, wv_scales, "e4m3")
    wt_ = unpack_weight(wt_words, wt_scales, "e4m3")
    hv = wv_.T @ tab_
    ht = wt_.T @ tab2_
    av = silu(hv)
    at = silu(ht)
    out = np.zeros((N, T))
    out[:, idx] = f64(wgo)[0] * (at + gate * (av - at))
    return (out,) + planes(out)

@@ -1,0 +1,240 @@
+from contextlib import ExitStack
+
+import concourse.mybir as mybir
+from concourse.masks import make_identity
+
+K, L, N, T, J = 512, 1024, 512, 2048, 1024
+FLOPS = 2 * 2 * (K + L) * N * J
+
+F32 = mybir.dt.float32
+BF16 = mybir.dt.bfloat16
+I32 = mybir.dt.int32
+U32 = mybir.dt.uint32
+U16 = mybir.dt.uint16
+U8 = mybir.dt.uint8
+FP8X4 = mybir.dt.float8_e4m3fn_x4
+FP4X4 = mybir.dt.float4_e2m1fn_x4
+ACT = mybir.ActivationFunctionType
+ALU = mybir.AluOpType
+
+P = 128
+H = 512
+HALVES = J // H
+VCOLS = 896
+
+
+def tile_list_gmu_silu_scatP_kernel(
+    tc, tab_words, tab_scales, tab2_words, tab2_scales, zv, zt, b, wv_words, wv_scales, wt_words, wt_scales,
+    wgo, offs, offs2, out_0, out_1, out_2,
+):
+    nc = tc.nc
+    with ExitStack() as ctx:
+        keep = ctx.enter_context(tc.tile_pool(name="keep", bufs=1))
+        work = ctx.enter_context(tc.tile_pool(name="work", bufs=8))
+        psum = ctx.enter_context(tc.psum_pool(name="psum", bufs=2))
+
+        def kt(name, shape, dtype, tag=None):
+            return keep.tile(shape, dtype, name=name, tag=tag or name, align_bytes=64)
+
+        idx = keep.tile([P, J // 16], U16, name="idx")
+        idx2 = keep.tile([P, J // 16], U16, name="idx2")
+        tabw = kt("tabw", [P, T], U32)
+        tab2w = kt("tab2w", [P, T], U32)
+        tabs = kt("tabs", [P, T], U8)
+        tab2s = kt("tab2s", [P, T], U8)
+        wsraw = kt("wsraw", [P, 2 * N], U8)
+        moved = [kt("moved%d" % h, [P, H], U8) for h in range(HALVES)]
+        pages = [kt("page%d" % t, [P, T], F32) for t in range(2)]
+
+        nc.vector.memset(tabs[:].bitcast(I32), 0)
+        nc.vector.memset(tab2s[:].bitcast(I32), 0)
+        nc.vector.memset(wsraw[:].bitcast(I32), 0)
+        warm = kt("warm", [P, 8], F32)
+        nc.vector.memset(warm[:], 0.0)
+        warm2 = kt("warm2", [P, 8], F32)
+        nc.scalar.activation(warm2[:], warm[:], ACT.Silu)
+        for h in range(HALVES):
+            nc.vector.memset(moved[h][:].bitcast(I32), 0)
+        for t in range(2):
+            nc.vector.memset(pages[t][:].bitcast(I32), 0)
+        ident = kt("ident", [P, P], F32)
+        make_identity(nc, ident[:])
+
+        zraw = [kt("zraw0", [P, 4, N], F32), kt("zraw1", [P, 4, N], F32),
+                kt("zraw2a", [P, 4, N // 2], F32), kt("zraw2b", [P, 4, N // 2], F32)]
+        wvraw = kt("wvraw", [P, N], I32)
+        wtraw = kt("wtraw", [P, 2, N], I32)
+        wrows = kt("wrows", [P, P], F32)
+        braw = kt("braw", [P, 4], F32)
+
+        def words(ap):
+            return ap.rearrange("p n i -> p (n i)").bitcast(I32)
+
+        def rows(ap):
+            return ap.rearrange("(p j) n -> p j n", j=4)
+
+        dma = nc.sync.dma_start
+        dma(out=tabw[:].bitcast(I32), in_=words(tab_words[0]))
+        dma(out=zraw[0][:], in_=rows(zv))
+        dma(out=idx[:], in_=offs)
+        dma(out=idx2[:], in_=offs2)
+        for q in range(4):
+            dma(out=tabs[32 * q : 32 * q + 4, :].bitcast(I32), in_=tab_scales[0, 4 * q : 4 * q + 4, :].bitcast(I32))
+        dma(out=tab2w[:].bitcast(I32), in_=words(tab2_words[0]))
+        dma(out=wtraw[:], in_=wt_words.rearrange("a p n i -> p a (n i)").bitcast(I32))
+        dma(out=wvraw[:], in_=words(wv_words[0]))
+        for q in range(4):
+            dma(out=tab2s[32 * q : 32 * q + 8, :].bitcast(I32), in_=tab2_scales[:, 4 * q : 4 * q + 4, :].bitcast(I32))
+        dma(out=wrows[:], in_=wgo[0:16, :].rearrange("r (i n) -> (r i) n", n=P))
+        dma(out=zraw[1][:], in_=rows(zt[0:512, :]))
+        for q in range(4):
+            dma(
+                out=wsraw[32 * q : 32 * q + 4, :].bitcast(I32).rearrange("r (a n) -> r a n", a=2),
+                in_=wt_scales[:, 4 * q : 4 * q + 4, :].bitcast(I32).rearrange("a r n -> r a n"),
+            )
+        dma(out=zraw[2][:], in_=rows(zt[512:1024, :])[:, :, 0 : N // 2])
+        dma(out=zraw[3][:], in_=rows(zt[512:1024, :])[:, :, N // 2 : N])
+        for q in range(4):
+            dma(out=wsraw[32 * q + 4 : 32 * q + 8, 0:N].bitcast(I32), in_=wv_scales[0, 4 * q : 4 * q + 4, :].bitcast(I32))
+        dma(out=braw[:], in_=b.rearrange("(p t) -> p t", t=4))
+
+        gv = [kt("gv%d" % h, [P, H], U32) for h in range(HALVES)]
+        gvs = [kt("gvs%d" % h, [P, H], U8) for h in range(HALVES)]
+        g2 = [kt("g20", [P, H], U32)]
+        g2s = [kt("g2s0", [P, H], U8)]
+        part = [kt("part%d" % h, [P, 2, 2 * H], U8) for h in range(HALVES)]
+
+        def cols(lst, h):
+            return lst[:, h * (H // 16) : (h + 1) * (H // 16)]
+
+        def gather(h):
+            nc.vector.tensor_copy(gv[h][:], tabw[:].indirect(cols(idx, h)))
+            nc.vector.tensor_copy(gvs[h][:], tabs[:].indirect(cols(idx, h)))
+            nc.vector.tensor_copy(g2[h][:], tab2w[:].indirect(cols(idx2, h)))
+            nc.vector.tensor_copy(g2s[h][:], tab2s[:].indirect(cols(idx2, h)))
+            nc.gpsimd.dma_start(out=moved[h][0 : P - 4, :].bitcast(I32), in_=g2s[h][4:P, :].bitcast(I32))
+            nc.vector.tensor_copy(
+                part[h][:].bitcast(U16), g2[h][:].bitcast(U16).rearrange("p (j d) -> p d j", d=2)
+            )
+
+        gather(0)
+
+        zb = [kt("zb%d" % a, [P, 4 * N], BF16) for a in range(3)]
+        zc = [kt("zc%d" % a, [P, N], U32) for a in range(3)]
+        zs = [kt("zs%d" % a, [P, N], U8) for a in range(3)]
+
+        def cast(a, raw, m0, m1):
+            nc.scalar.copy(
+                zb[a][:].rearrange("p (t m j) -> p m t j", t=4, j=4)[:, m0:m1],
+                raw[:].rearrange("p j (m t) -> p m t j", t=4),
+            )
+
+        def quant(a, c0, c1):
+            nc.vector.quantize_mx(zc[a][:, c0:c1].bitcast(FP8X4), zs[a][:, c0:c1], zb[a][:, 4 * c0 : 4 * c1])
+
+        def late_page(t, tag):
+            pages.append(kt("page%d" % t, [P, T], F32, tag))
+            for c in range(0, T, 1024):
+                nc.gpsimd.memset(pages[t][:, c : c + 1024], 0.0)
+
+        cast(0, zraw[0], 0, P)
+        late_page(2, "zraw0")
+        quant(0, 0, N)
+
+        wp = kt("wp", [P, 3, N], I32)
+        wsp = kt("wsp", [P, 2 * N], U8)
+        nc.vector.tensor_copy(
+            wp[:, 1:3, :].rearrange("p a (t m i) -> p a m t i", t=4, i=4),
+            wtraw[:].rearrange("p a (m i t) -> p a m t i", t=4, i=4),
+        )
+        nc.vector.tensor_copy(
+            wp[:, 0, :].rearrange("p (t m i) -> p m t i", t=4, i=4),
+            wvraw[:].rearrange("p (m i t) -> p m t i", t=4, i=4),
+        )
+        cast(1, zraw[1], 0, P)
+        late_page(3, "zraw1")
+        quant(1, 0, N)
+        nc.vector.tensor_copy(
+            wsp[:].rearrange("p (a t m) -> p a t m", a=2, t=4),
+            wsraw[:].rearrange("p (a m t) -> p a t m", a=2, t=4),
+        )
+        cast(2, zraw[2], 0, P // 2)
+        cast(2, zraw[3], P // 2, P)
+        quant(2, 0, N // 2)
+        quant(2, N // 2, N)
+
+        halfb = kt("halfb", [P, 4], F32, "grouped")
+        nc.vector.tensor_scalar(halfb[:], braw[:], 0.5, None, ALU.mult)
+
+        turned = psum.tile([P, H], F32, name="turned", tag="z")
+        nc.tensor.transpose(turned[:, 0:P], wrows[:], ident[:])
+        wcol = kt("wcol", [P, 8], F32)
+        nc.scalar.copy(wcol[:], turned[:, 0:8])
+        wps = [psum.tile([P, H], F32, name="wps%d" % h, tag="w") for h in range(HALVES)]
+        for i in range(8):
+            nc.tensor.transpose(
+                wps[i // 4][:, (i % 4) * P : (i % 4 + 1) * P], wcol[:, i : i + 1].to_broadcast([P, P]), ident[:]
+            )
+
+        g2.append(kt("g21", [P, H], U32, "zraw2b"))
+        g2s.append(kt("g2s1", [P, H], U8, "zraw2a"))
+        gather(1)
+
+        stage = kt("stage", [P, 2, T], F32)
+        out_rows = out_0.rearrange("(p t) c -> p t c", t=4)
+
+        for t in range(4):
+            tc_ = slice(t * P, (t + 1) * P)
+            for h in range(HALVES):
+                fp4 = [part[h][:, a, :].bitcast(FP4X4) for a in range(2)]
+                fp4s = [g2s[h][:], moved[h][:]]
+                hv = psum.tile([P, H], F32, name="hv", tag="hv")
+                nc.tensor.matmul_mx(hv[:], wp[:, 0, tc_].bitcast(FP8X4), wsp[4:P, tc_], gv[h][:].bitcast(FP8X4), gvs[h][:],
+                                    start=True, stop=True)
+                ht = psum.tile([P, H], F32, name="ht", tag="ht")
+                for a in range(2):
+                    nc.tensor.matmul_mx(ht[:], wp[:, 1 + a, tc_].bitcast(FP8X4), wsp[:, a * N + t * P : a * N + (t + 1) * P],
+                                        fp4[a], fp4s[a], start=(a == 0), stop=(a == 1))
+                z = psum.tile([P, H], F32, name="z", tag="z")
+                nc.tensor.matmul_mx(z[:], zc[0][:, tc_].bitcast(FP8X4), zs[0][:, tc_], gv[h][:].bitcast(FP8X4), gvs[h][:],
+                                    start=True, stop=False)
+                for a in range(2):
+                    nc.tensor.matmul_mx(z[:], zc[1 + a][:, tc_].bitcast(FP8X4), zs[1 + a][:, tc_], fp4[a], fp4s[a],
+                                        start=False, stop=(a == 1))
+                av = work.tile([P, H], F32, name="av")
+                at = work.tile([P, H], F32, name="at")
+                th = work.tile([P, H], F32, name="th")
+                nc.scalar.activation(av[:], hv[:], ACT.Silu)
+                nc.scalar.activation(at[:], ht[:], ACT.Silu)
+                nc.scalar.activation(th[:], z[:], ACT.Tanh, bias=halfb[:, t : t + 1], scale=0.5)
+                nc.gpsimd.tensor_tensor(av[:], av[:], at[:], ALU.subtract)
+                nc.scalar.activation(th[:], th[:], ACT.Identity, bias=0.5, scale=0.5)
+                nc.gpsimd.tensor_tensor(av[:], av[:], th[:], ALU.mult)
+                nc.gpsimd.tensor_tensor(av[:], av[:], at[:], ALU.add)
+                fw = work.tile([P, H], F32, name="fw", bufs=2)
+                nc.vector.tensor_tensor(fw[:], av[:], wps[h][:], ALU.mult)
+                nc.vector.tensor_copy(pages[t][:].indirect(cols(idx, h)), fw[:])
+            if t < 2:
+                dma(out=stage[:, t, :], in_=pages[t][:])
+            dma(out=out_rows[:, t, :], in_=pages[t][:])
+
+        grouped = kt("grouped", [P, 4 * T], BF16)
+        g4 = grouped[:].rearrange("p (c t) -> p c t", t=4)
+        nc.scalar.copy(g4[:, :, 0:2], stage[:].rearrange("p t c -> p c t"))
+        nc.scalar.copy(g4[:, :, 2:4], pages[2][:].unsqueeze(2).to_broadcast([P, T, 2]))
+
+        nc.vector.tensor_copy(g4[:, 0:512, 3], pages[3][:, 0:512])
+        nc.scalar.copy(g4[:, VCOLS:1024, 3], pages[3][:, VCOLS:1024])
+        nc.vector.tensor_copy(g4[:, 512:VCOLS, 3], pages[3][:, 512:VCOLS])
+        nc.scalar.copy(g4[:, 1024:1536, 3], pages[3][:, 1024:1536])
+        nc.scalar.copy(g4[:, 1536:T, 3], pages[3][:, 1536:T])
+        ocodes = kt("ocodes", [P, T], U32)
+        oscale = kt("oscale", [P, T], U8)
+        ow = words(out_1[0])
+        for c in range(4):
+            cs = slice(512 * c, 512 * (c + 1))
+            nc.vector.quantize_mx(ocodes[:, cs].bitcast(FP8X4), oscale[:, cs], grouped[:, 2048 * c : 2048 * (c + 1)])
+            dma(out=ow[:, cs], in_=ocodes[:, cs].bitcast(I32))
+        for q in range(4):
+            eng = nc.scalar if q % 2 else nc.sync
+            eng.dma_start(out=out_2[0, 4 * q : 4 * q + 4, :].bitcast(I32), in_=oscale[32 * q : 32 * q + 4, :].bitcast(I32))

@@ -18,9 +18,16 @@ ACT = mybir.ActivationFunctionType
 ALU = mybir.AluOpType
 
 P = 128
-H = 512
-HALVES = J // H
-VCOLS = 896
+PACK = 4
+QUADS = 4
+HALF = 512
+HALVES = J // HALF
+CHUNK = 512
+CHUNKS = T // CHUNK
+CLEAR = 1024
+VECTOR_CHUNKS = 2
+
+STEPS = [(0, 0), (1, 0), (0, 1), (1, 1), (2, 0), (2, 1), (3, 0), (3, 1)]
 
 
 def tile_list_gmu_silu_scatP_kernel(
@@ -30,211 +37,245 @@ def tile_list_gmu_silu_scatP_kernel(
     nc = tc.nc
     with ExitStack() as ctx:
         keep = ctx.enter_context(tc.tile_pool(name="keep", bufs=1))
-        work = ctx.enter_context(tc.tile_pool(name="work", bufs=8))
+        work = ctx.enter_context(tc.tile_pool(name="work", bufs=2))
         psum = ctx.enter_context(tc.psum_pool(name="psum", bufs=2))
 
-        def kt(name, shape, dtype, tag=None):
-            return keep.tile(shape, dtype, name=name, tag=tag or name, align_bytes=64)
+        def sbuf(name, shape, dtype, after=None):
+            return keep.tile(shape, dtype, name=name, tag=after or name, align_bytes=64)
+
+        def as_words(ap):
+            return ap.rearrange("p n i -> p (n i)").bitcast(I32)
+
+        def by_partition(ap):
+            return ap.rearrange("(p i) n -> p i n", i=PACK)
+
+        def entries(list_tile, j0, count):
+            return list_tile[:, j0 // 16 : (j0 + count) // 16]
+
+        dma = nc.sync.dma_start
 
         idx = keep.tile([P, J // 16], U16, name="idx")
         idx2 = keep.tile([P, J // 16], U16, name="idx2")
-        tabw = kt("tabw", [P, T], U32)
-        tab2w = kt("tab2w", [P, T], U32)
-        tabs = kt("tabs", [P, T], U8)
-        tab2s = kt("tab2s", [P, T], U8)
-        wsraw = kt("wsraw", [P, 2 * N], U8)
-        moved = [kt("moved%d" % h, [P, H], U8) for h in range(HALVES)]
-        pages = [kt("page%d" % t, [P, T], F32) for t in range(2)]
+        tab_w = sbuf("tab_w", [P, T], U32)
+        tab2_w = sbuf("tab2_w", [P, T], U32)
+        tab_s = sbuf("tab_s", [P, T], U8)
+        tab2_s = sbuf("tab2_s", [P, T], U8)
+        w_s_raw = sbuf("w_s_raw", [P, 2 * N], U8)
+        lowered = [sbuf("lowered%d" % h, [P, HALF], U8) for h in range(HALVES)]
+        pages = [sbuf("page%d" % t, [P, T], F32) for t in range(PACK)]
 
-        nc.vector.memset(tabs[:].bitcast(I32), 0)
-        nc.vector.memset(tab2s[:].bitcast(I32), 0)
-        nc.vector.memset(wsraw[:].bitcast(I32), 0)
-        warm = kt("warm", [P, 8], F32)
-        nc.vector.memset(warm[:], 0.0)
-        warm2 = kt("warm2", [P, 8], F32)
-        nc.scalar.activation(warm2[:], warm[:], ACT.Silu)
+        nc.gpsimd.memset(tab_s[:].bitcast(I32), 0)
+        nc.gpsimd.memset(w_s_raw[:].bitcast(I32), 0)
+        nc.vector.memset(tab2_s[:].bitcast(I32), 0)
+        zero = sbuf("zero", [P, 1], F32)
+        nc.vector.memset(zero[:], 0.0)
+        no_bias = sbuf("no_bias", [P, 1], F32)
+        nc.scalar.activation(no_bias[:], zero[:], ACT.Silu)
         for h in range(HALVES):
-            nc.vector.memset(moved[h][:].bitcast(I32), 0)
+            nc.vector.memset(lowered[h][:].bitcast(I32), 0)
         for t in range(2):
             nc.vector.memset(pages[t][:].bitcast(I32), 0)
-        ident = kt("ident", [P, P], F32)
+        ident = sbuf("ident", [P, P], F32)
         make_identity(nc, ident[:])
 
-        zraw = [kt("zraw0", [P, 4, N], F32), kt("zraw1", [P, 4, N], F32),
-                kt("zraw2a", [P, 4, N // 2], F32), kt("zraw2b", [P, 4, N // 2], F32)]
-        wvraw = kt("wvraw", [P, N], I32)
-        wtraw = kt("wtraw", [P, 2, N], I32)
-        wrows = kt("wrows", [P, P], F32)
-        braw = kt("braw", [P, 4], F32)
+        zv_raw = sbuf("zv_raw", [P, PACK, N], F32)
+        zt0_raw = sbuf("zt0_raw", [P, PACK, N], F32)
+        wv_raw = sbuf("wv_raw", [P, N], I32)
+        wt_raw = sbuf("wt_raw", [P, 2, N], I32)
+        wgo_rows = sbuf("wgo_rows", [P, P], F32)
+        b_raw = sbuf("b_raw", [P, PACK], F32)
 
-        def words(ap):
-            return ap.rearrange("p n i -> p (n i)").bitcast(I32)
+        def load_wv_scales(q):
+            dma(out=w_s_raw[32 * q + 4 : 32 * q + 8, 0:N].bitcast(I32), in_=wv_scales[0, 4 * q : 4 * q + 4, :].bitcast(I32))
 
-        def rows(ap):
-            return ap.rearrange("(p j) n -> p j n", j=4)
-
-        dma = nc.sync.dma_start
-        dma(out=tabw[:].bitcast(I32), in_=words(tab_words[0]))
-        dma(out=zraw[0][:], in_=rows(zv))
         dma(out=idx[:], in_=offs)
+        dma(out=tab_w[:].bitcast(I32), in_=as_words(tab_words[0]))
         dma(out=idx2[:], in_=offs2)
-        for q in range(4):
-            dma(out=tabs[32 * q : 32 * q + 4, :].bitcast(I32), in_=tab_scales[0, 4 * q : 4 * q + 4, :].bitcast(I32))
-        dma(out=tab2w[:].bitcast(I32), in_=words(tab2_words[0]))
-        dma(out=wtraw[:], in_=wt_words.rearrange("a p n i -> p a (n i)").bitcast(I32))
-        dma(out=wvraw[:], in_=words(wv_words[0]))
-        for q in range(4):
-            dma(out=tab2s[32 * q : 32 * q + 8, :].bitcast(I32), in_=tab2_scales[:, 4 * q : 4 * q + 4, :].bitcast(I32))
-        dma(out=wrows[:], in_=wgo[0:16, :].rearrange("r (i n) -> (r i) n", n=P))
-        dma(out=zraw[1][:], in_=rows(zt[0:512, :]))
-        for q in range(4):
+        for q in range(QUADS):
+            dma(out=tab_s[32 * q : 32 * q + 4, :].bitcast(I32), in_=tab_scales[0, 4 * q : 4 * q + 4, :].bitcast(I32))
+        dma(out=zv_raw[:], in_=by_partition(zv))
+        dma(out=tab2_w[:].bitcast(I32), in_=as_words(tab2_words[0]))
+        for q in range(QUADS):
+            dma(out=tab2_s[32 * q : 32 * q + 8, :].bitcast(I32), in_=tab2_scales[:, 4 * q : 4 * q + 4, :].bitcast(I32))
+        for q in range(QUADS // 2):
+            load_wv_scales(q)
+        dma(out=zt0_raw[:], in_=by_partition(zt[0:512, :]))
+        dma(out=wt_raw[:], in_=wt_words.rearrange("a p n i -> p a (n i)").bitcast(I32))
+        dma(out=wv_raw[:], in_=as_words(wv_words[0]))
+        for q in range(QUADS // 2, QUADS):
+            load_wv_scales(q)
+        for q in range(QUADS):
             dma(
-                out=wsraw[32 * q : 32 * q + 4, :].bitcast(I32).rearrange("r (a n) -> r a n", a=2),
+                out=w_s_raw[32 * q : 32 * q + 4, :].bitcast(I32).rearrange("r (a n) -> r a n", a=2),
                 in_=wt_scales[:, 4 * q : 4 * q + 4, :].bitcast(I32).rearrange("a r n -> r a n"),
             )
-        dma(out=zraw[2][:], in_=rows(zt[512:1024, :])[:, :, 0 : N // 2])
-        dma(out=zraw[3][:], in_=rows(zt[512:1024, :])[:, :, N // 2 : N])
-        for q in range(4):
-            dma(out=wsraw[32 * q + 4 : 32 * q + 8, 0:N].bitcast(I32), in_=wv_scales[0, 4 * q : 4 * q + 4, :].bitcast(I32))
-        dma(out=braw[:], in_=b.rearrange("(p t) -> p t", t=4))
+        nc.gpsimd.dma_start(out=wgo_rows[:], in_=wgo[0:16, :].rearrange("r (i n) -> (r i) n", n=P))
+        nc.gpsimd.dma_start(out=b_raw[:], in_=b.rearrange("(p t) -> p t", t=PACK))
+        for t in range(2, PACK):
+            for c in range(0, T, CLEAR):
+                nc.gpsimd.memset(pages[t][:, c : c + CLEAR], 0.0)
 
-        gv = [kt("gv%d" % h, [P, H], U32) for h in range(HALVES)]
-        gvs = [kt("gvs%d" % h, [P, H], U8) for h in range(HALVES)]
-        g2 = [kt("g20", [P, H], U32)]
-        g2s = [kt("g2s0", [P, H], U8)]
-        part = [kt("part%d" % h, [P, 2, 2 * H], U8) for h in range(HALVES)]
+        v_w = [sbuf("v_w%d" % h, [P, HALF], U32) for h in range(HALVES)]
+        v2_w = [sbuf("v2_w%d" % h, [P, 2, 2 * HALF], U8) for h in range(HALVES)]
+        v_s, v2_s = [], []
 
-        def cols(lst, h):
-            return lst[:, h * (H // 16) : (h + 1) * (H // 16)]
+        def gather_v_words(h):
+            nc.vector.tensor_copy(v_w[h][:], tab_w[:].indirect(entries(idx, h * HALF, HALF)))
 
-        def gather(h):
-            nc.vector.tensor_copy(gv[h][:], tabw[:].indirect(cols(idx, h)))
-            nc.vector.tensor_copy(gvs[h][:], tabs[:].indirect(cols(idx, h)))
-            nc.vector.tensor_copy(g2[h][:], tab2w[:].indirect(cols(idx2, h)))
-            nc.vector.tensor_copy(g2s[h][:], tab2s[:].indirect(cols(idx2, h)))
-            nc.gpsimd.dma_start(out=moved[h][0 : P - 4, :].bitcast(I32), in_=g2s[h][4:P, :].bitcast(I32))
-            nc.vector.tensor_copy(
-                part[h][:].bitcast(U16), g2[h][:].bitcast(U16).rearrange("p (j d) -> p d j", d=2)
-            )
+        def gather_v_scales(h, after=None):
+            v_s.append(sbuf("v_s%d" % h, [P, HALF], U8, after))
+            nc.vector.tensor_copy(v_s[h][:], tab_s[:].indirect(entries(idx, h * HALF, HALF)))
 
-        gather(0)
+        def gather_v2_scales(h, queue, after=None):
+            v2_s.append(sbuf("v2_s%d" % h, [P, HALF], U8, after))
+            nc.vector.tensor_copy(v2_s[h][:], tab2_s[:].indirect(entries(idx2, h * HALF, HALF)))
+            queue.dma_start(out=lowered[h][0 : P - 4, :].bitcast(I32), in_=v2_s[h][4:P, :].bitcast(I32))
 
-        zb = [kt("zb%d" % a, [P, 4 * N], BF16) for a in range(3)]
-        zc = [kt("zc%d" % a, [P, N], U32) for a in range(3)]
-        zs = [kt("zs%d" % a, [P, N], U8) for a in range(3)]
+        def gather_v2_words(h, after=None):
+            pairs = sbuf("pairs%d" % h, [P, HALF], U32, after)
+            nc.vector.tensor_copy(pairs[:], tab2_w[:].indirect(entries(idx2, h * HALF, HALF)))
+            nc.vector.tensor_copy(v2_w[h][:].bitcast(U16), pairs[:].bitcast(U16).rearrange("p (j d) -> p d j", d=2))
 
-        def cast(a, raw, m0, m1):
+        gather_v_words(0)
+        gather_v_scales(0)
+        gather_v_words(1)
+        zt1_raw = by_partition(zt[512:1024, :])
+        zt1_low = sbuf("zt1_low", [P, PACK, N // 2], F32, "tab_w")
+        dma(out=zt1_low[:], in_=zt1_raw[:, :, 0 : N // 2])
+        gather_v2_scales(0, nc.gpsimd)
+        gather_v2_words(0)
+
+        z_bf = [sbuf("z_bf%d" % a, [P, PACK * N], BF16) for a in range(3)]
+        z_w = [sbuf("z_w%d" % a, [P, N], U32) for a in range(3)]
+        z_s = [sbuf("z_s%d" % a, [P, N], U8) for a in range(3)]
+
+        def round_and_deal(a, raw, m0, m1):
             nc.scalar.copy(
-                zb[a][:].rearrange("p (t m j) -> p m t j", t=4, j=4)[:, m0:m1],
-                raw[:].rearrange("p j (m t) -> p m t j", t=4),
+                z_bf[a][:].rearrange("p (t m i) -> p m t i", t=PACK, i=PACK)[:, m0:m1],
+                raw[:].rearrange("p i (m t) -> p m t i", t=PACK),
             )
 
-        def quant(a, c0, c1):
-            nc.vector.quantize_mx(zc[a][:, c0:c1].bitcast(FP8X4), zs[a][:, c0:c1], zb[a][:, 4 * c0 : 4 * c1])
+        def quantise_z(a, c0, c1):
+            nc.vector.quantize_mx(z_w[a][:, c0:c1].bitcast(FP8X4), z_s[a][:, c0:c1], z_bf[a][:, PACK * c0 : PACK * c1])
 
-        def late_page(t, tag):
-            pages.append(kt("page%d" % t, [P, T], F32, tag))
-            for c in range(0, T, 1024):
-                nc.gpsimd.memset(pages[t][:, c : c + 1024], 0.0)
+        round_and_deal(0, zv_raw, 0, P)
+        zt1_high = sbuf("zt1_high", [P, PACK, N // 2], F32, "zv_raw")
+        dma(out=zt1_high[:], in_=zt1_raw[:, :, N // 2 : N])
+        quantise_z(0, 0, N)
+        gather_v_scales(1, "z_bf0")
 
-        cast(0, zraw[0], 0, P)
-        late_page(2, "zraw0")
-        quant(0, 0, N)
+        turned = psum.tile([P, HALF], F32, name="turned", tag="z", bufs=1)
+        nc.tensor.transpose(turned[:, 0:P], wgo_rows[:], ident[:])
+        wgo_cols = sbuf("wgo_cols", [P, J // P], F32, "pairs0")
+        nc.scalar.copy(wgo_cols[:], turned[:, 0 : J // P])
+        wgo_ps = [psum.tile([P, HALF], F32, name="wgo_ps%d" % h, tag="wgo") for h in range(HALVES)]
+        for i in range(J // P):
+            h, c = divmod(i * P, HALF)
+            nc.tensor.transpose(wgo_ps[h][:, c : c + P], wgo_cols[:, i : i + 1].to_broadcast([P, P]), ident[:])
 
-        wp = kt("wp", [P, 3, N], I32)
-        wsp = kt("wsp", [P, 2 * N], U8)
-        nc.vector.tensor_copy(
-            wp[:, 1:3, :].rearrange("p a (t m i) -> p a m t i", t=4, i=4),
-            wtraw[:].rearrange("p a (m i t) -> p a m t i", t=4, i=4),
-        )
-        nc.vector.tensor_copy(
-            wp[:, 0, :].rearrange("p (t m i) -> p m t i", t=4, i=4),
-            wvraw[:].rearrange("p (m i t) -> p m t i", t=4, i=4),
-        )
-        cast(1, zraw[1], 0, P)
-        late_page(3, "zraw1")
-        quant(1, 0, N)
-        nc.vector.tensor_copy(
-            wsp[:].rearrange("p (a t m) -> p a t m", a=2, t=4),
-            wsraw[:].rearrange("p (a m t) -> p a t m", a=2, t=4),
-        )
-        cast(2, zraw[2], 0, P // 2)
-        cast(2, zraw[3], P // 2, P)
-        quant(2, 0, N // 2)
-        quant(2, N // 2, N)
+        w_w, w_s = {}, {}
 
-        halfb = kt("halfb", [P, 4], F32, "grouped")
-        nc.vector.tensor_scalar(halfb[:], braw[:], 0.5, None, ALU.mult)
-
-        turned = psum.tile([P, H], F32, name="turned", tag="z")
-        nc.tensor.transpose(turned[:, 0:P], wrows[:], ident[:])
-        wcol = kt("wcol", [P, 8], F32)
-        nc.scalar.copy(wcol[:], turned[:, 0:8])
-        wps = [psum.tile([P, H], F32, name="wps%d" % h, tag="w") for h in range(HALVES)]
-        for i in range(8):
-            nc.tensor.transpose(
-                wps[i // 4][:, (i % 4) * P : (i % 4 + 1) * P], wcol[:, i : i + 1].to_broadcast([P, P]), ident[:]
+        def deal_weights(t0, t1, words_after=None, scales_after=None):
+            dealt_w = sbuf("dealt_w%d" % t0, [P, 3, t1 - t0, P], I32, words_after)
+            dealt_s = sbuf("dealt_s%d" % t0, [P, 2, t1 - t0, P], U8, scales_after)
+            nc.vector.tensor_copy(
+                dealt_w[:, 0].rearrange("p t (g e) -> p g t e", e=4),
+                wv_raw[:].rearrange("p (g e t) -> p g t e", t=PACK, e=4)[:, :, t0:t1],
             )
+            nc.vector.tensor_copy(
+                dealt_w[:, 1:3].rearrange("p a t (g e) -> p a g t e", e=4),
+                wt_raw[:].rearrange("p a (g e t) -> p a g t e", t=PACK, e=4)[:, :, :, t0:t1],
+            )
+            nc.vector.tensor_copy(dealt_s[:], w_s_raw[:].rearrange("p (a m t) -> p a t m", a=2, t=PACK)[:, :, t0:t1])
+            for t in range(t0, t1):
+                w_w[t] = dealt_w[:, :, t - t0]
+                w_s[t] = dealt_s[:, :, t - t0]
 
-        g2.append(kt("g21", [P, H], U32, "zraw2b"))
-        g2s.append(kt("g2s1", [P, H], U8, "zraw2a"))
-        gather(1)
+        deal_weights(0, 1)
+        round_and_deal(1, zt0_raw, 0, P)
+        quantise_z(1, 0, N)
+        gather_v2_scales(1, nc.sync, "z_bf1")
+        round_and_deal(2, zt1_low, 0, P // 2)
+        round_and_deal(2, zt1_high, P // 2, P)
+        quantise_z(2, 0, P)
+        deal_weights(1, PACK, "zv_raw", "zt0_raw")
+        quantise_z(2, P, 2 * P)
+        quantise_z(2, 2 * P, N)
 
-        stage = kt("stage", [P, 2, T], F32)
-        out_rows = out_0.rearrange("(p t) c -> p t c", t=4)
+        half_b = sbuf("half_b", [P, PACK], F32)
+        nc.vector.tensor_scalar(half_b[:], b_raw[:], 0.5, None, ALU.mult)
+        gather_v2_words(1, "tab_w")
 
-        for t in range(4):
-            tc_ = slice(t * P, (t + 1) * P)
-            for h in range(HALVES):
-                fp4 = [part[h][:, a, :].bitcast(FP4X4) for a in range(2)]
-                fp4s = [g2s[h][:], moved[h][:]]
-                hv = psum.tile([P, H], F32, name="hv", tag="hv")
-                nc.tensor.matmul_mx(hv[:], wp[:, 0, tc_].bitcast(FP8X4), wsp[4:P, tc_], gv[h][:].bitcast(FP8X4), gvs[h][:],
-                                    start=True, stop=True)
-                ht = psum.tile([P, H], F32, name="ht", tag="ht")
-                for a in range(2):
-                    nc.tensor.matmul_mx(ht[:], wp[:, 1 + a, tc_].bitcast(FP8X4), wsp[:, a * N + t * P : a * N + (t + 1) * P],
-                                        fp4[a], fp4s[a], start=(a == 0), stop=(a == 1))
-                z = psum.tile([P, H], F32, name="z", tag="z")
-                nc.tensor.matmul_mx(z[:], zc[0][:, tc_].bitcast(FP8X4), zs[0][:, tc_], gv[h][:].bitcast(FP8X4), gvs[h][:],
-                                    start=True, stop=False)
-                for a in range(2):
-                    nc.tensor.matmul_mx(z[:], zc[1 + a][:, tc_].bitcast(FP8X4), zs[1 + a][:, tc_], fp4[a], fp4s[a],
-                                        start=False, stop=(a == 1))
-                av = work.tile([P, H], F32, name="av")
-                at = work.tile([P, H], F32, name="at")
-                th = work.tile([P, H], F32, name="th")
-                nc.scalar.activation(av[:], hv[:], ACT.Silu)
-                nc.scalar.activation(at[:], ht[:], ACT.Silu)
-                nc.scalar.activation(th[:], z[:], ACT.Tanh, bias=halfb[:, t : t + 1], scale=0.5)
-                nc.gpsimd.tensor_tensor(av[:], av[:], at[:], ALU.subtract)
-                nc.scalar.activation(th[:], th[:], ACT.Identity, bias=0.5, scale=0.5)
-                nc.gpsimd.tensor_tensor(av[:], av[:], th[:], ALU.mult)
-                nc.gpsimd.tensor_tensor(av[:], av[:], at[:], ALU.add)
-                fw = work.tile([P, H], F32, name="fw", bufs=2)
-                nc.vector.tensor_tensor(fw[:], av[:], wps[h][:], ALU.mult)
-                nc.vector.tensor_copy(pages[t][:].indirect(cols(idx, h)), fw[:])
-            if t < 2:
-                dma(out=stage[:, t, :], in_=pages[t][:])
-            dma(out=out_rows[:, t, :], in_=pages[t][:])
+        staged = [sbuf("staged%d" % c, [P, 2, CHUNK], F32) for c in range(CHUNKS)]
+        out_rows = out_0.rearrange("(p t) c -> p t c", t=PACK)
 
-        grouped = kt("grouped", [P, 4 * T], BF16)
-        g4 = grouped[:].rearrange("p (c t) -> p c t", t=4)
-        nc.scalar.copy(g4[:, :, 0:2], stage[:].rearrange("p t c -> p c t"))
-        nc.scalar.copy(g4[:, :, 2:4], pages[2][:].unsqueeze(2).to_broadcast([P, T, 2]))
+        for step, (t, h) in enumerate(STEPS):
+            ts = slice(t * P, (t + 1) * P)
+            fp8, fp8_s = v_w[h][:].bitcast(FP8X4), v_s[h][:]
+            fp4 = [v2_w[h][:, a, :].bitcast(FP4X4) for a in range(2)]
+            fp4_s = [v2_s[h][:], lowered[h][:]]
+            hv = psum.tile([P, HALF], F32, name="hv", tag="hv")
+            nc.tensor.matmul_mx(hv[:], w_w[t][:, 0].bitcast(FP8X4), w_s[t][4:P, 0], fp8, fp8_s, start=True, stop=True)
+            ht = psum.tile([P, HALF], F32, name="ht", tag="ht")
+            for a in range(2):
+                nc.tensor.matmul_mx(
+                    ht[:], w_w[t][:, 1 + a].bitcast(FP8X4), w_s[t][:, a], fp4[a], fp4_s[a], start=(a == 0), stop=(a == 1)
+                )
+            z = psum.tile([P, HALF], F32, name="z", tag="z", bufs=1)
+            nc.tensor.matmul_mx(z[:], z_w[0][:, ts].bitcast(FP8X4), z_s[0][:, ts], fp8, fp8_s, start=True, stop=False)
+            for a in range(2):
+                nc.tensor.matmul_mx(
+                    z[:], z_w[1 + a][:, ts].bitcast(FP8X4), z_s[1 + a][:, ts], fp4[a], fp4_s[a], start=False, stop=(a == 1)
+                )
+            mix = sbuf("mix%d" % step, [P, HALF], F32)
+            at = sbuf("at%d" % step, [P, HALF], F32)
+            gate = sbuf("gate%d" % step, [P, HALF], F32)
+            weighted = work.tile([P, HALF], F32, name="weighted")
+            nc.scalar.activation(mix[:], hv[:], ACT.Silu, bias=no_bias[:])
+            nc.scalar.activation(at[:], ht[:], ACT.Silu, bias=no_bias[:])
+            nc.gpsimd.tensor_tensor(mix[:], mix[:], at[:], ALU.subtract)
+            width = HALF // 2 if step == 0 else HALF
+            for c in range(0, HALF, width):
+                cs = slice(c, c + width)
+                nc.scalar.activation(gate[:, cs], z[:, cs], ACT.Tanh, bias=half_b[:, t : t + 1], scale=0.5)
+                nc.scalar.activation(gate[:, cs], gate[:, cs], ACT.Identity, bias=0.5, scale=0.5)
+                nc.gpsimd.tensor_tensor(mix[:, cs], mix[:, cs], gate[:, cs], ALU.mult)
+                nc.gpsimd.tensor_tensor(mix[:, cs], mix[:, cs], at[:, cs], ALU.add)
+                nc.vector.tensor_tensor(weighted[:, cs], mix[:, cs], wgo_ps[h][:, cs], ALU.mult)
+                nc.vector.tensor_copy(pages[t][:].indirect(entries(idx, h * HALF + c, width)), weighted[:, cs])
+            if h == HALVES - 1:
+                if t < 2:
+                    for c in range(CHUNKS):
+                        dma(out=staged[c][:, t, :], in_=pages[t][:, CHUNK * c : CHUNK * (c + 1)])
+                dma(out=out_rows[:, t, :], in_=pages[t][:])
 
-        nc.vector.tensor_copy(g4[:, 0:512, 3], pages[3][:, 0:512])
-        nc.scalar.copy(g4[:, VCOLS:1024, 3], pages[3][:, VCOLS:1024])
-        nc.vector.tensor_copy(g4[:, 512:VCOLS, 3], pages[3][:, 512:VCOLS])
-        nc.scalar.copy(g4[:, 1024:1536, 3], pages[3][:, 1024:1536])
-        nc.scalar.copy(g4[:, 1536:T, 3], pages[3][:, 1536:T])
-        ocodes = kt("ocodes", [P, T], U32)
-        oscale = kt("oscale", [P, T], U8)
-        ow = words(out_1[0])
-        for c in range(4):
-            cs = slice(512 * c, 512 * (c + 1))
-            nc.vector.quantize_mx(ocodes[:, cs].bitcast(FP8X4), oscale[:, cs], grouped[:, 2048 * c : 2048 * (c + 1)])
-            dma(out=ow[:, cs], in_=ocodes[:, cs].bitcast(I32))
-        for q in range(4):
-            eng = nc.scalar if q % 2 else nc.sync
-            eng.dma_start(out=out_2[0, 4 * q : 4 * q + 4, :].bitcast(I32), in_=oscale[32 * q : 32 * q + 4, :].bitcast(I32))
+        last = len(STEPS) - 1
+        after = ["half_b", "gate4", "gate5", "at%d" % last]
+        grouped = [sbuf("grouped%d" % c, [P, PACK * CHUNK], BF16, after[c]) for c in range(CHUNKS)]
+        places = [g[:].rearrange("p (c t) -> p c t", t=PACK) for g in grouped]
+        for c in range(CHUNKS - 1):
+            nc.scalar.copy(
+                places[c].rearrange("p c (r t) -> p c r t", r=2),
+                staged[c][:].rearrange("p t c -> p c t").unsqueeze(2).to_broadcast([P, CHUNK, 2, 2]),
+            )
+        twice = pages[2][:].unsqueeze(2).to_broadcast([P, T, 2])
+        for c in range(CHUNKS):
+            nc.scalar.copy(places[c][:, :, 2:4], twice[:, CHUNK * c : CHUNK * (c + 1)])
+        nc.gpsimd.tensor_scalar(
+            places[CHUNKS - 1][:, :, 0:2], staged[CHUNKS - 1][:].rearrange("p t c -> p c t"), 1.0, 0.0, ALU.mult, ALU.add
+        )
+        for c in range(VECTOR_CHUNKS):
+            nc.vector.tensor_copy(places[c][:, :, 3], pages[3][:, CHUNK * c : CHUNK * (c + 1)])
+        for c in range(VECTOR_CHUNKS, CHUNKS):
+            nc.scalar.copy(places[c][:, :, 3], pages[3][:, CHUNK * c : CHUNK * (c + 1)])
+
+        out_w = sbuf("out_w", [P, T], U32)
+        out_s = sbuf("out_s", [P, T], U8)
+        out_words = as_words(out_1[0])
+        for c in range(CHUNKS):
+            cs = slice(CHUNK * c, CHUNK * (c + 1))
+            nc.vector.quantize_mx(out_w[:, cs].bitcast(FP8X4), out_s[:, cs], grouped[c][:])
+            dma(out=out_words[:, cs], in_=out_w[:, cs].bitcast(I32))
+        for q in range(QUADS):
+            queue = nc.scalar if q % 2 else nc.sync
+            queue.dma_start(out=out_2[0, 4 * q : 4 * q + 4, :].bitcast(I32), in_=out_s[32 * q : 32 * q + 4, :].bitcast(I32))

@@ -88,6 +88,12 @@ def tile_list_gmu_silu_scatP_kernel(
         def load_wv_scales(q):
             dma(out=w_s_raw[32 * q + 4 : 32 * q + 8, 0:N].bitcast(I32), in_=wv_scales[0, 4 * q : 4 * q + 4, :].bitcast(I32))
 
+        def load_wt_scales(q):
+            dma(
+                out=w_s_raw[32 * q : 32 * q + 4, :].bitcast(I32).rearrange("r (a n) -> r a n", a=2),
+                in_=wt_scales[:, 4 * q : 4 * q + 4, :].bitcast(I32).rearrange("a r n -> r a n"),
+            )
+
         dma(out=idx[:], in_=offs)
         dma(out=tab_w[:].bitcast(I32), in_=as_words(tab_words[0]))
         dma(out=idx2[:], in_=offs2)
@@ -104,11 +110,8 @@ def tile_list_gmu_silu_scatP_kernel(
         dma(out=wv_raw[:], in_=as_words(wv_words[0]))
         for q in range(QUADS // 2, QUADS):
             load_wv_scales(q)
-        for q in range(QUADS):
-            dma(
-                out=w_s_raw[32 * q : 32 * q + 4, :].bitcast(I32).rearrange("r (a n) -> r a n", a=2),
-                in_=wt_scales[:, 4 * q : 4 * q + 4, :].bitcast(I32).rearrange("a r n -> r a n"),
-            )
+        for q in range(QUADS - 1):
+            load_wt_scales(q)
         nc.gpsimd.dma_start(out=wgo_rows[:], in_=wgo[0:16, :].rearrange("r (i n) -> (r i) n", n=P))
         nc.gpsimd.dma_start(out=b_raw[:], in_=b.rearrange("(p t) -> p t", t=PACK))
         for t in range(2, PACK):
@@ -142,6 +145,7 @@ def tile_list_gmu_silu_scatP_kernel(
         zt1_raw = by_partition(zt[512:1024, :])
         zt1_low = sbuf("zt1_low", [P, PACK, N // 2], F32, "tab_w")
         dma(out=zt1_low[:], in_=zt1_raw[:, :, 0 : N // 2])
+        load_wt_scales(QUADS - 1)
         gather_v2_scales(0, nc.gpsimd)
         gather_v2_words(0)
 
@@ -216,7 +220,7 @@ def tile_list_gmu_silu_scatP_kernel(
             fp4_s = [v2_s[h][:], lowered[h][:]]
             hv = psum.tile([P, HALF], F32, name="hv", tag="hv")
             nc.tensor.matmul_mx(hv[:], w_w[t][:, 0].bitcast(FP8X4), w_s[t][4:P, 0], fp8, fp8_s, start=True, stop=True)
-            ht = psum.tile([P, HALF], F32, name="ht", tag="ht")
+            ht = psum.tile([P, HALF], F32, name="ht", tag="ht", bufs=1)
             for a in range(2):
                 nc.tensor.matmul_mx(
                     ht[:], w_w[t][:, 1 + a].bitcast(FP8X4), w_s[t][:, a], fp4[a], fp4_s[a], start=(a == 0), stop=(a == 1)

@@ -1,7 +1,6 @@
 from contextlib import ExitStack
 
 import concourse.mybir as mybir
-from concourse.masks import make_identity
 
 K, L, N, T, J = 512, 1024, 512, 2048, 1024
 FLOPS = 2 * 2 * (K + L) * N * J
@@ -20,14 +19,13 @@ ALU = mybir.AluOpType
 P = 128
 PACK = 4
 QUADS = 4
+SLICES = N // P
 HALF = 512
 HALVES = J // HALF
-CHUNK = 512
-CHUNKS = T // CHUNK
-CLEAR = 1024
-VECTOR_CHUNKS = 2
-
-STEPS = [(0, 0), (1, 0), (0, 1), (1, 1), (2, 0), (2, 1), (3, 0), (3, 1)]
+BANK = 512
+PAGES = 4
+LATE_WORDS = 2 * T + 3 * PACK * N + 3 * N
+Z_GROUPS = [(0, 1), (1, 2), (2, 4)]
 
 
 def tile_list_gmu_silu_scatP_kernel(
@@ -38,10 +36,13 @@ def tile_list_gmu_silu_scatP_kernel(
     with ExitStack() as ctx:
         keep = ctx.enter_context(tc.tile_pool(name="keep", bufs=1))
         work = ctx.enter_context(tc.tile_pool(name="work", bufs=2))
-        psum = ctx.enter_context(tc.psum_pool(name="psum", bufs=2))
+        psum = ctx.enter_context(tc.psum_pool(name="psum", bufs=1))
 
-        def sbuf(name, shape, dtype, after=None):
-            return keep.tile(shape, dtype, name=name, tag=after or name, align_bytes=64)
+        def sbuf(name, shape, dtype, after=None, pool=keep):
+            return pool.tile(shape, dtype, name=name, tag=after or name, align_bytes=64)
+
+        def bank(number, name):
+            return psum.tile([P, BANK], F32, name=name, tag="bank%d" % number)
 
         def as_words(ap):
             return ap.rearrange("p n i -> p (n i)").bitcast(I32)
@@ -56,230 +57,230 @@ def tile_list_gmu_silu_scatP_kernel(
 
         idx = keep.tile([P, J // 16], U16, name="idx")
         idx2 = keep.tile([P, J // 16], U16, name="idx2")
-        tab_w = sbuf("tab_w", [P, T], U32)
-        tab2_w = sbuf("tab2_w", [P, T], U32)
         tab_s = sbuf("tab_s", [P, T], U8)
         tab2_s = sbuf("tab2_s", [P, T], U8)
-        w_s_raw = sbuf("w_s_raw", [P, 2 * N], U8)
-        lowered = [sbuf("lowered%d" % h, [P, HALF], U8) for h in range(HALVES)]
-        pages = [sbuf("page%d" % t, [P, T], F32) for t in range(PACK)]
+        wv_s = sbuf("wv_s", [P, N], U8)
+        wt_s = sbuf("wt_s", [P, 2, N], U8)
+        lowered = sbuf("lowered", [P, J], U8)
+        pages = [sbuf("page%d" % t, [P, T], F32) for t in range(PAGES)]
+        rows = sbuf("rows", [P, P], F32)
 
-        nc.gpsimd.memset(tab_s[:].bitcast(I32), 0)
-        nc.gpsimd.memset(w_s_raw[:].bitcast(I32), 0)
-        nc.vector.memset(tab2_s[:].bitcast(I32), 0)
+        nc.gpsimd.memset(tab2_s[:].bitcast(I32), 0)
+        nc.vector.memset(tab_s[:].bitcast(I32), 0)
+        ident = sbuf("ident", [P, P], F32)
+        with tc.tile_pool(name="early", bufs=1) as early:
+            zeros = sbuf("zeros", [P, LATE_WORDS], F32, pool=early)
+            nc.gpsimd.memset(zeros[:, 0:P], 0.0)
+            nc.gpsimd.affine_select(
+                out=ident[:], in_=zeros[:, 0:P], pattern=[[-1, P]], compare_op=ALU.not_equal, fill=1.0, base=0,
+                channel_multiplier=1,
+            )
+        late = ctx.enter_context(tc.tile_pool(name="late", bufs=1))
+        tab_w = sbuf("tab_w", [P, T], U32, pool=late)
+        tab2_w = sbuf("tab2_w", [P, T], U32, pool=late)
+        nc.gpsimd.memset(rows[:], 0.0)
+        nc.gpsimd.memset(wv_s[:].bitcast(I32), 0)
+        nc.vector.memset(wt_s[:].rearrange("p a n -> p (a n)").bitcast(I32), 0)
         zero = sbuf("zero", [P, 1], F32)
         nc.vector.memset(zero[:], 0.0)
         no_bias = sbuf("no_bias", [P, 1], F32)
         nc.scalar.activation(no_bias[:], zero[:], ACT.Silu)
-        for h in range(HALVES):
-            nc.vector.memset(lowered[h][:].bitcast(I32), 0)
+        nc.vector.memset(lowered[:].bitcast(I32), 0)
         for t in range(2):
             nc.vector.memset(pages[t][:].bitcast(I32), 0)
-        ident = sbuf("ident", [P, P], F32)
-        make_identity(nc, ident[:])
 
-        zv_raw = sbuf("zv_raw", [P, PACK, N], F32)
-        zt0_raw = sbuf("zt0_raw", [P, PACK, N], F32)
-        wv_raw = sbuf("wv_raw", [P, N], I32)
-        wt_raw = sbuf("wt_raw", [P, 2, N], I32)
-        wgo_rows = sbuf("wgo_rows", [P, P], F32)
-        b_raw = sbuf("b_raw", [P, PACK], F32)
+        wv_w = sbuf("wv_w", [P, N], U32, pool=late)
+        wt_w = sbuf("wt_w", [P, 2, N], U32, pool=late)
+        z_src = [by_partition(zt[0:512, :]), by_partition(zt[512:1024, :]), by_partition(zv)]
+        z_raw = {}
 
-        def load_wv_scales(q):
-            dma(out=w_s_raw[32 * q + 4 : 32 * q + 8, 0:N].bitcast(I32), in_=wv_scales[0, 4 * q : 4 * q + 4, :].bitcast(I32))
+        def load_z(group, a):
+            s0, s1 = Z_GROUPS[group]
+            z_raw[group, a] = sbuf("z_raw%d_%d" % (group, a), [P, PACK, (s1 - s0) * P], F32, pool=late)
+            dma(out=z_raw[group, a][:], in_=z_src[a][:, :, s0 * P : s1 * P])
+
+        def load_w(c0, c1):
+            dma(out=wt_w[:, :, c0:c1].bitcast(I32), in_=wt_words.rearrange("a p n i -> p a (n i)").bitcast(I32)[:, :, c0:c1])
+            dma(out=wv_w[:, c0:c1].bitcast(I32), in_=as_words(wv_words[0])[:, c0:c1])
 
         def load_wt_scales(q):
             dma(
-                out=w_s_raw[32 * q : 32 * q + 4, :].bitcast(I32).rearrange("r (a n) -> r a n", a=2),
+                out=wt_s[32 * q : 32 * q + 4].bitcast(I32),
                 in_=wt_scales[:, 4 * q : 4 * q + 4, :].bitcast(I32).rearrange("a r n -> r a n"),
             )
 
-        dma(out=idx[:], in_=offs)
-        dma(out=tab_w[:].bitcast(I32), in_=as_words(tab_words[0]))
         dma(out=idx2[:], in_=offs2)
         for q in range(QUADS):
-            dma(out=tab_s[32 * q : 32 * q + 4, :].bitcast(I32), in_=tab_scales[0, 4 * q : 4 * q + 4, :].bitcast(I32))
-        dma(out=zv_raw[:], in_=by_partition(zv))
-        dma(out=tab2_w[:].bitcast(I32), in_=as_words(tab2_words[0]))
-        for q in range(QUADS):
             dma(out=tab2_s[32 * q : 32 * q + 8, :].bitcast(I32), in_=tab2_scales[:, 4 * q : 4 * q + 4, :].bitcast(I32))
-        for q in range(QUADS // 2):
-            load_wv_scales(q)
-        dma(out=zt0_raw[:], in_=by_partition(zt[0:512, :]))
-        dma(out=wt_raw[:], in_=wt_words.rearrange("a p n i -> p a (n i)").bitcast(I32))
-        dma(out=wv_raw[:], in_=as_words(wv_words[0]))
-        for q in range(QUADS // 2, QUADS):
-            load_wv_scales(q)
-        for q in range(QUADS - 1):
+        dma(out=tab2_w[:].bitcast(I32), in_=as_words(tab2_words[0]))
+        dma(out=idx[:], in_=offs)
+        for q in range(QUADS):
+            dma(out=tab_s[32 * q : 32 * q + 4, :].bitcast(I32), in_=tab_scales[0, 4 * q : 4 * q + 4, :].bitcast(I32))
+        dma(out=tab_w[:].bitcast(I32), in_=as_words(tab_words[0]))
+        load_wt_scales(0)
+        for a in range(3):
+            load_z(0, a)
+        load_w(0, P)
+        for q in range(1, QUADS):
             load_wt_scales(q)
-        nc.gpsimd.dma_start(out=wgo_rows[:], in_=wgo[0:16, :].rearrange("r (i n) -> (r i) n", n=P))
-        nc.gpsimd.dma_start(out=b_raw[:], in_=b.rearrange("(p t) -> p t", t=PACK))
-        for t in range(2, PACK):
-            for c in range(0, T, CLEAR):
-                nc.gpsimd.memset(pages[t][:, c : c + CLEAR], 0.0)
+        for a in range(3):
+            load_z(1, a)
+        load_w(P, N)
+        for a in range(3):
+            load_z(2, a)
 
-        v_w = [sbuf("v_w%d" % h, [P, HALF], U32) for h in range(HALVES)]
-        v2_w = [sbuf("v2_w%d" % h, [P, 2, 2 * HALF], U8) for h in range(HALVES)]
-        v_s, v2_s = [], []
+        nc.gpsimd.dma_start(out=rows[0 : J // P, :], in_=wgo[0:1, :].rearrange("r (i n) -> (r i) n", n=P))
+        nc.gpsimd.dma_start(out=rows[J // P : J // P + SLICES, :], in_=b.rearrange("(s n) -> s n", n=P))
+        for q in range(QUADS):
+            nc.gpsimd.dma_start(
+                out=wv_s[32 * q : 32 * q + 4, :].bitcast(I32), in_=wv_scales[0, 4 * q : 4 * q + 4, :].bitcast(I32)
+            )
 
-        def gather_v_words(h):
+        v2_s = sbuf("v2_s", [P, J], U8)
+        nc.vector.tensor_copy(v2_s[:], tab2_s[:].indirect(idx2[:]))
+        nc.gpsimd.dma_start(out=lowered[0 : P - 4, :].bitcast(I32), in_=v2_s[4:P, :].bitcast(I32))
+        v_w, v2_w = [], []
+
+        def gather_v_words(h, after=None):
+            v_w.append(sbuf("v_w%d" % h, [P, HALF], U32, after))
             nc.vector.tensor_copy(v_w[h][:], tab_w[:].indirect(entries(idx, h * HALF, HALF)))
+
+        def gather_v2_words(h, after=None):
+            pairs = sbuf("pairs%d" % h, [P, HALF], U32, after, late)
+            v2_w.append(sbuf("v2_w%d" % h, [P, 2, 2 * HALF], U8))
+            nc.vector.tensor_copy(pairs[:], tab2_w[:].indirect(entries(idx2, h * HALF, HALF)))
+            nc.vector.tensor_copy(v2_w[h][:].bitcast(U16), pairs[:].bitcast(U16).rearrange("p (j d) -> p d j", d=2))
+
+        gather_v2_words(0)
+        v_s = []
 
         def gather_v_scales(h, after=None):
             v_s.append(sbuf("v_s%d" % h, [P, HALF], U8, after))
             nc.vector.tensor_copy(v_s[h][:], tab_s[:].indirect(entries(idx, h * HALF, HALF)))
 
-        def gather_v2_scales(h, queue, after=None):
-            v2_s.append(sbuf("v2_s%d" % h, [P, HALF], U8, after))
-            nc.vector.tensor_copy(v2_s[h][:], tab2_s[:].indirect(entries(idx2, h * HALF, HALF)))
-            queue.dma_start(out=lowered[h][0 : P - 4, :].bitcast(I32), in_=v2_s[h][4:P, :].bitcast(I32))
-
-        def gather_v2_words(h, after=None):
-            pairs = sbuf("pairs%d" % h, [P, HALF], U32, after)
-            nc.vector.tensor_copy(pairs[:], tab2_w[:].indirect(entries(idx2, h * HALF, HALF)))
-            nc.vector.tensor_copy(v2_w[h][:].bitcast(U16), pairs[:].bitcast(U16).rearrange("p (j d) -> p d j", d=2))
-
-        gather_v_words(0)
         gather_v_scales(0)
-        gather_v_words(1)
-        zt1_raw = by_partition(zt[512:1024, :])
-        zt1_low = sbuf("zt1_low", [P, PACK, N // 2], F32, "tab_w")
-        dma(out=zt1_low[:], in_=zt1_raw[:, :, 0 : N // 2])
-        load_wt_scales(QUADS - 1)
-        gather_v2_scales(0, nc.gpsimd)
-        gather_v2_words(0)
+        gather_v_words(0)
 
-        z_bf = [sbuf("z_bf%d" % a, [P, PACK * N], BF16) for a in range(3)]
-        z_w = [sbuf("z_w%d" % a, [P, N], U32) for a in range(3)]
-        z_s = [sbuf("z_s%d" % a, [P, N], U8) for a in range(3)]
+        z_w, z_s = {}, {}
 
-        def round_and_deal(a, raw, m0, m1):
-            nc.scalar.copy(
-                z_bf[a][:].rearrange("p (t m i) -> p m t i", t=PACK, i=PACK)[:, m0:m1],
-                raw[:].rearrange("p i (m t) -> p m t i", t=PACK),
-            )
+        def make_z(group):
+            s0, s1 = Z_GROUPS[group]
+            width = (s1 - s0) * P
+            codes = sbuf("z_w%d" % group, [P, 3, width], U32)
+            scales = sbuf("z_s%d" % group, [P, 3, width], U8)
+            for name, a0, a1 in (("zt", 0, 2), ("zv", 2, 3)):
+                rounded = sbuf("%s_bf%d" % (name, group), [P, a1 - a0, PACK * width], BF16)
+                for a in range(a0, a1):
+                    nc.scalar.copy(
+                        rounded[:, a - a0].rearrange("p (c e i) -> p c i e", e=4, i=PACK),
+                        z_raw[group, a][:].rearrange("p i (c e) -> p c i e", e=4),
+                    )
+                nc.vector.quantize_mx(
+                    codes[:, a0:a1].rearrange("p a n -> p (a n)").bitcast(FP8X4),
+                    scales[:, a0:a1].rearrange("p a n -> p (a n)"),
+                    rounded[:].rearrange("p a n -> p (a n)"),
+                )
+            for s in range(s0, s1):
+                z_w[s] = codes[:, :, (s - s0) * P : (s - s0 + 1) * P]
+                z_s[s] = scales[:, :, (s - s0) * P : (s - s0 + 1) * P]
 
-        def quantise_z(a, c0, c1):
-            nc.vector.quantize_mx(z_w[a][:, c0:c1].bitcast(FP8X4), z_s[a][:, c0:c1], z_bf[a][:, PACK * c0 : PACK * c1])
+        make_z(0)
+        gather_v_words(1, "zv_bf0")
+        gather_v2_words(1, "tab_w")
+        gather_v_scales(1, "zt_bf0")
 
-        round_and_deal(0, zv_raw, 0, P)
-        zt1_high = sbuf("zt1_high", [P, PACK, N // 2], F32, "zv_raw")
-        dma(out=zt1_high[:], in_=zt1_raw[:, :, N // 2 : N])
-        quantise_z(0, 0, N)
-        gather_v_scales(1, "z_bf0")
-
-        turned = psum.tile([P, HALF], F32, name="turned", tag="z", bufs=1)
-        nc.tensor.transpose(turned[:, 0:P], wgo_rows[:], ident[:])
-        wgo_cols = sbuf("wgo_cols", [P, J // P], F32, "pairs0")
+        turned = bank(5, "turned")
+        nc.tensor.transpose(turned[:, 0:P], rows[:], ident[:])
+        wgo_cols = sbuf("wgo_cols", [P, J // P], F32, "z_raw0_2", late)
         nc.scalar.copy(wgo_cols[:], turned[:, 0 : J // P])
-        wgo_ps = [psum.tile([P, HALF], F32, name="wgo_ps%d" % h, tag="wgo") for h in range(HALVES)]
+        half_b = sbuf("half_b", [P, SLICES], F32, "z_raw0_1", late)
+        nc.scalar.mul(half_b[:], turned[:, J // P : J // P + SLICES], 0.5)
+        wgo_ps = [bank(6 + h, "wgo_ps%d" % h) for h in range(HALVES)]
         for i in range(J // P):
             h, c = divmod(i * P, HALF)
             nc.tensor.transpose(wgo_ps[h][:, c : c + P], wgo_cols[:, i : i + 1].to_broadcast([P, P]), ident[:])
 
-        w_w, w_s = {}, {}
 
-        def deal_weights(t0, t1, words_after=None, scales_after=None):
-            dealt_w = sbuf("dealt_w%d" % t0, [P, 3, t1 - t0, P], I32, words_after)
-            dealt_s = sbuf("dealt_s%d" % t0, [P, 2, t1 - t0, P], U8, scales_after)
-            nc.vector.tensor_copy(
-                dealt_w[:, 0].rearrange("p t (g e) -> p g t e", e=4),
-                wv_raw[:].rearrange("p (g e t) -> p g t e", t=PACK, e=4)[:, :, t0:t1],
-            )
-            nc.vector.tensor_copy(
-                dealt_w[:, 1:3].rearrange("p a t (g e) -> p a g t e", e=4),
-                wt_raw[:].rearrange("p a (g e t) -> p a g t e", t=PACK, e=4)[:, :, :, t0:t1],
-            )
-            nc.vector.tensor_copy(dealt_s[:], w_s_raw[:].rearrange("p (a m t) -> p a t m", a=2, t=PACK)[:, :, t0:t1])
-            for t in range(t0, t1):
-                w_w[t] = dealt_w[:, :, t - t0]
-                w_s[t] = dealt_s[:, :, t - t0]
-
-        deal_weights(0, 1)
-        round_and_deal(1, zt0_raw, 0, P)
-        quantise_z(1, 0, N)
-        gather_v2_scales(1, nc.sync, "z_bf1")
-        round_and_deal(2, zt1_low, 0, P // 2)
-        round_and_deal(2, zt1_high, P // 2, P)
-        quantise_z(2, 0, P)
-        deal_weights(1, PACK, "zv_raw", "zt0_raw")
-        quantise_z(2, P, 2 * P)
-        quantise_z(2, 2 * P, N)
-
-        half_b = sbuf("half_b", [P, PACK], F32)
-        nc.vector.tensor_scalar(half_b[:], b_raw[:], 0.5, None, ALU.mult)
-        gather_v2_words(1, "tab_w")
-
-        staged = [sbuf("staged%d" % c, [P, 2, CHUNK], F32) for c in range(CHUNKS)]
-        out_rows = out_0.rearrange("(p t) c -> p t c", t=PACK)
-
-        for step, (t, h) in enumerate(STEPS):
-            ts = slice(t * P, (t + 1) * P)
+        steps = [(s, h) for s in range(SLICES) for h in range(HALVES)]
+        for step, (s, h) in enumerate(steps):
+            page = pages[s % PAGES]
+            cols = slice(s * P, (s + 1) * P)
+            js = slice(h * HALF, (h + 1) * HALF)
             fp8, fp8_s = v_w[h][:].bitcast(FP8X4), v_s[h][:]
             fp4 = [v2_w[h][:, a, :].bitcast(FP4X4) for a in range(2)]
-            fp4_s = [v2_s[h][:], lowered[h][:]]
-            hv = psum.tile([P, HALF], F32, name="hv", tag="hv")
-            nc.tensor.matmul_mx(hv[:], w_w[t][:, 0].bitcast(FP8X4), w_s[t][4:P, 0], fp8, fp8_s, start=True, stop=True)
-            ht = psum.tile([P, HALF], F32, name="ht", tag="ht", bufs=1)
+            fp4_s = [v2_s[:, js], lowered[:, js]]
+            hv = bank(step % 2, "hv")
+            ht = bank(2 + step % 2, "ht")
+            z = bank(4 + step % 2, "z")
             for a in range(2):
                 nc.tensor.matmul_mx(
-                    ht[:], w_w[t][:, 1 + a].bitcast(FP8X4), w_s[t][:, a], fp4[a], fp4_s[a], start=(a == 0), stop=(a == 1)
+                    ht[:], wt_w[:, a, cols].bitcast(FP8X4), wt_s[:, a, cols], fp4[a], fp4_s[a], start=(a == 0), stop=(a == 1)
                 )
-            z = psum.tile([P, HALF], F32, name="z", tag="z", bufs=1)
-            nc.tensor.matmul_mx(z[:], z_w[0][:, ts].bitcast(FP8X4), z_s[0][:, ts], fp8, fp8_s, start=True, stop=False)
+            nc.tensor.matmul_mx(hv[:], wv_w[:, cols].bitcast(FP8X4), wv_s[:, cols], fp8, fp8_s, start=True, stop=True)
             for a in range(2):
-                nc.tensor.matmul_mx(
-                    z[:], z_w[1 + a][:, ts].bitcast(FP8X4), z_s[1 + a][:, ts], fp4[a], fp4_s[a], start=False, stop=(a == 1)
-                )
+                nc.tensor.matmul_mx(z[:], z_w[s][:, a].bitcast(FP8X4), z_s[s][:, a], fp4[a], fp4_s[a], start=(a == 0), stop=False)
+            nc.tensor.matmul_mx(z[:], z_w[s][:, 2].bitcast(FP8X4), z_s[s][:, 2], fp8, fp8_s, start=False, stop=True)
             mix = sbuf("mix%d" % step, [P, HALF], F32)
             at = sbuf("at%d" % step, [P, HALF], F32)
             gate = sbuf("gate%d" % step, [P, HALF], F32)
             weighted = work.tile([P, HALF], F32, name="weighted")
-            nc.scalar.activation(mix[:], hv[:], ACT.Silu, bias=no_bias[:])
             nc.scalar.activation(at[:], ht[:], ACT.Silu, bias=no_bias[:])
+            nc.scalar.activation(mix[:], hv[:], ACT.Silu, bias=no_bias[:])
             nc.gpsimd.tensor_tensor(mix[:], mix[:], at[:], ALU.subtract)
             width = HALF // 2 if step == 0 else HALF
             for c in range(0, HALF, width):
                 cs = slice(c, c + width)
-                nc.scalar.activation(gate[:, cs], z[:, cs], ACT.Tanh, bias=half_b[:, t : t + 1], scale=0.5)
+                nc.scalar.activation(gate[:, cs], z[:, cs], ACT.Tanh, bias=half_b[:, s : s + 1], scale=0.5)
                 nc.scalar.activation(gate[:, cs], gate[:, cs], ACT.Identity, bias=0.5, scale=0.5)
                 nc.gpsimd.tensor_tensor(mix[:, cs], mix[:, cs], gate[:, cs], ALU.mult)
                 nc.gpsimd.tensor_tensor(mix[:, cs], mix[:, cs], at[:, cs], ALU.add)
                 nc.vector.tensor_tensor(weighted[:, cs], mix[:, cs], wgo_ps[h][:, cs], ALU.mult)
-                nc.vector.tensor_copy(pages[t][:].indirect(entries(idx, h * HALF + c, width)), weighted[:, cs])
+                nc.vector.tensor_copy(page[:].indirect(entries(idx, h * HALF + c, width)), weighted[:, cs])
+            if step < len(Z_GROUPS) - 1:
+                make_z(step + 1)
+            if step < PAGES - 2:
+                for c in range(0, T, BANK):
+                    nc.gpsimd.memset(pages[step + 2][:, c : c + BANK], 0.0)
             if h == HALVES - 1:
-                if t < 2:
-                    for c in range(CHUNKS):
-                        dma(out=staged[c][:, t, :], in_=pages[t][:, CHUNK * c : CHUNK * (c + 1)])
-                dma(out=out_rows[:, t, :], in_=pages[t][:])
+                dma(out=out_0[cols, :], in_=page[:])
 
-        last = len(STEPS) - 1
-        after = ["half_b", "gate4", "gate5", "at%d" % last]
-        grouped = [sbuf("grouped%d" % c, [P, PACK * CHUNK], BF16, after[c]) for c in range(CHUNKS)]
-        places = [g[:].rearrange("p (c t) -> p c t", t=PACK) for g in grouped]
-        for c in range(CHUNKS - 1):
-            nc.scalar.copy(
-                places[c].rearrange("p c (r t) -> p c r t", r=2),
-                staged[c][:].rearrange("p t c -> p c t").unsqueeze(2).to_broadcast([P, CHUNK, 2, 2]),
+        out_s = sbuf("out_s", [P, SLICES, BANK], U8)
+        for s in range(SLICES):
+            blocks = pages[s][:].rearrange("p (g k c) -> p k g c", g=QUADS, c=P)
+            out_w = sbuf("out_w%d" % s, [P, BANK], U32)
+            for half in range(2):
+                back = bank(4 + half, "back")
+                for k2 in range(2):
+                    k = 2 * half + k2
+                    turned = bank(k, "turned")
+                    for g in range(QUADS):
+                        nc.tensor.transpose(turned[:, g * P : (g + 1) * P], blocks[:, k, g], ident[:])
+                    rounded = sbuf("rounded%d_%d" % (s, k), [P, BANK], BF16)
+                    copy = nc.vector.tensor_copy if s == SLICES - 1 and k2 == 0 else nc.scalar.copy
+                    copy(
+                        rounded[:].rearrange("p (u m e) -> p u m e", u=2, e=2),
+                        turned[:].rearrange("p (m u e) -> p u m e", u=2, e=2),
+                    )
+                    for u in range(2):
+                        c0 = (2 * k2 + u) * P
+                        nc.tensor.transpose(back[:, c0 : c0 + P], rounded[:].bitcast(F32)[:, u * P : (u + 1) * P], ident[:])
+                grouped = sbuf("grouped%d_%d" % (s, half), [P, 2 * BANK], BF16)
+                copy = nc.vector.tensor_copy if s == SLICES - 1 and half == 0 else nc.scalar.copy
+                copy(
+                    grouped[:].bitcast(F32).rearrange("p (k c u) -> p k c u", k=2, u=2),
+                    back[:].rearrange("p (k u c) -> p k c u", k=2, u=2),
+                )
+                ws = slice(half * 2 * P, (half + 1) * 2 * P)
+                nc.vector.quantize_mx(out_w[:, ws].bitcast(FP8X4), out_s[:, s, ws], grouped[:])
+            for g in range(QUADS):
+                queue = nc.scalar if s == SLICES - 1 and g % 2 else nc.sync
+                queue.dma_start(
+                    out=as_words(out_1[0])[32 * s : 32 * (s + 1), g * BANK : (g + 1) * BANK],
+                    in_=out_w[32 * g : 32 * (g + 1), :].bitcast(I32),
+                )
+        for g in range(QUADS):
+            queue = nc.scalar if g % 2 else nc.sync
+            queue.dma_start(
+                out=out_2[0].rearrange("(s r) (g c) -> g r s c", r=4, g=QUADS)[g].bitcast(I32),
+                in_=out_s[32 * g : 32 * g + 4].bitcast(I32),
             )
-        twice = pages[2][:].unsqueeze(2).to_broadcast([P, T, 2])
-        for c in range(CHUNKS):
-            nc.scalar.copy(places[c][:, :, 2:4], twice[:, CHUNK * c : CHUNK * (c + 1)])
-        nc.gpsimd.tensor_scalar(
-            places[CHUNKS - 1][:, :, 0:2], staged[CHUNKS - 1][:].rearrange("p t c -> p c t"), 1.0, 0.0, ALU.mult, ALU.add
-        )
-        for c in range(VECTOR_CHUNKS):
-            nc.vector.tensor_copy(places[c][:, :, 3], pages[3][:, CHUNK * c : CHUNK * (c + 1)])
-        for c in range(VECTOR_CHUNKS, CHUNKS):
-            nc.scalar.copy(places[c][:, :, 3], pages[3][:, CHUNK * c : CHUNK * (c + 1)])
-
-        out_w = sbuf("out_w", [P, T], U32)
-        out_s = sbuf("out_s", [P, T], U8)
-        out_words = as_words(out_1[0])
-        for c in range(CHUNKS):
-            cs = slice(CHUNK * c, CHUNK * (c + 1))
-            nc.vector.quantize_mx(out_w[:, cs].bitcast(FP8X4), out_s[:, cs], grouped[c][:])
-            dma(out=out_words[:, cs], in_=out_w[:, cs].bitcast(I32))
-        for q in range(QUADS):
-            queue = nc.scalar if q % 2 else nc.sync
-            queue.dma_start(out=out_2[0, 4 * q : 4 * q + 4, :].bitcast(I32), in_=out_s[32 * q : 32 * q + 4, :].bitcast(I32))

@@ -23,9 +23,17 @@ SLICES = N // P
 HALF = 512
 HALVES = J // HALF
 BANK = 512
-PAGES = 4
-LATE_WORDS = 2 * T + 3 * PACK * N + 3 * N
-Z_GROUPS = [(0, 1), (1, 2), (2, 4)]
+Z_COLS = 2 * P
+SHIFT_ROWS = 112
+ODD = T // 2 - 1
+Z_WORDS = PACK * Z_COLS
+TAB_AT = Z_WORDS - 16
+PAIRS_AT = Z_WORDS
+V_S_AT = PAIRS_AT + HALF
+LATE_Z_AT = [0, V_S_AT + HALF // 4, V_S_AT + HALF // 4 + Z_WORDS]
+W_AT = LATE_Z_AT[2] + Z_WORDS
+Z_AT = W_AT + 3 * N
+STEPS = [(0, 0), (1, 0), (0, 1), (1, 1), (2, 0), (2, 1), (3, 0), (3, 1)]
 
 
 def tile_list_gmu_silu_scatP_kernel(
@@ -35,7 +43,6 @@ def tile_list_gmu_silu_scatP_kernel(
     nc = tc.nc
     with ExitStack() as ctx:
         keep = ctx.enter_context(tc.tile_pool(name="keep", bufs=1))
-        work = ctx.enter_context(tc.tile_pool(name="work", bufs=2))
         psum = ctx.enter_context(tc.psum_pool(name="psum", bufs=1))
 
         def sbuf(name, shape, dtype, after=None, pool=keep):
@@ -59,117 +66,90 @@ def tile_list_gmu_silu_scatP_kernel(
         idx2 = keep.tile([P, J // 16], U16, name="idx2")
         tab_s = sbuf("tab_s", [P, T], U8)
         tab2_s = sbuf("tab2_s", [P, T], U8)
-        wv_s = sbuf("wv_s", [P, N], U8)
-        wt_s = sbuf("wt_s", [P, 2, N], U8)
+        tab2_w = sbuf("tab2_w", [P, T], U32)
         lowered = sbuf("lowered", [P, J], U8)
-        pages = [sbuf("page%d" % t, [P, T], F32) for t in range(PAGES)]
-        rows = sbuf("rows", [P, P], F32)
-
-        nc.gpsimd.memset(tab2_s[:].bitcast(I32), 0)
-        nc.vector.memset(tab_s[:].bitcast(I32), 0)
+        pages = [sbuf("page%d" % t, [P, T], F32) for t in range(SLICES)]
         ident = sbuf("ident", [P, P], F32)
-        with tc.tile_pool(name="early", bufs=1) as early:
-            zeros = sbuf("zeros", [P, LATE_WORDS], F32, pool=early)
-            nc.gpsimd.memset(zeros[:, 0:P], 0.0)
-            nc.gpsimd.affine_select(
-                out=ident[:], in_=zeros[:, 0:P], pattern=[[-1, P]], compare_op=ALU.not_equal, fill=1.0, base=0,
-                channel_multiplier=1,
-            )
-        late = ctx.enter_context(tc.tile_pool(name="late", bufs=1))
-        tab_w = sbuf("tab_w", [P, T], U32, pool=late)
-        tab2_w = sbuf("tab2_w", [P, T], U32, pool=late)
-        nc.gpsimd.memset(rows[:], 0.0)
-        nc.gpsimd.memset(wv_s[:].bitcast(I32), 0)
-        nc.vector.memset(wt_s[:].rearrange("p a n -> p (a n)").bitcast(I32), 0)
-        zero = sbuf("zero", [P, 1], F32)
-        nc.vector.memset(zero[:], 0.0)
         no_bias = sbuf("no_bias", [P, 1], F32)
-        nc.scalar.activation(no_bias[:], zero[:], ACT.Silu)
+
+        zeros = sbuf("zeros", [P, P], F32)
+        nc.gpsimd.memset(zeros[:], 0.0)
+        nc.gpsimd.memset(tab2_s[:].bitcast(I32), 0)
+        nc.gpsimd.affine_select(
+            out=ident[:], in_=zeros[:], pattern=[[-1, P]], compare_op=ALU.not_equal, fill=1.0, base=0, channel_multiplier=1
+        )
+        with tc.tile_pool(name="early", bufs=1) as early:
+            zero = sbuf("zero", [P, Z_AT + 3 * Z_WORDS], F32, pool=early)
+            nc.vector.memset(zero[:, 0:1], 0.0)
+            nc.scalar.activation(no_bias[:], zero[:, 0:1], ACT.Silu)
+        w_pool = ctx.enter_context(tc.tile_pool(name="w_pool", bufs=1))
         nc.vector.memset(lowered[:].bitcast(I32), 0)
-        for t in range(2):
-            nc.vector.memset(pages[t][:].bitcast(I32), 0)
+        nc.vector.memset(pages[0][:, 0:ODD], 0.0)
+        nc.vector.memset(pages[0][:, ODD:T], 0.0)
+        nc.vector.memset(tab_s[:].bitcast(I32), 0)
+        w_s = sbuf("w_s", [P, 3, N], U8)
+        nc.vector.memset(w_s[:].rearrange("p a n -> p (a n)").bitcast(I32), 0)
+        rows = sbuf("rows", [P, P], F32)
+        nc.vector.memset(rows[:], 0.0)
 
-        wv_w = sbuf("wv_w", [P, N], U32, pool=late)
-        wt_w = sbuf("wt_w", [P, 2, N], U32, pool=late)
+        def placed(name, shape, dtype, word):
+            return w_pool.tile(shape, dtype, name=name, align_bytes=64, offset=4 * word)
+
+        tab_w = placed("tab_w", [P, T], U32, TAB_AT)
+        w_w = [placed("w_w%d" % g, [P, 3, Z_COLS], U32, W_AT + 3 * g * Z_COLS) for g in range(2)]
+        z_raw = {(0, a): placed("z_raw0_%d" % a, [P, PACK, Z_COLS], F32, Z_AT + a * Z_WORDS) for a in range(3)}
+
+        for t in range(1, SLICES):
+            for c in range(0, T, BANK):
+                nc.gpsimd.memset(pages[t][:, c : c + BANK], 0.0)
+
         z_src = [by_partition(zt[0:512, :]), by_partition(zt[512:1024, :]), by_partition(zv)]
-        z_raw = {}
 
-        def load_z(group, a):
-            s0, s1 = Z_GROUPS[group]
-            z_raw[group, a] = sbuf("z_raw%d_%d" % (group, a), [P, PACK, (s1 - s0) * P], F32, pool=late)
-            dma(out=z_raw[group, a][:], in_=z_src[a][:, :, s0 * P : s1 * P])
+        def load_z(group):
+            for a in range(3):
+                if group:
+                    z_raw[group, a] = placed("z_raw1_%d" % a, [P, PACK, Z_COLS], F32, LATE_Z_AT[a])
+                dma(out=z_raw[group, a][:], in_=z_src[a][:, :, group * Z_COLS : (group + 1) * Z_COLS])
 
-        def load_w(c0, c1):
-            dma(out=wt_w[:, :, c0:c1].bitcast(I32), in_=wt_words.rearrange("a p n i -> p a (n i)").bitcast(I32)[:, :, c0:c1])
-            dma(out=wv_w[:, c0:c1].bitcast(I32), in_=as_words(wv_words[0])[:, c0:c1])
-
-        def load_wt_scales(q):
-            dma(
-                out=wt_s[32 * q : 32 * q + 4].bitcast(I32),
-                in_=wt_scales[:, 4 * q : 4 * q + 4, :].bitcast(I32).rearrange("a r n -> r a n"),
-            )
+        def load_w(group):
+            cs = slice(group * Z_COLS, (group + 1) * Z_COLS)
+            dma(out=w_w[group][:, 0:2].bitcast(I32), in_=wt_words.rearrange("a p n i -> p a (n i)").bitcast(I32)[:, :, cs])
+            dma(out=w_w[group][:, 2].bitcast(I32), in_=as_words(wv_words[0])[:, cs])
 
         dma(out=idx2[:], in_=offs2)
+        dma(out=idx[:], in_=offs)
+        dma(out=tab2_w[:].bitcast(I32), in_=as_words(tab2_words[0]))
         for q in range(QUADS):
             dma(out=tab2_s[32 * q : 32 * q + 8, :].bitcast(I32), in_=tab2_scales[:, 4 * q : 4 * q + 4, :].bitcast(I32))
-        dma(out=tab2_w[:].bitcast(I32), in_=as_words(tab2_words[0]))
-        dma(out=idx[:], in_=offs)
+        load_z(0)
         for q in range(QUADS):
             dma(out=tab_s[32 * q : 32 * q + 4, :].bitcast(I32), in_=tab_scales[0, 4 * q : 4 * q + 4, :].bitcast(I32))
         dma(out=tab_w[:].bitcast(I32), in_=as_words(tab_words[0]))
-        load_wt_scales(0)
-        for a in range(3):
-            load_z(0, a)
-        load_w(0, P)
-        for q in range(1, QUADS):
-            load_wt_scales(q)
-        for a in range(3):
-            load_z(1, a)
-        load_w(P, N)
-        for a in range(3):
-            load_z(2, a)
+        load_w(0)
 
-        nc.gpsimd.dma_start(out=rows[0 : J // P, :], in_=wgo[0:1, :].rearrange("r (i n) -> (r i) n", n=P))
-        nc.gpsimd.dma_start(out=rows[J // P : J // P + SLICES, :], in_=b.rearrange("(s n) -> s n", n=P))
-        for q in range(QUADS):
-            nc.gpsimd.dma_start(
-                out=wv_s[32 * q : 32 * q + 4, :].bitcast(I32), in_=wv_scales[0, 4 * q : 4 * q + 4, :].bitcast(I32)
-            )
-
+        v_w, v_s, v2_w = {}, {}, {}
         v2_s = sbuf("v2_s", [P, J], U8)
-        nc.vector.tensor_copy(v2_s[:], tab2_s[:].indirect(idx2[:]))
-        nc.gpsimd.dma_start(out=lowered[0 : P - 4, :].bitcast(I32), in_=v2_s[4:P, :].bitcast(I32))
-        v_w, v2_w = [], []
 
-        def gather_v_words(h, after=None):
-            v_w.append(sbuf("v_w%d" % h, [P, HALF], U32, after))
-            nc.vector.tensor_copy(v_w[h][:], tab_w[:].indirect(entries(idx, h * HALF, HALF)))
-
-        def gather_v2_words(h, after=None):
-            pairs = sbuf("pairs%d" % h, [P, HALF], U32, after, late)
-            v2_w.append(sbuf("v2_w%d" % h, [P, 2, 2 * HALF], U8))
+        def gather_v2_words(h, pairs):
+            v2_w[h] = sbuf("v2_w%d" % h, [P, 2, 2 * HALF], U8)
             nc.vector.tensor_copy(pairs[:], tab2_w[:].indirect(entries(idx2, h * HALF, HALF)))
             nc.vector.tensor_copy(v2_w[h][:].bitcast(U16), pairs[:].bitcast(U16).rearrange("p (j d) -> p d j", d=2))
 
-        gather_v2_words(0)
-        v_s = []
+        def gather_v_scales(h, tile):
+            v_s[h] = tile
+            nc.vector.tensor_copy(tile[:], tab_s[:].indirect(entries(idx, h * HALF, HALF)))
 
-        def gather_v_scales(h, after=None):
-            v_s.append(sbuf("v_s%d" % h, [P, HALF], U8, after))
-            nc.vector.tensor_copy(v_s[h][:], tab_s[:].indirect(entries(idx, h * HALF, HALF)))
-
-        gather_v_scales(0)
-        gather_v_words(0)
+        def gather_v_words(h):
+            v_w[h] = sbuf("v_w%d" % h, [P, HALF], U32)
+            nc.vector.tensor_copy(v_w[h][:], tab_w[:].indirect(entries(idx, h * HALF, HALF)))
 
         z_w, z_s = {}, {}
 
         def make_z(group):
-            s0, s1 = Z_GROUPS[group]
-            width = (s1 - s0) * P
-            codes = sbuf("z_w%d" % group, [P, 3, width], U32)
-            scales = sbuf("z_s%d" % group, [P, 3, width], U8)
+            codes = sbuf("z_w%d" % group, [P, 3, Z_COLS], U32)
+            scales = sbuf("z_s%d" % group, [P, 3, Z_COLS], U8)
             for name, a0, a1 in (("zt", 0, 2), ("zv", 2, 3)):
-                rounded = sbuf("%s_bf%d" % (name, group), [P, a1 - a0, PACK * width], BF16)
+                rounded = sbuf("%s_bf%d" % (name, group), [P, a1 - a0, PACK * Z_COLS], BF16)
                 for a in range(a0, a1):
                     nc.scalar.copy(
                         rounded[:, a - a0].rearrange("p (c e i) -> p c i e", e=4, i=PACK),
@@ -180,83 +160,55 @@ def tile_list_gmu_silu_scatP_kernel(
                     scales[:, a0:a1].rearrange("p a n -> p (a n)"),
                     rounded[:].rearrange("p a n -> p (a n)"),
                 )
-            for s in range(s0, s1):
-                z_w[s] = codes[:, :, (s - s0) * P : (s - s0 + 1) * P]
-                z_s[s] = scales[:, :, (s - s0) * P : (s - s0 + 1) * P]
+            for s in range(2):
+                z_w[2 * group + s] = codes[:, :, s * P : (s + 1) * P]
+                z_s[2 * group + s] = scales[:, :, s * P : (s + 1) * P]
 
+        nc.vector.tensor_copy(v2_s[:], tab2_s[:].indirect(idx2[:]))
+        dma(out=lowered[0:SHIFT_ROWS, :].bitcast(I32), in_=v2_s[4 : 4 + SHIFT_ROWS, :].bitcast(I32))
+        for q in range(QUADS):
+            dma(
+                out=w_s[32 * q : 32 * q + 4, 0:2].bitcast(I32),
+                in_=wt_scales[:, 4 * q : 4 * q + 4, :].bitcast(I32).rearrange("a r n -> r a n"),
+            )
+        for q in range(QUADS):
+            dma(out=w_s[32 * q : 32 * q + 4, 2].bitcast(I32), in_=wv_scales[0, 4 * q : 4 * q + 4, :].bitcast(I32))
+        dma(out=rows[0 : J // P, :], in_=wgo[0:1, :].rearrange("r (i n) -> (r i) n", n=P))
+        dma(out=rows[J // P : J // P + SLICES, :], in_=b.rearrange("(s n) -> s n", n=P))
+        load_w(1)
+        gather_v2_words(0, sbuf("pairs0", [P, HALF], U32))
         make_z(0)
-        gather_v_words(1, "zv_bf0")
-        gather_v2_words(1, "tab_w")
-        gather_v_scales(1, "zt_bf0")
 
-        turned = bank(5, "turned")
+        turned = bank(3, "turned")
         nc.tensor.transpose(turned[:, 0:P], rows[:], ident[:])
-        wgo_cols = sbuf("wgo_cols", [P, J // P], F32, "z_raw0_2", late)
+        wgo_cols = sbuf("wgo_cols", [P, J // P], F32)
         nc.scalar.copy(wgo_cols[:], turned[:, 0 : J // P])
-        half_b = sbuf("half_b", [P, SLICES], F32, "z_raw0_1", late)
+        half_b = sbuf("half_b", [P, SLICES], F32)
         nc.scalar.mul(half_b[:], turned[:, J // P : J // P + SLICES], 0.5)
         wgo_ps = [bank(6 + h, "wgo_ps%d" % h) for h in range(HALVES)]
-        for i in range(J // P):
-            h, c = divmod(i * P, HALF)
-            nc.tensor.transpose(wgo_ps[h][:, c : c + P], wgo_cols[:, i : i + 1].to_broadcast([P, P]), ident[:])
 
-
-        steps = [(s, h) for s in range(SLICES) for h in range(HALVES)]
-        for step, (s, h) in enumerate(steps):
-            page = pages[s % PAGES]
-            cols = slice(s * P, (s + 1) * P)
-            js = slice(h * HALF, (h + 1) * HALF)
-            fp8, fp8_s = v_w[h][:].bitcast(FP8X4), v_s[h][:]
-            fp4 = [v2_w[h][:, a, :].bitcast(FP4X4) for a in range(2)]
-            fp4_s = [v2_s[:, js], lowered[:, js]]
-            hv = bank(step % 2, "hv")
-            ht = bank(2 + step % 2, "ht")
-            z = bank(4 + step % 2, "z")
-            for a in range(2):
-                nc.tensor.matmul_mx(
-                    ht[:], wt_w[:, a, cols].bitcast(FP8X4), wt_s[:, a, cols], fp4[a], fp4_s[a], start=(a == 0), stop=(a == 1)
-                )
-            nc.tensor.matmul_mx(hv[:], wv_w[:, cols].bitcast(FP8X4), wv_s[:, cols], fp8, fp8_s, start=True, stop=True)
-            for a in range(2):
-                nc.tensor.matmul_mx(z[:], z_w[s][:, a].bitcast(FP8X4), z_s[s][:, a], fp4[a], fp4_s[a], start=(a == 0), stop=False)
-            nc.tensor.matmul_mx(z[:], z_w[s][:, 2].bitcast(FP8X4), z_s[s][:, 2], fp8, fp8_s, start=False, stop=True)
-            mix = sbuf("mix%d" % step, [P, HALF], F32)
-            at = sbuf("at%d" % step, [P, HALF], F32)
-            gate = sbuf("gate%d" % step, [P, HALF], F32)
-            weighted = work.tile([P, HALF], F32, name="weighted")
-            nc.scalar.activation(at[:], ht[:], ACT.Silu, bias=no_bias[:])
-            nc.scalar.activation(mix[:], hv[:], ACT.Silu, bias=no_bias[:])
-            nc.gpsimd.tensor_tensor(mix[:], mix[:], at[:], ALU.subtract)
-            width = HALF // 2 if step == 0 else HALF
-            for c in range(0, HALF, width):
-                cs = slice(c, c + width)
-                nc.scalar.activation(gate[:, cs], z[:, cs], ACT.Tanh, bias=half_b[:, s : s + 1], scale=0.5)
-                nc.scalar.activation(gate[:, cs], gate[:, cs], ACT.Identity, bias=0.5, scale=0.5)
-                nc.gpsimd.tensor_tensor(mix[:, cs], mix[:, cs], gate[:, cs], ALU.mult)
-                nc.gpsimd.tensor_tensor(mix[:, cs], mix[:, cs], at[:, cs], ALU.add)
-                nc.vector.tensor_tensor(weighted[:, cs], mix[:, cs], wgo_ps[h][:, cs], ALU.mult)
-                nc.vector.tensor_copy(page[:].indirect(entries(idx, h * HALF + c, width)), weighted[:, cs])
-            if step < len(Z_GROUPS) - 1:
-                make_z(step + 1)
-            if step < PAGES - 2:
-                for c in range(0, T, BANK):
-                    nc.gpsimd.memset(pages[step + 2][:, c : c + BANK], 0.0)
-            if h == HALVES - 1:
-                dma(out=out_0[cols, :], in_=page[:])
+        gather_v_scales(0, sbuf("v_s0", [P, HALF], U8))
+        gather_v_words(0)
+        gather_v_words(1)
+        load_z(1)
+        gather_v2_words(1, placed("pairs1", [P, HALF], U32, PAIRS_AT))
+        gather_v_scales(1, placed("v_s1", [P, HALF], U8, V_S_AT))
 
         out_s = sbuf("out_s", [P, SLICES, BANK], U8)
-        for s in range(SLICES):
+
+        def make_planes(s, turn_banks, back_banks):
+            last = s == SLICES - 1
             blocks = pages[s][:].rearrange("p (g k c) -> p k g c", g=QUADS, c=P)
             out_w = sbuf("out_w%d" % s, [P, BANK], U32)
             for half in range(2):
-                back = bank(4 + half, "back")
+                back = bank(back_banks[half], "back")
                 for k2 in range(2):
                     k = 2 * half + k2
-                    turned = bank(k, "turned")
+                    turned = bank(turn_banks[k], "turned")
                     for g in range(QUADS):
                         nc.tensor.transpose(turned[:, g * P : (g + 1) * P], blocks[:, k, g], ident[:])
                     rounded = sbuf("rounded%d_%d" % (s, k), [P, BANK], BF16)
-                    copy = nc.vector.tensor_copy if s == SLICES - 1 and k2 == 0 else nc.scalar.copy
+                    copy = nc.vector.tensor_copy if last and k2 == 1 else nc.scalar.copy
                     copy(
                         rounded[:].rearrange("p (u m e) -> p u m e", u=2, e=2),
                         turned[:].rearrange("p (m u e) -> p u m e", u=2, e=2),
@@ -265,7 +217,7 @@ def tile_list_gmu_silu_scatP_kernel(
                         c0 = (2 * k2 + u) * P
                         nc.tensor.transpose(back[:, c0 : c0 + P], rounded[:].bitcast(F32)[:, u * P : (u + 1) * P], ident[:])
                 grouped = sbuf("grouped%d_%d" % (s, half), [P, 2 * BANK], BF16)
-                copy = nc.vector.tensor_copy if s == SLICES - 1 and half == 0 else nc.scalar.copy
+                copy = nc.vector.tensor_copy if last and half == 1 else nc.scalar.copy
                 copy(
                     grouped[:].bitcast(F32).rearrange("p (k c u) -> p k c u", k=2, u=2),
                     back[:].rearrange("p (k u c) -> p k c u", k=2, u=2),
@@ -273,11 +225,57 @@ def tile_list_gmu_silu_scatP_kernel(
                 ws = slice(half * 2 * P, (half + 1) * 2 * P)
                 nc.vector.quantize_mx(out_w[:, ws].bitcast(FP8X4), out_s[:, s, ws], grouped[:])
             for g in range(QUADS):
-                queue = nc.scalar if s == SLICES - 1 and g % 2 else nc.sync
+                queue = nc.scalar if last and g % 2 else nc.sync
                 queue.dma_start(
                     out=as_words(out_1[0])[32 * s : 32 * (s + 1), g * BANK : (g + 1) * BANK],
                     in_=out_w[32 * g : 32 * (g + 1), :].bitcast(I32),
                 )
+
+        for step, (s, h) in enumerate(STEPS):
+            cols = slice(s * P, (s + 1) * P)
+            group_cols = slice(s % 2 * P, (s % 2 + 1) * P)
+            js = slice(h * HALF, (h + 1) * HALF)
+            fp8, fp8_s = v_w[h][:].bitcast(FP8X4), v_s[h][:]
+            fp4 = [v2_w[h][:, a, :].bitcast(FP4X4) for a in range(2)]
+            fp4_s = [v2_s[:, js], lowered[:, js]]
+            ht = bank(2 * step % 3, "ht")
+            hv = bank((2 * step + 1) % 3, "hv")
+            z = bank((2 * step + 2) % 3, "z")
+            for a in range(2):
+                nc.tensor.matmul_mx(
+                    ht[:], w_w[s // 2][:, a, group_cols].bitcast(FP8X4), w_s[:, a, cols], fp4[a], fp4_s[a], start=(a == 0), stop=(a == 1)
+                )
+            for a in range(2):
+                nc.tensor.matmul_mx(z[:], z_w[s][:, a].bitcast(FP8X4), z_s[s][:, a], fp4[a], fp4_s[a], start=(a == 0), stop=False)
+            nc.tensor.matmul_mx(hv[:], w_w[s // 2][:, 2, group_cols].bitcast(FP8X4), w_s[:, 2, cols], fp8, fp8_s, start=True, stop=True)
+            nc.tensor.matmul_mx(z[:], z_w[s][:, 2].bitcast(FP8X4), z_s[s][:, 2], fp8, fp8_s, start=False, stop=True)
+            if step == 0:
+                for i in range(J // P):
+                    half, c = divmod(i * P, HALF)
+                    nc.tensor.transpose(wgo_ps[half][:, c : c + P], wgo_cols[:, i : i + 1].to_broadcast([P, P]), ident[:])
+            av = sbuf("av%d" % step, [P, HALF], F32)
+            at = sbuf("at%d" % step, [P, HALF], F32)
+            gate = sbuf("gate%d" % step, [P, HALF], F32)
+            nc.scalar.activation(at[:], ht[:], ACT.Silu, bias=no_bias[:])
+            nc.scalar.activation(av[:], hv[:], ACT.Silu, bias=no_bias[:])
+            nc.scalar.activation(gate[:], z[:], ACT.Tanh, bias=half_b[:, s : s + 1], scale=0.5)
+            nc.scalar.activation(gate[:], gate[:], ACT.Identity, bias=0.5, scale=0.5)
+            if step == 2:
+                make_z(1)
+            if step == len(STEPS) - 1:
+                for early_page in range(SLICES - 1):
+                    make_planes(early_page, [3, 4, 3, 4], [5, 5])
+            held = {2: "zv_bf1", 7: "grouped2_0"}
+            weighted = sbuf("weighted%d" % step, [P, HALF], F32, held.get(step, "weighted%d" % (step % 2)))
+            nc.gpsimd.tensor_tensor(av[:], av[:], at[:], ALU.subtract)
+            nc.gpsimd.tensor_tensor(av[:], av[:], gate[:], ALU.mult)
+            nc.gpsimd.tensor_tensor(av[:], av[:], at[:], ALU.add)
+            nc.vector.tensor_tensor(weighted[:], av[:], wgo_ps[h][:], ALU.mult)
+            nc.vector.tensor_copy(pages[s][:].indirect(entries(idx, h * HALF, HALF)), weighted[:])
+            if h == HALVES - 1:
+                dma(out=out_0[cols, :], in_=pages[s][:])
+
+        make_planes(SLICES - 1, [3, 4, 0, 1], [5, 2])
         for g in range(QUADS):
             queue = nc.scalar if g % 2 else nc.sync
             queue.dma_start(

@@ -33,6 +33,7 @@ V_S_AT = PAIRS_AT + HALF
 LATE_Z_AT = [0, V_S_AT + HALF // 4, V_S_AT + HALF // 4 + Z_WORDS]
 W_AT = LATE_Z_AT[2] + Z_WORDS
 Z_AT = W_AT + 3 * N
+VECTOR_STEPS = (0,)
 STEPS = [(0, 0), (1, 0), (0, 1), (1, 1), (2, 0), (2, 1), (3, 0), (3, 1)]
 
 
@@ -68,13 +69,25 @@ def tile_list_gmu_silu_scatP_kernel(
         tab2_s = sbuf("tab2_s", [P, T], U8)
         tab2_w = sbuf("tab2_w", [P, T], U32)
         lowered = sbuf("lowered", [P, J], U8)
-        pages = [sbuf("page%d" % t, [P, T], F32) for t in range(SLICES)]
+        pages = [sbuf("page%d" % t, [P, T], F32) for t in range(SLICES - 1)]
         ident = sbuf("ident", [P, P], F32)
         no_bias = sbuf("no_bias", [P, 1], F32)
 
         zeros = sbuf("zeros", [P, P], F32)
-        nc.gpsimd.memset(zeros[:], 0.0)
+        w_s = sbuf("w_s", [P, 3, N], U8)
+        rows = sbuf("rows", [P, P], F32)
+
+        def clear_page(t):
+            for c in range(0, T, BANK):
+                nc.gpsimd.memset(pages[t][:, c : c + BANK], 0.0)
+
         nc.gpsimd.memset(tab2_s[:].bitcast(I32), 0)
+        nc.gpsimd.memset(zeros[:], 0.0)
+        nc.gpsimd.memset(lowered[:].bitcast(I32), 0)
+        clear_page(2)
+        nc.gpsimd.memset(tab_s[:].bitcast(I32), 0)
+        nc.gpsimd.memset(w_s[:].rearrange("p a n -> p (a n)").bitcast(I32), 0)
+        nc.gpsimd.memset(rows[:], 0.0)
         nc.gpsimd.affine_select(
             out=ident[:], in_=zeros[:], pattern=[[-1, P]], compare_op=ALU.not_equal, fill=1.0, base=0, channel_multiplier=1
         )
@@ -83,14 +96,9 @@ def tile_list_gmu_silu_scatP_kernel(
             nc.vector.memset(zero[:, 0:1], 0.0)
             nc.scalar.activation(no_bias[:], zero[:, 0:1], ACT.Silu)
         w_pool = ctx.enter_context(tc.tile_pool(name="w_pool", bufs=1))
-        nc.vector.memset(lowered[:].bitcast(I32), 0)
-        nc.vector.memset(pages[0][:, 0:ODD], 0.0)
-        nc.vector.memset(pages[0][:, ODD:T], 0.0)
-        nc.vector.memset(tab_s[:].bitcast(I32), 0)
-        w_s = sbuf("w_s", [P, 3, N], U8)
-        nc.vector.memset(w_s[:].rearrange("p a n -> p (a n)").bitcast(I32), 0)
-        rows = sbuf("rows", [P, P], F32)
-        nc.vector.memset(rows[:], 0.0)
+        for t in range(2):
+            nc.vector.memset(pages[t][:, 0:ODD], 0.0)
+            nc.vector.memset(pages[t][:, ODD:T], 0.0)
 
         def placed(name, shape, dtype, word):
             return w_pool.tile(shape, dtype, name=name, align_bytes=64, offset=4 * word)
@@ -99,9 +107,6 @@ def tile_list_gmu_silu_scatP_kernel(
         w_w = [placed("w_w%d" % g, [P, 3, Z_COLS], U32, W_AT + 3 * g * Z_COLS) for g in range(2)]
         z_raw = {(0, a): placed("z_raw0_%d" % a, [P, PACK, Z_COLS], F32, Z_AT + a * Z_WORDS) for a in range(3)}
 
-        for t in range(1, SLICES):
-            for c in range(0, T, BANK):
-                nc.gpsimd.memset(pages[t][:, c : c + BANK], 0.0)
 
         z_src = [by_partition(zt[0:512, :]), by_partition(zt[512:1024, :]), by_partition(zv)]
 
@@ -193,22 +198,24 @@ def tile_list_gmu_silu_scatP_kernel(
         load_z(1)
         gather_v2_words(1, placed("pairs1", [P, HALF], U32, PAIRS_AT))
         gather_v_scales(1, placed("v_s1", [P, HALF], U8, V_S_AT))
+        pages.append(sbuf("page3", [P, T], F32, "tab_s"))
+        clear_page(3)
 
         out_s = sbuf("out_s", [P, SLICES, BANK], U8)
+        grouped = {}
 
-        def make_planes(s, turn_banks, back_banks):
+        def regroup(s, turn_banks, back_banks):
             last = s == SLICES - 1
             blocks = pages[s][:].rearrange("p (g k c) -> p k g c", g=QUADS, c=P)
-            out_w = sbuf("out_w%d" % s, [P, BANK], U32)
             for half in range(2):
                 back = bank(back_banks[half], "back")
+                copy = nc.vector.tensor_copy if last and half == 1 else nc.scalar.copy
                 for k2 in range(2):
                     k = 2 * half + k2
                     turned = bank(turn_banks[k], "turned")
                     for g in range(QUADS):
                         nc.tensor.transpose(turned[:, g * P : (g + 1) * P], blocks[:, k, g], ident[:])
                     rounded = sbuf("rounded%d_%d" % (s, k), [P, BANK], BF16)
-                    copy = nc.vector.tensor_copy if last and k2 == 1 else nc.scalar.copy
                     copy(
                         rounded[:].rearrange("p (u m e) -> p u m e", u=2, e=2),
                         turned[:].rearrange("p (m u e) -> p u m e", u=2, e=2),
@@ -216,20 +223,21 @@ def tile_list_gmu_silu_scatP_kernel(
                     for u in range(2):
                         c0 = (2 * k2 + u) * P
                         nc.tensor.transpose(back[:, c0 : c0 + P], rounded[:].bitcast(F32)[:, u * P : (u + 1) * P], ident[:])
-                grouped = sbuf("grouped%d_%d" % (s, half), [P, 2 * BANK], BF16)
-                copy = nc.vector.tensor_copy if last and half == 1 else nc.scalar.copy
-                copy(
-                    grouped[:].bitcast(F32).rearrange("p (k c u) -> p k c u", k=2, u=2),
+                grouped[s, half] = sbuf("grouped%d_%d" % (s, half), [P, 2 * BANK], BF16)
+                nc.scalar.copy(
+                    grouped[s, half][:].bitcast(F32).rearrange("p (k c u) -> p k c u", k=2, u=2),
                     back[:].rearrange("p (k u c) -> p k c u", k=2, u=2),
                 )
-                ws = slice(half * 2 * P, (half + 1) * 2 * P)
-                nc.vector.quantize_mx(out_w[:, ws].bitcast(FP8X4), out_s[:, s, ws], grouped[:])
+
+        def quantise(s0, s1, after, queues):
+            out_w = sbuf("out_w%d" % s0, [P, s1 - s0, BANK], U32, after)
+            for s in range(s0, s1):
+                for half in range(2):
+                    ws = slice(half * 2 * P, (half + 1) * 2 * P)
+                    nc.vector.quantize_mx(out_w[:, s - s0, ws].bitcast(FP8X4), out_s[:, s, ws], grouped[s, half][:])
+            rows_out = as_words(out_1[0]).rearrange("(s q) (g c) -> g q s c", s=SLICES, g=QUADS)
             for g in range(QUADS):
-                queue = nc.scalar if last and g % 2 else nc.sync
-                queue.dma_start(
-                    out=as_words(out_1[0])[32 * s : 32 * (s + 1), g * BANK : (g + 1) * BANK],
-                    in_=out_w[32 * g : 32 * (g + 1), :].bitcast(I32),
-                )
+                queues[g % 2].dma_start(out=rows_out[g][:, s0:s1], in_=out_w[32 * g : 32 * (g + 1)].bitcast(I32))
 
         for step, (s, h) in enumerate(STEPS):
             cols = slice(s * P, (s + 1) * P)
@@ -249,33 +257,41 @@ def tile_list_gmu_silu_scatP_kernel(
                 nc.tensor.matmul_mx(z[:], z_w[s][:, a].bitcast(FP8X4), z_s[s][:, a], fp4[a], fp4_s[a], start=(a == 0), stop=False)
             nc.tensor.matmul_mx(hv[:], w_w[s // 2][:, 2, group_cols].bitcast(FP8X4), w_s[:, 2, cols], fp8, fp8_s, start=True, stop=True)
             nc.tensor.matmul_mx(z[:], z_w[s][:, 2].bitcast(FP8X4), z_s[s][:, 2], fp8, fp8_s, start=False, stop=True)
-            if step == 0:
-                for i in range(J // P):
-                    half, c = divmod(i * P, HALF)
-                    nc.tensor.transpose(wgo_ps[half][:, c : c + P], wgo_cols[:, i : i + 1].to_broadcast([P, P]), ident[:])
+            if s == 0:
+                for c in range(0, HALF, P):
+                    i = (h * HALF + c) // P
+                    nc.tensor.transpose(wgo_ps[h][:, c : c + P], wgo_cols[:, i : i + 1].to_broadcast([P, P]), ident[:])
             av = sbuf("av%d" % step, [P, HALF], F32)
             at = sbuf("at%d" % step, [P, HALF], F32)
             gate = sbuf("gate%d" % step, [P, HALF], F32)
             nc.scalar.activation(at[:], ht[:], ACT.Silu, bias=no_bias[:])
             nc.scalar.activation(av[:], hv[:], ACT.Silu, bias=no_bias[:])
             nc.scalar.activation(gate[:], z[:], ACT.Tanh, bias=half_b[:, s : s + 1], scale=0.5)
-            nc.scalar.activation(gate[:], gate[:], ACT.Identity, bias=0.5, scale=0.5)
+            if step not in VECTOR_STEPS:
+                nc.scalar.activation(gate[:], gate[:], ACT.Identity, bias=0.5, scale=0.5)
             if step == 2:
                 make_z(1)
             if step == len(STEPS) - 1:
                 for early_page in range(SLICES - 1):
-                    make_planes(early_page, [3, 4, 3, 4], [5, 5])
-            held = {2: "zv_bf1", 7: "grouped2_0"}
+                    regroup(early_page, [3, 4, 3, 4], [5, 5])
+            held = {2: "zv_bf1", 7: "rounded2_3"}
             weighted = sbuf("weighted%d" % step, [P, HALF], F32, held.get(step, "weighted%d" % (step % 2)))
-            nc.gpsimd.tensor_tensor(av[:], av[:], at[:], ALU.subtract)
-            nc.gpsimd.tensor_tensor(av[:], av[:], gate[:], ALU.mult)
-            nc.gpsimd.tensor_tensor(av[:], av[:], at[:], ALU.add)
+            if step in VECTOR_STEPS:
+                nc.vector.tensor_tensor(av[:], av[:], at[:], ALU.subtract)
+                nc.vector.scalar_tensor_tensor(av[:], gate[:], 1.0, av[:], ALU.add, ALU.mult)
+                nc.vector.scalar_tensor_tensor(av[:], av[:], 0.5, at[:], ALU.mult, ALU.add)
+            else:
+                nc.gpsimd.tensor_tensor(av[:], av[:], at[:], ALU.subtract)
+                nc.gpsimd.tensor_tensor(av[:], av[:], gate[:], ALU.mult)
+                nc.gpsimd.tensor_tensor(av[:], av[:], at[:], ALU.add)
             nc.vector.tensor_tensor(weighted[:], av[:], wgo_ps[h][:], ALU.mult)
             nc.vector.tensor_copy(pages[s][:].indirect(entries(idx, h * HALF, HALF)), weighted[:])
             if h == HALVES - 1:
                 dma(out=out_0[cols, :], in_=pages[s][:])
 
-        make_planes(SLICES - 1, [3, 4, 0, 1], [5, 2])
+        quantise(0, SLICES - 1, "rounded2_3", [nc.sync, nc.sync])
+        regroup(SLICES - 1, [3, 4, 0, 1], [5, 2])
+        quantise(SLICES - 1, SLICES, None, [nc.sync, nc.scalar])
         for g in range(QUADS):
             queue = nc.scalar if g % 2 else nc.sync
             queue.dma_start(

@@ -33,6 +33,8 @@ V_S_AT = PAIRS_AT + HALF
 LATE_Z_AT = [0, V_S_AT + HALF // 4, V_S_AT + HALF // 4 + Z_WORDS]
 W_AT = LATE_Z_AT[2] + Z_WORDS
 Z_AT = W_AT + 3 * N
+TURN_BANKS = (0, 1, 3, 4)
+BACK_BANKS = (2, 5)
 VECTOR_STEPS = (0,)
 STEPS = [(0, 0), (1, 0), (0, 1), (1, 1), (2, 0), (2, 1), (3, 0), (3, 1)]
 
@@ -184,7 +186,7 @@ def tile_list_gmu_silu_scatP_kernel(
         gather_v2_words(0, sbuf("pairs0", [P, HALF], U32))
         make_z(0)
 
-        turned = bank(3, "turned")
+        turned = bank(7, "turned")
         nc.tensor.transpose(turned[:, 0:P], rows[:], ident[:])
         wgo_cols = sbuf("wgo_cols", [P, J // P], F32)
         nc.scalar.copy(wgo_cols[:], turned[:, 0 : J // P])
@@ -204,15 +206,15 @@ def tile_list_gmu_silu_scatP_kernel(
         out_s = sbuf("out_s", [P, SLICES, BANK], U8)
         grouped = {}
 
-        def regroup(s, turn_banks, back_banks):
+        def regroup(s):
             last = s == SLICES - 1
             blocks = pages[s][:].rearrange("p (g k c) -> p k g c", g=QUADS, c=P)
             for half in range(2):
-                back = bank(back_banks[half], "back")
+                back = bank(BACK_BANKS[half], "back")
                 copy = nc.vector.tensor_copy if last and half == 1 else nc.scalar.copy
                 for k2 in range(2):
                     k = 2 * half + k2
-                    turned = bank(turn_banks[k], "turned")
+                    turned = bank(TURN_BANKS[k], "turned")
                     for g in range(QUADS):
                         nc.tensor.transpose(turned[:, g * P : (g + 1) * P], blocks[:, k, g], ident[:])
                     rounded = sbuf("rounded%d_%d" % (s, k), [P, BANK], BF16)
@@ -246,9 +248,10 @@ def tile_list_gmu_silu_scatP_kernel(
             fp8, fp8_s = v_w[h][:].bitcast(FP8X4), v_s[h][:]
             fp4 = [v2_w[h][:, a, :].bitcast(FP4X4) for a in range(2)]
             fp4_s = [v2_s[:, js], lowered[:, js]]
-            ht = bank(2 * step % 3, "ht")
-            hv = bank((2 * step + 1) % 3, "hv")
-            z = bank((2 * step + 2) % 3, "z")
+            first = 3 * (step % 2)
+            ht = bank(first + step // 2 % 2, "ht")
+            hv = bank(first + 1 - step // 2 % 2, "hv")
+            z = bank(first + 2, "z")
             for a in range(2):
                 nc.tensor.matmul_mx(
                     ht[:], w_w[s // 2][:, a, group_cols].bitcast(FP8X4), w_s[:, a, cols], fp4[a], fp4_s[a], start=(a == 0), stop=(a == 1)
@@ -273,8 +276,8 @@ def tile_list_gmu_silu_scatP_kernel(
                 make_z(1)
             if step == len(STEPS) - 1:
                 for early_page in range(SLICES - 1):
-                    regroup(early_page, [3, 4, 3, 4], [5, 5])
-            held = {2: "zv_bf1", 7: "rounded2_3"}
+                    regroup(early_page)
+            held = {2: "zv_bf1", 7: "rounded2_2"}
             weighted = sbuf("weighted%d" % step, [P, HALF], F32, held.get(step, "weighted%d" % (step % 2)))
             if step in VECTOR_STEPS:
                 nc.vector.tensor_tensor(av[:], av[:], at[:], ALU.subtract)
@@ -289,8 +292,8 @@ def tile_list_gmu_silu_scatP_kernel(
             if h == HALVES - 1:
                 dma(out=out_0[cols, :], in_=pages[s][:])
 
-        quantise(0, SLICES - 1, "rounded2_3", [nc.sync, nc.sync])
-        regroup(SLICES - 1, [3, 4, 0, 1], [5, 2])
+        quantise(0, SLICES - 1, "rounded2_2", [nc.sync, nc.gpsimd])
+        regroup(SLICES - 1)
         quantise(SLICES - 1, SLICES, None, [nc.sync, nc.scalar])
         for g in range(QUADS):
             queue = nc.scalar if g % 2 else nc.sync

@@ -35,6 +35,8 @@ W_AT = LATE_Z_AT[2] + Z_WORDS
 Z_AT = W_AT + 3 * N
 TURN_BANKS = (0, 1, 3, 4)
 BACK_BANKS = (2, 5)
+LAST_TURN_BANKS = (5, 4, 5, 4)
+LAST_BACK_BANKS = (2, 3)
 VECTOR_STEPS = (0,)
 STEPS = [(0, 0), (1, 0), (0, 1), (1, 1), (2, 0), (2, 1), (3, 0), (3, 1)]
 
@@ -131,8 +133,8 @@ def tile_list_gmu_silu_scatP_kernel(
         load_z(0)
         for q in range(QUADS):
             dma(out=tab_s[32 * q : 32 * q + 4, :].bitcast(I32), in_=tab_scales[0, 4 * q : 4 * q + 4, :].bitcast(I32))
-        dma(out=tab_w[:].bitcast(I32), in_=as_words(tab_words[0]))
         load_w(0)
+        dma(out=tab_w[:].bitcast(I32), in_=as_words(tab_words[0]))
 
         v_w, v_s, v2_w = {}, {}, {}
         v2_s = sbuf("v2_s", [P, J], U8)
@@ -152,39 +154,42 @@ def tile_list_gmu_silu_scatP_kernel(
 
         z_w, z_s = {}, {}
 
-        def make_z(group):
-            codes = sbuf("z_w%d" % group, [P, 3, Z_COLS], U32)
-            scales = sbuf("z_s%d" % group, [P, 3, Z_COLS], U8)
+        def make_z(s0, s1):
+            width = (s1 - s0) * P
+            c0 = s0 % 2 * P
+            codes = sbuf("z_w%d" % s0, [P, 3, width], U32)
+            scales = sbuf("z_s%d" % s0, [P, 3, width], U8)
             for name, a0, a1 in (("zt", 0, 2), ("zv", 2, 3)):
-                rounded = sbuf("%s_bf%d" % (name, group), [P, a1 - a0, PACK * Z_COLS], BF16)
+                rounded = sbuf("%s_bf%d" % (name, s0), [P, a1 - a0, PACK * width], BF16)
                 for a in range(a0, a1):
                     nc.scalar.copy(
                         rounded[:, a - a0].rearrange("p (c e i) -> p c i e", e=4, i=PACK),
-                        z_raw[group, a][:].rearrange("p i (c e) -> p c i e", e=4),
+                        z_raw[s0 // 2, a][:, :, c0 : c0 + width].rearrange("p i (c e) -> p c i e", e=4),
                     )
                 nc.vector.quantize_mx(
                     codes[:, a0:a1].rearrange("p a n -> p (a n)").bitcast(FP8X4),
                     scales[:, a0:a1].rearrange("p a n -> p (a n)"),
                     rounded[:].rearrange("p a n -> p (a n)"),
                 )
-            for s in range(2):
-                z_w[2 * group + s] = codes[:, :, s * P : (s + 1) * P]
-                z_s[2 * group + s] = scales[:, :, s * P : (s + 1) * P]
+            for s in range(s0, s1):
+                z_w[s] = codes[:, :, (s - s0) * P : (s - s0 + 1) * P]
+                z_s[s] = scales[:, :, (s - s0) * P : (s - s0 + 1) * P]
 
         nc.vector.tensor_copy(v2_s[:], tab2_s[:].indirect(idx2[:]))
-        dma(out=lowered[0:SHIFT_ROWS, :].bitcast(I32), in_=v2_s[4 : 4 + SHIFT_ROWS, :].bitcast(I32))
         for q in range(QUADS):
             dma(
                 out=w_s[32 * q : 32 * q + 4, 0:2].bitcast(I32),
                 in_=wt_scales[:, 4 * q : 4 * q + 4, :].bitcast(I32).rearrange("a r n -> r a n"),
             )
+        dma(out=lowered[0:SHIFT_ROWS, :].bitcast(I32), in_=v2_s[4 : 4 + SHIFT_ROWS, :].bitcast(I32))
         for q in range(QUADS):
-            dma(out=w_s[32 * q : 32 * q + 4, 2].bitcast(I32), in_=wv_scales[0, 4 * q : 4 * q + 4, :].bitcast(I32))
+            queue = nc.sync if q < 2 else nc.gpsimd
+            queue.dma_start(out=w_s[32 * q : 32 * q + 4, 2].bitcast(I32), in_=wv_scales[0, 4 * q : 4 * q + 4, :].bitcast(I32))
         dma(out=rows[0 : J // P, :], in_=wgo[0:1, :].rearrange("r (i n) -> (r i) n", n=P))
         dma(out=rows[J // P : J // P + SLICES, :], in_=b.rearrange("(s n) -> s n", n=P))
         load_w(1)
         gather_v2_words(0, sbuf("pairs0", [P, HALF], U32))
-        make_z(0)
+        make_z(0, 2)
 
         turned = bank(7, "turned")
         nc.tensor.transpose(turned[:, 0:P], rows[:], ident[:])
@@ -198,6 +203,8 @@ def tile_list_gmu_silu_scatP_kernel(
         gather_v_words(0)
         gather_v_words(1)
         load_z(1)
+        wgo_last = placed("wgo_last", [P, HALF], F32, Z_AT)
+        dma(out=wgo_last[:], in_=wgo[:, J - HALF : J])
         gather_v2_words(1, placed("pairs1", [P, HALF], U32, PAIRS_AT))
         gather_v_scales(1, placed("v_s1", [P, HALF], U8, V_S_AT))
         pages.append(sbuf("page3", [P, T], F32, "tab_s"))
@@ -210,11 +217,11 @@ def tile_list_gmu_silu_scatP_kernel(
             last = s == SLICES - 1
             blocks = pages[s][:].rearrange("p (g k c) -> p k g c", g=QUADS, c=P)
             for half in range(2):
-                back = bank(BACK_BANKS[half], "back")
+                back = bank((LAST_BACK_BANKS if last else BACK_BANKS)[half], "back")
                 copy = nc.vector.tensor_copy if last and half == 1 else nc.scalar.copy
                 for k2 in range(2):
                     k = 2 * half + k2
-                    turned = bank(TURN_BANKS[k], "turned")
+                    turned = bank((LAST_TURN_BANKS if last else TURN_BANKS)[k], "turned")
                     for g in range(QUADS):
                         nc.tensor.transpose(turned[:, g * P : (g + 1) * P], blocks[:, k, g], ident[:])
                     rounded = sbuf("rounded%d_%d" % (s, k), [P, BANK], BF16)
@@ -272,13 +279,11 @@ def tile_list_gmu_silu_scatP_kernel(
             nc.scalar.activation(gate[:], z[:], ACT.Tanh, bias=half_b[:, s : s + 1], scale=0.5)
             if step not in VECTOR_STEPS:
                 nc.scalar.activation(gate[:], gate[:], ACT.Identity, bias=0.5, scale=0.5)
-            if step == 2:
-                make_z(1)
+            if step in (1, 3):
+                make_z(2 + step // 2, 3 + step // 2)
             if step == len(STEPS) - 1:
                 for early_page in range(SLICES - 1):
                     regroup(early_page)
-            held = {2: "zv_bf1", 7: "rounded2_2"}
-            weighted = sbuf("weighted%d" % step, [P, HALF], F32, held.get(step, "weighted%d" % (step % 2)))
             if step in VECTOR_STEPS:
                 nc.vector.tensor_tensor(av[:], av[:], at[:], ALU.subtract)
                 nc.vector.scalar_tensor_tensor(av[:], gate[:], 1.0, av[:], ALU.add, ALU.mult)
@@ -287,12 +292,17 @@ def tile_list_gmu_silu_scatP_kernel(
                 nc.gpsimd.tensor_tensor(av[:], av[:], at[:], ALU.subtract)
                 nc.gpsimd.tensor_tensor(av[:], av[:], gate[:], ALU.mult)
                 nc.gpsimd.tensor_tensor(av[:], av[:], at[:], ALU.add)
-            nc.vector.tensor_tensor(weighted[:], av[:], wgo_ps[h][:], ALU.mult)
-            nc.vector.tensor_copy(pages[s][:].indirect(entries(idx, h * HALF, HALF)), weighted[:])
+            places = pages[s][:].indirect(entries(idx, h * HALF, HALF))
+            if step == len(STEPS) - 1:
+                nc.vector.tensor_tensor(places, av[:], wgo_last[:], ALU.mult)
+            else:
+                weighted = sbuf("weighted%d" % step, [P, HALF], F32, {2: "zv_bf2", 4: "zv_bf3"}.get(step, "weighted%d" % (step % 2)))
+                nc.vector.tensor_tensor(weighted[:], av[:], wgo_ps[h][:], ALU.mult)
+                nc.vector.tensor_copy(places, weighted[:])
             if h == HALVES - 1:
                 dma(out=out_0[cols, :], in_=pages[s][:])
 
-        quantise(0, SLICES - 1, "rounded2_2", [nc.sync, nc.gpsimd])
+        quantise(0, SLICES - 1, "av7", [nc.sync, nc.gpsimd])
         regroup(SLICES - 1)
         quantise(SLICES - 1, SLICES, None, [nc.sync, nc.scalar])
         for g in range(QUADS):

@@ -33,11 +33,11 @@ V_S_AT = PAIRS_AT + HALF
 LATE_Z_AT = [0, V_S_AT + HALF // 4, V_S_AT + HALF // 4 + Z_WORDS]
 W_AT = LATE_Z_AT[2] + Z_WORDS
 Z_AT = W_AT + 3 * N
+WGO_AT = Z_AT + 3 * Z_WORDS
 TURN_BANKS = (0, 1, 3, 4)
 BACK_BANKS = (2, 5)
 LAST_TURN_BANKS = (5, 4, 5, 4)
 LAST_BACK_BANKS = (2, 3)
-VECTOR_STEPS = (0,)
 STEPS = [(0, 0), (1, 0), (0, 1), (1, 1), (2, 0), (2, 1), (3, 0), (3, 1)]
 
 
@@ -73,7 +73,7 @@ def tile_list_gmu_silu_scatP_kernel(
         tab2_s = sbuf("tab2_s", [P, T], U8)
         tab2_w = sbuf("tab2_w", [P, T], U32)
         lowered = sbuf("lowered", [P, J], U8)
-        pages = [sbuf("page%d" % t, [P, T], F32) for t in range(SLICES - 1)]
+        pages = {t: sbuf("page%d" % t, [P, T], F32) for t in (0, 2)}
         ident = sbuf("ident", [P, P], F32)
         no_bias = sbuf("no_bias", [P, 1], F32)
 
@@ -96,19 +96,19 @@ def tile_list_gmu_silu_scatP_kernel(
             out=ident[:], in_=zeros[:], pattern=[[-1, P]], compare_op=ALU.not_equal, fill=1.0, base=0, channel_multiplier=1
         )
         with tc.tile_pool(name="early", bufs=1) as early:
-            zero = sbuf("zero", [P, Z_AT + 3 * Z_WORDS], F32, pool=early)
+            zero = sbuf("zero", [P, WGO_AT + J], F32, pool=early)
             nc.vector.memset(zero[:, 0:1], 0.0)
             nc.scalar.activation(no_bias[:], zero[:, 0:1], ACT.Silu)
         w_pool = ctx.enter_context(tc.tile_pool(name="w_pool", bufs=1))
-        for t in range(2):
-            nc.vector.memset(pages[t][:, 0:ODD], 0.0)
-            nc.vector.memset(pages[t][:, ODD:T], 0.0)
+        nc.vector.memset(pages[0][:, 0:ODD], 0.0)
+        nc.vector.memset(pages[0][:, ODD:T], 0.0)
 
         def placed(name, shape, dtype, word):
             return w_pool.tile(shape, dtype, name=name, align_bytes=64, offset=4 * word)
 
         tab_w = placed("tab_w", [P, T], U32, TAB_AT)
         w_w = [placed("w_w%d" % g, [P, 3, Z_COLS], U32, W_AT + 3 * g * Z_COLS) for g in range(2)]
+        wgo_sb = placed("wgo_sb", [P, J], F32, WGO_AT)
         z_raw = {(0, a): placed("z_raw0_%d" % a, [P, PACK, Z_COLS], F32, Z_AT + a * Z_WORDS) for a in range(3)}
 
 
@@ -183,32 +183,26 @@ def tile_list_gmu_silu_scatP_kernel(
             )
         dma(out=lowered[0:SHIFT_ROWS, :].bitcast(I32), in_=v2_s[4 : 4 + SHIFT_ROWS, :].bitcast(I32))
         for q in range(QUADS):
-            queue = nc.sync if q < 2 else nc.gpsimd
-            queue.dma_start(out=w_s[32 * q : 32 * q + 4, 2].bitcast(I32), in_=wv_scales[0, 4 * q : 4 * q + 4, :].bitcast(I32))
-        dma(out=rows[0 : J // P, :], in_=wgo[0:1, :].rearrange("r (i n) -> (r i) n", n=P))
-        dma(out=rows[J // P : J // P + SLICES, :], in_=b.rearrange("(s n) -> s n", n=P))
+            dma(out=w_s[32 * q : 32 * q + 4, 2].bitcast(I32), in_=wv_scales[0, 4 * q : 4 * q + 4, :].bitcast(I32))
+        dma(out=rows[0:SLICES, :], in_=b.rearrange("(s n) -> s n", n=P))
+        dma(out=wgo_sb[:], in_=wgo)
         load_w(1)
         gather_v2_words(0, sbuf("pairs0", [P, HALF], U32))
         make_z(0, 2)
 
         turned = bank(7, "turned")
         nc.tensor.transpose(turned[:, 0:P], rows[:], ident[:])
-        wgo_cols = sbuf("wgo_cols", [P, J // P], F32)
-        nc.scalar.copy(wgo_cols[:], turned[:, 0 : J // P])
         half_b = sbuf("half_b", [P, SLICES], F32)
-        nc.scalar.mul(half_b[:], turned[:, J // P : J // P + SLICES], 0.5)
-        wgo_ps = [bank(6 + h, "wgo_ps%d" % h) for h in range(HALVES)]
+        nc.scalar.mul(half_b[:], turned[:, 0:SLICES], 0.5)
 
         gather_v_scales(0, sbuf("v_s0", [P, HALF], U8))
         gather_v_words(0)
         gather_v_words(1)
         load_z(1)
-        wgo_last = placed("wgo_last", [P, HALF], F32, Z_AT)
-        dma(out=wgo_last[:], in_=wgo[:, J - HALF : J])
         gather_v2_words(1, placed("pairs1", [P, HALF], U32, PAIRS_AT))
         gather_v_scales(1, placed("v_s1", [P, HALF], U8, V_S_AT))
-        pages.append(sbuf("page3", [P, T], F32, "tab_s"))
-        clear_page(3)
+        pages[1] = sbuf("page1", [P, T], F32, "tab_s")
+        clear_page(1)
 
         out_s = sbuf("out_s", [P, SLICES, BANK], U8)
         grouped = {}
@@ -267,42 +261,29 @@ def tile_list_gmu_silu_scatP_kernel(
                 nc.tensor.matmul_mx(z[:], z_w[s][:, a].bitcast(FP8X4), z_s[s][:, a], fp4[a], fp4_s[a], start=(a == 0), stop=False)
             nc.tensor.matmul_mx(hv[:], w_w[s // 2][:, 2, group_cols].bitcast(FP8X4), w_s[:, 2, cols], fp8, fp8_s, start=True, stop=True)
             nc.tensor.matmul_mx(z[:], z_w[s][:, 2].bitcast(FP8X4), z_s[s][:, 2], fp8, fp8_s, start=False, stop=True)
-            if s == 0:
-                for c in range(0, HALF, P):
-                    i = (h * HALF + c) // P
-                    nc.tensor.transpose(wgo_ps[h][:, c : c + P], wgo_cols[:, i : i + 1].to_broadcast([P, P]), ident[:])
             av = sbuf("av%d" % step, [P, HALF], F32)
             at = sbuf("at%d" % step, [P, HALF], F32)
             gate = sbuf("gate%d" % step, [P, HALF], F32)
             nc.scalar.activation(at[:], ht[:], ACT.Silu, bias=no_bias[:])
             nc.scalar.activation(av[:], hv[:], ACT.Silu, bias=no_bias[:])
             nc.scalar.activation(gate[:], z[:], ACT.Tanh, bias=half_b[:, s : s + 1], scale=0.5)
-            if step not in VECTOR_STEPS:
-                nc.scalar.activation(gate[:], gate[:], ACT.Identity, bias=0.5, scale=0.5)
+            if step == 1:
+                pages[3] = sbuf("page3", [P, T], F32, "at0")
+                clear_page(3)
             if step in (1, 3):
                 make_z(2 + step // 2, 3 + step // 2)
             if step == len(STEPS) - 1:
                 for early_page in range(SLICES - 1):
                     regroup(early_page)
-            if step in VECTOR_STEPS:
-                nc.vector.tensor_tensor(av[:], av[:], at[:], ALU.subtract)
-                nc.vector.scalar_tensor_tensor(av[:], gate[:], 1.0, av[:], ALU.add, ALU.mult)
-                nc.vector.scalar_tensor_tensor(av[:], av[:], 0.5, at[:], ALU.mult, ALU.add)
-            else:
-                nc.gpsimd.tensor_tensor(av[:], av[:], at[:], ALU.subtract)
-                nc.gpsimd.tensor_tensor(av[:], av[:], gate[:], ALU.mult)
-                nc.gpsimd.tensor_tensor(av[:], av[:], at[:], ALU.add)
-            places = pages[s][:].indirect(entries(idx, h * HALF, HALF))
-            if step == len(STEPS) - 1:
-                nc.vector.tensor_tensor(places, av[:], wgo_last[:], ALU.mult)
-            else:
-                weighted = sbuf("weighted%d" % step, [P, HALF], F32, {2: "zv_bf2", 4: "zv_bf3"}.get(step, "weighted%d" % (step % 2)))
-                nc.vector.tensor_tensor(weighted[:], av[:], wgo_ps[h][:], ALU.mult)
-                nc.vector.tensor_copy(places, weighted[:])
+            mixed = sbuf("mixed%d" % step, [P, HALF], F32, {2: "zv_bf2", 4: "zv_bf3"}.get(step))
+            nc.vector.tensor_tensor(av[:], av[:], at[:], ALU.subtract)
+            nc.vector.scalar_tensor_tensor(av[:], gate[:], 1.0, av[:], ALU.add, ALU.mult)
+            nc.vector.scalar_tensor_tensor(mixed[:], av[:], 0.5, at[:], ALU.mult, ALU.add)
+            nc.vector.tensor_tensor(pages[s][:].indirect(entries(idx, h * HALF, HALF)), mixed[:], wgo_sb[:, js], ALU.mult)
             if h == HALVES - 1:
                 dma(out=out_0[cols, :], in_=pages[s][:])
 
-        quantise(0, SLICES - 1, "av7", [nc.sync, nc.gpsimd])
+        quantise(0, SLICES - 1, "mixed7", [nc.sync, nc.gpsimd])
         regroup(SLICES - 1)
         quantise(SLICES - 1, SLICES, None, [nc.sync, nc.scalar])
         for g in range(QUADS):

@@ -23,22 +23,21 @@ SLICES = N // P
 HALF = 512
 HALVES = J // HALF
 BANK = 512
-Z_COLS = 2 * P
-SHIFT_ROWS = 112
+ROWS_AT = 96
 ODD = T // 2 - 1
-Z_WORDS = PACK * Z_COLS
-TAB_AT = Z_WORDS - 16
-PAIRS_AT = Z_WORDS
-V_S_AT = PAIRS_AT + HALF
-LATE_Z_AT = [0, V_S_AT + HALF // 4, V_S_AT + HALF // 4 + Z_WORDS]
-W_AT = LATE_Z_AT[2] + Z_WORDS
-Z_AT = W_AT + 3 * N
-WGO_AT = Z_AT + 3 * Z_WORDS
+Z_GROUPS = [(0, 1), (1, 2), (2, 4)]
+W_GROUPS = [(0, 1), (1, 4)]
+TAB_AT = 0
+TAB2_AT = TAB_AT + T
+W_AT = TAB2_AT + T
+LATE_AT = W_AT + 3 * P
+LATE_W_AT = LATE_AT + J
+LATE_Z_AT = LATE_W_AT + 3 * 3 * P
+HELD = LATE_Z_AT + 3 * 3 * PACK * P
 TURN_BANKS = (0, 1, 3, 4)
 BACK_BANKS = (2, 5)
-LAST_TURN_BANKS = (5, 4, 5, 4)
-LAST_BACK_BANKS = (2, 3)
-STEPS = [(0, 0), (1, 0), (0, 1), (1, 1), (2, 0), (2, 1), (3, 0), (3, 1)]
+LAST_BACK_BANKS = (6, 7, 2, 5)
+STEPS = [(s, h) for s in range(SLICES) for h in range(HALVES)]
 
 
 def tile_list_gmu_silu_scatP_kernel(
@@ -71,9 +70,9 @@ def tile_list_gmu_silu_scatP_kernel(
         idx2 = keep.tile([P, J // 16], U16, name="idx2")
         tab_s = sbuf("tab_s", [P, T], U8)
         tab2_s = sbuf("tab2_s", [P, T], U8)
-        tab2_w = sbuf("tab2_w", [P, T], U32)
-        lowered = sbuf("lowered", [P, J], U8)
-        pages = {t: sbuf("page%d" % t, [P, T], F32) for t in (0, 2)}
+        planes = sbuf("planes", [P, 2, 2, J], U8)
+        pages = {0: sbuf("page0", [P, T], F32)}
+        zero = sbuf("zero", [P, 1], F32)
         ident = sbuf("ident", [P, P], F32)
         no_bias = sbuf("no_bias", [P, 1], F32)
 
@@ -85,20 +84,20 @@ def tile_list_gmu_silu_scatP_kernel(
             for c in range(0, T, BANK):
                 nc.gpsimd.memset(pages[t][:, c : c + BANK], 0.0)
 
-        nc.gpsimd.memset(tab2_s[:].bitcast(I32), 0)
-        nc.gpsimd.memset(zeros[:], 0.0)
-        nc.gpsimd.memset(lowered[:].bitcast(I32), 0)
-        clear_page(2)
         nc.gpsimd.memset(tab_s[:].bitcast(I32), 0)
+        nc.gpsimd.memset(tab2_s[0:ROWS_AT].bitcast(I32), 0)
         nc.gpsimd.memset(w_s[:].rearrange("p a n -> p (a n)").bitcast(I32), 0)
+        nc.gpsimd.memset(planes[:].rearrange("p a g n -> p (a g n)").bitcast(I32), 0)
         nc.gpsimd.memset(rows[:], 0.0)
+        nc.gpsimd.memset(zeros[:], 0.0)
         nc.gpsimd.affine_select(
             out=ident[:], in_=zeros[:], pattern=[[-1, P]], compare_op=ALU.not_equal, fill=1.0, base=0, channel_multiplier=1
         )
         with tc.tile_pool(name="early", bufs=1) as early:
-            zero = sbuf("zero", [P, WGO_AT + J], F32, pool=early)
-            nc.vector.memset(zero[:, 0:1], 0.0)
-            nc.scalar.activation(no_bias[:], zero[:, 0:1], ACT.Silu)
+            seed = sbuf("seed", [P, HELD], F32, pool=early)
+            nc.vector.memset(seed[:, 0:1], 0.0)
+            nc.vector.tensor_copy(zero[:], seed[:, 0:1])
+        nc.scalar.activation(no_bias[:], zero[:], ACT.Silu)
         w_pool = ctx.enter_context(tc.tile_pool(name="w_pool", bufs=1))
         nc.vector.memset(pages[0][:, 0:ODD], 0.0)
         nc.vector.memset(pages[0][:, ODD:T], 0.0)
@@ -107,46 +106,56 @@ def tile_list_gmu_silu_scatP_kernel(
             return w_pool.tile(shape, dtype, name=name, align_bytes=64, offset=4 * word)
 
         tab_w = placed("tab_w", [P, T], U32, TAB_AT)
-        w_w = [placed("w_w%d" % g, [P, 3, Z_COLS], U32, W_AT + 3 * g * Z_COLS) for g in range(2)]
-        wgo_sb = placed("wgo_sb", [P, J], F32, WGO_AT)
-        z_raw = {(0, a): placed("z_raw0_%d" % a, [P, PACK, Z_COLS], F32, Z_AT + a * Z_WORDS) for a in range(3)}
-
-
+        tab2_w = placed("tab2_w", [P, T], U32, TAB2_AT)
         z_src = [by_partition(zt[0:512, :]), by_partition(zt[512:1024, :]), by_partition(zv)]
+        z_raw, w_w = {}, {}
 
         def load_z(group):
+            s0, s1 = Z_GROUPS[group]
             for a in range(3):
+                shape = [P, PACK, (s1 - s0) * P]
+                name = "z_raw%d_%d" % (group, a)
                 if group:
-                    z_raw[group, a] = placed("z_raw1_%d" % a, [P, PACK, Z_COLS], F32, LATE_Z_AT[a])
-                dma(out=z_raw[group, a][:], in_=z_src[a][:, :, group * Z_COLS : (group + 1) * Z_COLS])
+                    raw = placed(name, shape, F32, LATE_Z_AT + (3 * (s0 - 1) + a * (s1 - s0)) * PACK * P)
+                else:
+                    raw = sbuf(name, shape, F32)
+                dma(out=raw[:], in_=z_src[a][:, :, s0 * P : s1 * P])
+                for s in range(s0, s1):
+                    z_raw[s, a] = raw[:, :, (s - s0) * P : (s - s0 + 1) * P]
 
         def load_w(group):
-            cs = slice(group * Z_COLS, (group + 1) * Z_COLS)
-            dma(out=w_w[group][:, 0:2].bitcast(I32), in_=wt_words.rearrange("a p n i -> p a (n i)").bitcast(I32)[:, :, cs])
-            dma(out=w_w[group][:, 2].bitcast(I32), in_=as_words(wv_words[0])[:, cs])
+            s0, s1 = W_GROUPS[group]
+            cs = slice(s0 * P, s1 * P)
+            words = placed("w_w%d" % group, [P, 3, (s1 - s0) * P], U32, LATE_W_AT if group else W_AT)
+            dma(out=words[:, 0:2].bitcast(I32), in_=wt_words.rearrange("a p n i -> p a (n i)").bitcast(I32)[:, :, cs])
+            dma(out=words[:, 2].bitcast(I32), in_=as_words(wv_words[0])[:, cs])
+            for s in range(s0, s1):
+                w_w[s] = words[:, :, (s - s0) * P : (s - s0 + 1) * P]
 
         dma(out=idx2[:], in_=offs2)
+        dma(out=tab2_s[ROWS_AT:P].bitcast(I32), in_=tab2_scales.bitcast(I32).rearrange("a q n -> q a n"))
         dma(out=idx[:], in_=offs)
-        dma(out=tab2_w[:].bitcast(I32), in_=as_words(tab2_words[0]))
-        for q in range(QUADS):
-            dma(out=tab2_s[32 * q : 32 * q + 8, :].bitcast(I32), in_=tab2_scales[:, 4 * q : 4 * q + 4, :].bitcast(I32))
         load_z(0)
-        for q in range(QUADS):
-            dma(out=tab_s[32 * q : 32 * q + 4, :].bitcast(I32), in_=tab_scales[0, 4 * q : 4 * q + 4, :].bitcast(I32))
+        dma(out=tab_s[ROWS_AT:P:2].bitcast(I32), in_=tab_scales[0].bitcast(I32))
+        dma(out=tab2_w[:].bitcast(I32), in_=as_words(tab2_words[0]))
+        dma(out=w_s[0:16, 0:2].bitcast(I32), in_=wt_scales.bitcast(I32).rearrange("a q n -> q a n"))
+        dma(out=w_s[0:16, 2].bitcast(I32), in_=wv_scales[0].bitcast(I32))
+        dma(out=rows[0:SLICES, :], in_=b.rearrange("(s n) -> s n", n=P))
         load_w(0)
         dma(out=tab_w[:].bitcast(I32), in_=as_words(tab_words[0]))
+        for q in range(1, QUADS):
+            dma(out=w_s[32 * q : 32 * q + 4].bitcast(I32), in_=w_s[4 * q : 4 * q + 4].bitcast(I32))
 
-        v_w, v_s, v2_w = {}, {}, {}
-        v2_s = sbuf("v2_s", [P, J], U8)
+        v_w, v2_w, pairs = {}, {}, {}
+        picked_s = sbuf("picked_s", [P, 2, J], U8)
 
-        def gather_v2_words(h, pairs):
+        def gather_pairs(h, tile):
+            pairs[h] = tile[:, 0:HALF]
+            nc.vector.tensor_copy(pairs[h], tab2_w[:].indirect(entries(idx2, h * HALF, HALF)))
+
+        def part_pairs(h):
             v2_w[h] = sbuf("v2_w%d" % h, [P, 2, 2 * HALF], U8)
-            nc.vector.tensor_copy(pairs[:], tab2_w[:].indirect(entries(idx2, h * HALF, HALF)))
-            nc.vector.tensor_copy(v2_w[h][:].bitcast(U16), pairs[:].bitcast(U16).rearrange("p (j d) -> p d j", d=2))
-
-        def gather_v_scales(h, tile):
-            v_s[h] = tile
-            nc.vector.tensor_copy(tile[:], tab_s[:].indirect(entries(idx, h * HALF, HALF)))
+            nc.vector.tensor_copy(v2_w[h][:].bitcast(U16), pairs[h].bitcast(U16).rearrange("p (j d) -> p d j", d=2))
 
         def gather_v_words(h):
             v_w[h] = sbuf("v_w%d" % h, [P, HALF], U32)
@@ -154,72 +163,64 @@ def tile_list_gmu_silu_scatP_kernel(
 
         z_w, z_s = {}, {}
 
-        def make_z(s0, s1):
-            width = (s1 - s0) * P
-            c0 = s0 % 2 * P
-            codes = sbuf("z_w%d" % s0, [P, 3, width], U32)
-            scales = sbuf("z_s%d" % s0, [P, 3, width], U8)
+        def make_z(s):
+            z_w[s] = sbuf("z_w%d" % s, [P, 3, P], U32)
+            z_s[s] = sbuf("z_s%d" % s, [P, 3, P], U8)
             for name, a0, a1 in (("zt", 0, 2), ("zv", 2, 3)):
-                rounded = sbuf("%s_bf%d" % (name, s0), [P, a1 - a0, PACK * width], BF16)
+                rounded = sbuf("%s_bf%d" % (name, s), [P, a1 - a0, PACK * P], BF16)
                 for a in range(a0, a1):
                     nc.scalar.copy(
                         rounded[:, a - a0].rearrange("p (c e i) -> p c i e", e=4, i=PACK),
-                        z_raw[s0 // 2, a][:, :, c0 : c0 + width].rearrange("p i (c e) -> p c i e", e=4),
+                        z_raw[s, a].rearrange("p i (c e) -> p c i e", e=4),
                     )
                 nc.vector.quantize_mx(
-                    codes[:, a0:a1].rearrange("p a n -> p (a n)").bitcast(FP8X4),
-                    scales[:, a0:a1].rearrange("p a n -> p (a n)"),
+                    z_w[s][:, a0:a1].rearrange("p a n -> p (a n)").bitcast(FP8X4),
+                    z_s[s][:, a0:a1].rearrange("p a n -> p (a n)"),
                     rounded[:].rearrange("p a n -> p (a n)"),
                 )
-            for s in range(s0, s1):
-                z_w[s] = codes[:, :, (s - s0) * P : (s - s0 + 1) * P]
-                z_s[s] = scales[:, :, (s - s0) * P : (s - s0 + 1) * P]
 
-        nc.vector.tensor_copy(v2_s[:], tab2_s[:].indirect(idx2[:]))
+        nc.vector.tensor_copy(picked_s[:, 0], tab2_s[:].indirect(idx2[:]))
+        nc.vector.tensor_copy(picked_s[:, 1], tab_s[:].indirect(idx[:]))
         for q in range(QUADS):
             dma(
-                out=w_s[32 * q : 32 * q + 4, 0:2].bitcast(I32),
-                in_=wt_scales[:, 4 * q : 4 * q + 4, :].bitcast(I32).rearrange("a r n -> r a n"),
+                out=planes[32 * q : 32 * q + 4].rearrange("p a g n -> p a (g n)").bitcast(I32),
+                in_=picked_s[ROWS_AT + 8 * q : ROWS_AT + 8 * q + 8].rearrange("p g n -> p (g n)").bitcast(I32),
             )
-        dma(out=lowered[0:SHIFT_ROWS, :].bitcast(I32), in_=v2_s[4 : 4 + SHIFT_ROWS, :].bitcast(I32))
-        for q in range(QUADS):
-            dma(out=w_s[32 * q : 32 * q + 4, 2].bitcast(I32), in_=wv_scales[0, 4 * q : 4 * q + 4, :].bitcast(I32))
-        dma(out=rows[0:SLICES, :], in_=b.rearrange("(s n) -> s n", n=P))
+        make_z(0)
+        gather_pairs(0, placed("pairs0", [P, HELD - LATE_AT], U32, LATE_AT))
+        part_pairs(0)
+        wgo_sb = placed("wgo_sb", [P, J], F32, LATE_AT)
         dma(out=wgo_sb[:], in_=wgo)
+        load_z(1)
         load_w(1)
-        gather_v2_words(0, sbuf("pairs0", [P, HALF], U32))
-        make_z(0, 2)
+        load_z(2)
 
         turned = bank(7, "turned")
         nc.tensor.transpose(turned[:, 0:P], rows[:], ident[:])
         half_b = sbuf("half_b", [P, SLICES], F32)
         nc.scalar.mul(half_b[:], turned[:, 0:SLICES], 0.5)
 
-        gather_v_scales(0, sbuf("v_s0", [P, HALF], U8))
         gather_v_words(0)
         gather_v_words(1)
-        load_z(1)
-        gather_v2_words(1, placed("pairs1", [P, HALF], U32, PAIRS_AT))
-        gather_v_scales(1, placed("v_s1", [P, HALF], U8, V_S_AT))
-        pages[1] = sbuf("page1", [P, T], F32, "tab_s")
+        gather_pairs(1, placed("pairs1", [P, HALF], U32, TAB_AT))
+        part_pairs(1)
+        pages[1] = placed("page1", [P, T], F32, TAB_AT)
         clear_page(1)
 
         out_s = sbuf("out_s", [P, SLICES, BANK], U8)
         grouped = {}
 
         def regroup(s):
-            last = s == SLICES - 1
             blocks = pages[s][:].rearrange("p (g k c) -> p k g c", g=QUADS, c=P)
             for half in range(2):
-                back = bank((LAST_BACK_BANKS if last else BACK_BANKS)[half], "back")
-                copy = nc.vector.tensor_copy if last and half == 1 else nc.scalar.copy
+                back = bank(BACK_BANKS[half], "back")
                 for k2 in range(2):
                     k = 2 * half + k2
-                    turned = bank((LAST_TURN_BANKS if last else TURN_BANKS)[k], "turned")
+                    turned = bank(TURN_BANKS[k], "turned")
                     for g in range(QUADS):
                         nc.tensor.transpose(turned[:, g * P : (g + 1) * P], blocks[:, k, g], ident[:])
                     rounded = sbuf("rounded%d_%d" % (s, k), [P, BANK], BF16)
-                    copy(
+                    nc.scalar.copy(
                         rounded[:].rearrange("p (u m e) -> p u m e", u=2, e=2),
                         turned[:].rearrange("p (m u e) -> p u m e", u=2, e=2),
                     )
@@ -232,34 +233,64 @@ def tile_list_gmu_silu_scatP_kernel(
                     back[:].rearrange("p (k u c) -> p k c u", k=2, u=2),
                 )
 
-        def quantise(s0, s1, after, queues):
-            out_w = sbuf("out_w%d" % s0, [P, s1 - s0, BANK], U32, after)
-            for s in range(s0, s1):
-                for half in range(2):
-                    ws = slice(half * 2 * P, (half + 1) * 2 * P)
-                    nc.vector.quantize_mx(out_w[:, s - s0, ws].bitcast(FP8X4), out_s[:, s, ws], grouped[s, half][:])
+        def store_words(out_w, s0, s1, queues):
             rows_out = as_words(out_1[0]).rearrange("(s q) (g c) -> g q s c", s=SLICES, g=QUADS)
             for g in range(QUADS):
                 queues[g % 2].dma_start(out=rows_out[g][:, s0:s1], in_=out_w[32 * g : 32 * (g + 1)].bitcast(I32))
 
+        def finish_last_page():
+            s = SLICES - 1
+            late_ident = sbuf("late_ident", [P, P], F32, "rounded%d_%d" % (s - 1, QUADS - 1))
+            nc.scalar.copy(late_ident[:], ident[:])
+            blocks = pages[s][:].rearrange("p (g k c) -> p k g c", g=QUADS, c=P)
+            out_w = placed("out_w_late", [P, 2, BANK], U32, LATE_AT)
+            quantise(out_w, s - 1, s)
+            rounded = {}
+            for k in range(QUADS):
+                turned = bank(TURN_BANKS[k], "turned")
+                for g in range(QUADS):
+                    nc.tensor.transpose(turned[:, g * P : (g + 1) * P], blocks[:, k, g], late_ident[:])
+                rounded[k] = sbuf("rounded%d_%d" % (s, k), [P, BANK], BF16)
+                nc.scalar.copy(
+                    rounded[k][:].rearrange("p (u m e) -> p u m e", u=2, e=2),
+                    turned[:].rearrange("p (m u e) -> p u m e", u=2, e=2),
+                )
+            for k in range(QUADS):
+                back = bank(LAST_BACK_BANKS[k], "back")
+                for u in range(2):
+                    nc.tensor.transpose(back[:, u * P : (u + 1) * P], rounded[k][:].bitcast(F32)[:, u * P : (u + 1) * P], ident[:])
+                block = sbuf("block%d" % k, [P, BANK], BF16)
+                nc.vector.tensor_copy(
+                    block[:].bitcast(F32).rearrange("p (c u) -> p c u", u=2),
+                    back[:, 0 : 2 * P].rearrange("p (u c) -> p c u", u=2),
+                )
+                ws = slice(k * P, (k + 1) * P)
+                nc.vector.quantize_mx(out_w[:, 1, ws].bitcast(FP8X4), out_s[:, s, ws], block[:])
+            store_words(out_w, s - 1, s + 1, [nc.sync, nc.scalar])
+
+        def quantise(out_w, s0, s1):
+            for s in range(s0, s1):
+                for half in range(2):
+                    ws = slice(half * 2 * P, (half + 1) * 2 * P)
+                    nc.vector.quantize_mx(out_w[:, s - s0, ws].bitcast(FP8X4), out_s[:, s, ws], grouped[s, half][:])
+
         for step, (s, h) in enumerate(STEPS):
             cols = slice(s * P, (s + 1) * P)
-            group_cols = slice(s % 2 * P, (s % 2 + 1) * P)
             js = slice(h * HALF, (h + 1) * HALF)
-            fp8, fp8_s = v_w[h][:].bitcast(FP8X4), v_s[h][:]
+            fp8, fp8_s = v_w[h][:].bitcast(FP8X4), planes[:, 0, 1, js]
             fp4 = [v2_w[h][:, a, :].bitcast(FP4X4) for a in range(2)]
-            fp4_s = [v2_s[:, js], lowered[:, js]]
+            fp4_s = [planes[:, a, 0, js] for a in range(2)]
             first = 3 * (step % 2)
             ht = bank(first + step // 2 % 2, "ht")
             hv = bank(first + 1 - step // 2 % 2, "hv")
             z = bank(first + 2, "z")
             for a in range(2):
                 nc.tensor.matmul_mx(
-                    ht[:], w_w[s // 2][:, a, group_cols].bitcast(FP8X4), w_s[:, a, cols], fp4[a], fp4_s[a], start=(a == 0), stop=(a == 1)
+                    ht[:], w_w[s][:, a].bitcast(FP8X4), w_s[:, a, cols], fp4[a], fp4_s[a], start=(a == 0), stop=(a == 1)
                 )
+            nc.tensor.matmul_mx(hv[:], w_w[s][:, 2].bitcast(FP8X4), w_s[:, 2, cols], fp8, fp8_s, start=True, stop=True)
             for a in range(2):
                 nc.tensor.matmul_mx(z[:], z_w[s][:, a].bitcast(FP8X4), z_s[s][:, a], fp4[a], fp4_s[a], start=(a == 0), stop=False)
-            nc.tensor.matmul_mx(hv[:], w_w[s // 2][:, 2, group_cols].bitcast(FP8X4), w_s[:, 2, cols], fp8, fp8_s, start=True, stop=True)
             nc.tensor.matmul_mx(z[:], z_w[s][:, 2].bitcast(FP8X4), z_s[s][:, 2], fp8, fp8_s, start=False, stop=True)
             av = sbuf("av%d" % step, [P, HALF], F32)
             at = sbuf("at%d" % step, [P, HALF], F32)
@@ -268,24 +299,28 @@ def tile_list_gmu_silu_scatP_kernel(
             nc.scalar.activation(av[:], hv[:], ACT.Silu, bias=no_bias[:])
             nc.scalar.activation(gate[:], z[:], ACT.Tanh, bias=half_b[:, s : s + 1], scale=0.5)
             if step == 1:
-                pages[3] = sbuf("page3", [P, T], F32, "at0")
+                pages[2] = sbuf("page2", [P, T], F32, "at0")
+                clear_page(2)
+            if step == 2:
+                pages[3] = sbuf("page3", [P, T], F32, "at1")
                 clear_page(3)
-            if step in (1, 3):
-                make_z(2 + step // 2, 3 + step // 2)
+            if step in (0, 1, 3):
+                make_z(1 + (step + 1) // 2)
             if step == len(STEPS) - 1:
                 for early_page in range(SLICES - 1):
                     regroup(early_page)
-            mixed = sbuf("mixed%d" % step, [P, HALF], F32, {2: "zv_bf2", 4: "zv_bf3"}.get(step))
-            nc.vector.tensor_tensor(av[:], av[:], at[:], ALU.subtract)
-            nc.vector.scalar_tensor_tensor(av[:], gate[:], 1.0, av[:], ALU.add, ALU.mult)
-            nc.vector.scalar_tensor_tensor(mixed[:], av[:], 0.5, at[:], ALU.mult, ALU.add)
+            mixed = sbuf("mixed%d" % step, [P, HALF], F32, {1: "zv_bf1", 2: "zv_bf2", 4: "zv_bf3"}.get(step))
+            nc.vector.tensor_tensor(mixed[:], av[:], at[:], ALU.subtract)
+            nc.vector.scalar_tensor_tensor(mixed[:], gate[:], 1.0, mixed[:], ALU.add, ALU.mult)
+            nc.vector.scalar_tensor_tensor(mixed[:], mixed[:], 0.5, at[:], ALU.mult, ALU.add)
             nc.vector.tensor_tensor(pages[s][:].indirect(entries(idx, h * HALF, HALF)), mixed[:], wgo_sb[:, js], ALU.mult)
             if h == HALVES - 1:
                 dma(out=out_0[cols, :], in_=pages[s][:])
 
-        quantise(0, SLICES - 1, "mixed7", [nc.sync, nc.gpsimd])
-        regroup(SLICES - 1)
-        quantise(SLICES - 1, SLICES, None, [nc.sync, nc.scalar])
+        early_w = sbuf("out_w_early", [P, 2, BANK], U32, "mixed7")
+        quantise(early_w, 0, 2)
+        store_words(early_w, 0, 2, [nc.sync, nc.gpsimd])
+        finish_last_page()
         for g in range(QUADS):
             queue = nc.scalar if g % 2 else nc.sync
             queue.dma_start(

@@ -34,6 +34,7 @@ LATE_AT = W_AT + 3 * P
 LATE_W_AT = LATE_AT + J
 LATE_Z_AT = LATE_W_AT + 3 * 3 * P
 HELD = LATE_Z_AT + 3 * 3 * PACK * P
+WARM_PASSES = 4
 TURN_BANKS = (0, 1, 3, 4)
 BACK_BANKS = (2, 5)
 LAST_BACK_BANKS = (6, 7, 2, 5)
@@ -227,7 +228,8 @@ def tile_list_gmu_silu_scatP_kernel(
                     for u in range(2):
                         c0 = (2 * k2 + u) * P
                         nc.tensor.transpose(back[:, c0 : c0 + P], rounded[:].bitcast(F32)[:, u * P : (u + 1) * P], ident[:])
-                grouped[s, half] = sbuf("grouped%d_%d" % (s, half), [P, 2 * BANK], BF16)
+                late = (s, half) == (SLICES - 2, 1)
+                grouped[s, half] = sbuf("grouped%d_%d" % (s, half), [P, 2 * BANK], BF16, "at7" if late else None)
                 nc.scalar.copy(
                     grouped[s, half][:].bitcast(F32).rearrange("p (k c u) -> p k c u", k=2, u=2),
                     back[:].rearrange("p (k u c) -> p k c u", k=2, u=2),
@@ -251,7 +253,8 @@ def tile_list_gmu_silu_scatP_kernel(
                 for g in range(QUADS):
                     nc.tensor.transpose(turned[:, g * P : (g + 1) * P], blocks[:, k, g], late_ident[:])
                 rounded[k] = sbuf("rounded%d_%d" % (s, k), [P, BANK], BF16)
-                nc.scalar.copy(
+                copy = nc.vector.tensor_copy if k == 2 else nc.scalar.copy
+                copy(
                     rounded[k][:].rearrange("p (u m e) -> p u m e", u=2, e=2),
                     turned[:].rearrange("p (m u e) -> p u m e", u=2, e=2),
                 )
@@ -260,7 +263,8 @@ def tile_list_gmu_silu_scatP_kernel(
                 for u in range(2):
                     nc.tensor.transpose(back[:, u * P : (u + 1) * P], rounded[k][:].bitcast(F32)[:, u * P : (u + 1) * P], ident[:])
                 block = sbuf("block%d" % k, [P, BANK], BF16)
-                nc.vector.tensor_copy(
+                copy = nc.vector.tensor_copy if k % 2 else nc.scalar.copy
+                copy(
                     block[:].bitcast(F32).rearrange("p (c u) -> p c u", u=2),
                     back[:, 0 : 2 * P].rearrange("p (u c) -> p c u", u=2),
                 )
@@ -306,17 +310,20 @@ def tile_list_gmu_silu_scatP_kernel(
                 clear_page(3)
             if step in (0, 1, 3):
                 make_z(1 + (step + 1) // 2)
-            if step == len(STEPS) - 1:
-                for early_page in range(SLICES - 1):
-                    regroup(early_page)
             mixed = sbuf("mixed%d" % step, [P, HALF], F32, {1: "zv_bf1", 2: "zv_bf2", 4: "zv_bf3"}.get(step))
             nc.vector.tensor_tensor(mixed[:], av[:], at[:], ALU.subtract)
             nc.vector.scalar_tensor_tensor(mixed[:], gate[:], 1.0, mixed[:], ALU.add, ALU.mult)
             nc.vector.scalar_tensor_tensor(mixed[:], mixed[:], 0.5, at[:], ALU.mult, ALU.add)
+            if step == len(STEPS) - 1:
+                for early_page in range(SLICES - 1):
+                    regroup(early_page)
             nc.vector.tensor_tensor(pages[s][:].indirect(entries(idx, h * HALF, HALF)), mixed[:], wgo_sb[:, js], ALU.mult)
             if h == HALVES - 1:
                 dma(out=out_0[cols, :], in_=pages[s][:])
 
+        warm = bank(BACK_BANKS[1], "warm")
+        for repeat in range(WARM_PASSES):
+            nc.tensor.matmul_mx(warm[:], w_w[s][:, 2].bitcast(FP8X4), w_s[:, 2, cols], fp8, fp8_s, start=True, stop=True)
         early_w = sbuf("out_w_early", [P, 2, BANK], U32, "mixed7")
         quantise(early_w, 0, 2)
         store_words(early_w, 0, 2, [nc.sync, nc.gpsimd])

@@ -26,6 +26,8 @@ BANK = 512
 ROWS_AT = 96
 ODD = T // 2 - 1
 Z_GROUPS = [(0, 1), (1, 2), (2, 4)]
+TILES = HALF // P
+PAIR = (2, 3)
 W_GROUPS = [(0, 1), (1, 4)]
 TAB_AT = 0
 TAB2_AT = TAB_AT + T
@@ -33,11 +35,14 @@ W_AT = TAB2_AT + T
 LATE_AT = W_AT + 3 * P
 LATE_W_AT = LATE_AT + J
 LATE_Z_AT = LATE_W_AT + 3 * 3 * P
-HELD = LATE_Z_AT + 3 * 3 * PACK * P
+WGO_ROWS_AT = LATE_Z_AT + 3 * 3 * PACK * P
+HELD = WGO_ROWS_AT + P
 WARM_PASSES = 4
-TURN_BANKS = (0, 1, 3, 4)
-BACK_BANKS = (2, 5)
-LAST_BACK_BANKS = (6, 7, 2, 5)
+TURN_BANKS = (0, 1, 2, 5)
+BACK_BANKS = (6, 7)
+LAST_BACK_BANKS = (6, 3, 4, 7)
+SHARE_BANKS = {4: (0, 1), 5: (2, 5), 6: (6, 7), 7: (3, 4)}
+PAIR_Z_BANKS = ((6, 7), (2, 5))
 STEPS = [(s, h) for s in range(SLICES) for h in range(HALVES)]
 
 
@@ -195,6 +200,9 @@ def tile_list_gmu_silu_scatP_kernel(
         load_z(1)
         load_w(1)
         load_z(2)
+        wgo_rows = placed("wgo_rows", [P, P], F32, WGO_ROWS_AT)
+        nc.gpsimd.memset(wgo_rows[:], 0.0)
+        dma(out=wgo_rows[0 : J // P, :], in_=wgo[0].rearrange("(c n) -> c n", n=P))
 
         turned = bank(7, "turned")
         nc.tensor.transpose(turned[:, 0:P], rows[:], ident[:])
@@ -211,16 +219,19 @@ def tile_list_gmu_silu_scatP_kernel(
         out_s = sbuf("out_s", [P, SLICES, BANK], U8)
         grouped = {}
 
-        def regroup(s):
+        def regroup(s, unit, turn_banks, back_banks):
             blocks = pages[s][:].rearrange("p (g k c) -> p k g c", g=QUADS, c=P)
             for half in range(2):
-                back = bank(BACK_BANKS[half], "back")
+                back = bank(back_banks[half], "back")
                 for k2 in range(2):
                     k = 2 * half + k2
-                    turned = bank(TURN_BANKS[k], "turned")
+                    turned = bank(turn_banks[k], "turned")
                     for g in range(QUADS):
-                        nc.tensor.transpose(turned[:, g * P : (g + 1) * P], blocks[:, k, g], ident[:])
-                    rounded = sbuf("rounded%d_%d" % (s, k), [P, BANK], BF16)
+                        nc.tensor.transpose(turned[:, g * P : (g + 1) * P], blocks[:, k, g], unit[:])
+                    if (s, k) == (SLICES - 2, QUADS - 1):
+                        rounded = placed("rounded%d_%d" % (s, k), [P, BANK], BF16, LATE_Z_AT)
+                    else:
+                        rounded = sbuf("rounded%d_%d" % (s, k), [P, BANK], BF16)
                     nc.scalar.copy(
                         rounded[:].rearrange("p (u m e) -> p u m e", u=2, e=2),
                         turned[:].rearrange("p (m u e) -> p u m e", u=2, e=2),
@@ -235,6 +246,22 @@ def tile_list_gmu_silu_scatP_kernel(
                     back[:].rearrange("p (k u c) -> p k c u", k=2, u=2),
                 )
 
+        dealt = {}
+
+        def read_back(s):
+            dealt[s] = placed("dealt%d" % s, [P, PACK, BANK], F32, LATE_Z_AT + s * T)
+            rows_in = out_0[s * P : (s + 1) * P, :].rearrange("(q i) (g c) -> g q i c", i=PACK, g=QUADS)
+            for g in range(QUADS):
+                dma(out=dealt[s][32 * g : 32 * (g + 1)], in_=rows_in[g])
+
+        def round_dealt(s):
+            for half in range(2):
+                grouped[s, half] = sbuf("grouped%d_%d" % (s, half), [P, 2 * BANK], BF16)
+                nc.scalar.copy(
+                    grouped[s, half][:].rearrange("p (c e i) -> p c i e", e=4, i=PACK),
+                    dealt[s][:, :, half * 2 * P : (half + 1) * 2 * P].rearrange("p i (c e) -> p c i e", e=4),
+                )
+
         def store_words(out_w, s0, s1, queues):
             rows_out = as_words(out_1[0]).rearrange("(s q) (g c) -> g q s c", s=SLICES, g=QUADS)
             for g in range(QUADS):
@@ -242,11 +269,12 @@ def tile_list_gmu_silu_scatP_kernel(
 
         def finish_last_page():
             s = SLICES - 1
-            late_ident = sbuf("late_ident", [P, P], F32, "rounded%d_%d" % (s - 1, QUADS - 1))
+            late_ident = placed("late_ident", [P, P], F32, LATE_Z_AT)
             nc.scalar.copy(late_ident[:], ident[:])
             blocks = pages[s][:].rearrange("p (g k c) -> p k g c", g=QUADS, c=P)
-            out_w = placed("out_w_late", [P, 2, BANK], U32, LATE_AT)
-            quantise(out_w, s - 1, s)
+            out_w = sbuf("out_w_late", [P, 2, BANK], U32, "av7")
+            for half in range(2):
+                quantise(out_w, 0, s - 1, half)
             rounded = {}
             for k in range(QUADS):
                 turned = bank(TURN_BANKS[k], "turned")
@@ -263,8 +291,7 @@ def tile_list_gmu_silu_scatP_kernel(
                 for u in range(2):
                     nc.tensor.transpose(back[:, u * P : (u + 1) * P], rounded[k][:].bitcast(F32)[:, u * P : (u + 1) * P], ident[:])
                 block = sbuf("block%d" % k, [P, BANK], BF16)
-                copy = nc.vector.tensor_copy if k % 2 else nc.scalar.copy
-                copy(
+                nc.scalar.copy(
                     block[:].bitcast(F32).rearrange("p (c u) -> p c u", u=2),
                     back[:, 0 : 2 * P].rearrange("p (u c) -> p c u", u=2),
                 )
@@ -272,60 +299,189 @@ def tile_list_gmu_silu_scatP_kernel(
                 nc.vector.quantize_mx(out_w[:, 1, ws].bitcast(FP8X4), out_s[:, s, ws], block[:])
             store_words(out_w, s - 1, s + 1, [nc.sync, nc.scalar])
 
-        def quantise(out_w, s0, s1):
-            for s in range(s0, s1):
-                for half in range(2):
-                    ws = slice(half * 2 * P, (half + 1) * 2 * P)
-                    nc.vector.quantize_mx(out_w[:, s - s0, ws].bitcast(FP8X4), out_s[:, s, ws], grouped[s, half][:])
+        def quantise(out_w, row, s, half):
+            ws = slice(half * 2 * P, (half + 1) * 2 * P)
+            nc.vector.quantize_mx(out_w[:, row, ws].bitcast(FP8X4), out_s[:, s, ws], grouped[s, half][:])
 
-        for step, (s, h) in enumerate(STEPS):
-            cols = slice(s * P, (s + 1) * P)
+        av, at, mixed = {}, {}, {}
+
+        def operands(h):
             js = slice(h * HALF, (h + 1) * HALF)
-            fp8, fp8_s = v_w[h][:].bitcast(FP8X4), planes[:, 0, 1, js]
-            fp4 = [v2_w[h][:, a, :].bitcast(FP4X4) for a in range(2)]
-            fp4_s = [planes[:, a, 0, js] for a in range(2)]
-            first = 3 * (step % 2)
+            fp4 = [(v2_w[h][:, a, :].bitcast(FP4X4), planes[:, a, 0, js]) for a in range(2)]
+            return fp4 + [(v_w[h][:].bitcast(FP8X4), planes[:, 0, 1, js])]
+
+        def product(out, words, scales, h, passes):
+            for a in passes:
+                nc.tensor.matmul_mx(
+                    out[:], words[:, a].bitcast(FP8X4), scales[:, a], *operands(h)[a], start=(a == passes[0]), stop=(a == passes[-1])
+                )
+
+        def hidden(step, first):
+            s, h = STEPS[step]
             ht = bank(first + step // 2 % 2, "ht")
             hv = bank(first + 1 - step // 2 % 2, "hv")
-            z = bank(first + 2, "z")
-            for a in range(2):
-                nc.tensor.matmul_mx(
-                    ht[:], w_w[s][:, a].bitcast(FP8X4), w_s[:, a, cols], fp4[a], fp4_s[a], start=(a == 0), stop=(a == 1)
-                )
-            nc.tensor.matmul_mx(hv[:], w_w[s][:, 2].bitcast(FP8X4), w_s[:, 2, cols], fp8, fp8_s, start=True, stop=True)
-            for a in range(2):
-                nc.tensor.matmul_mx(z[:], z_w[s][:, a].bitcast(FP8X4), z_s[s][:, a], fp4[a], fp4_s[a], start=(a == 0), stop=False)
-            nc.tensor.matmul_mx(z[:], z_w[s][:, 2].bitcast(FP8X4), z_s[s][:, 2], fp8, fp8_s, start=False, stop=True)
-            av = sbuf("av%d" % step, [P, HALF], F32)
-            at = sbuf("at%d" % step, [P, HALF], F32)
-            gate = sbuf("gate%d" % step, [P, HALF], F32)
-            nc.scalar.activation(at[:], ht[:], ACT.Silu, bias=no_bias[:])
-            nc.scalar.activation(av[:], hv[:], ACT.Silu, bias=no_bias[:])
-            nc.scalar.activation(gate[:], z[:], ACT.Tanh, bias=half_b[:, s : s + 1], scale=0.5)
-            if step == 1:
-                pages[2] = sbuf("page2", [P, T], F32, "at0")
-                clear_page(2)
-            if step == 2:
-                pages[3] = sbuf("page3", [P, T], F32, "at1")
-                clear_page(3)
-            if step in (0, 1, 3):
-                make_z(1 + (step + 1) // 2)
-            mixed = sbuf("mixed%d" % step, [P, HALF], F32, {1: "zv_bf1", 2: "zv_bf2", 4: "zv_bf3"}.get(step))
-            nc.vector.tensor_tensor(mixed[:], av[:], at[:], ALU.subtract)
-            nc.vector.scalar_tensor_tensor(mixed[:], gate[:], 1.0, mixed[:], ALU.add, ALU.mult)
-            nc.vector.scalar_tensor_tensor(mixed[:], mixed[:], 0.5, at[:], ALU.mult, ALU.add)
-            if step == len(STEPS) - 1:
-                for early_page in range(SLICES - 1):
-                    regroup(early_page)
-            nc.vector.tensor_tensor(pages[s][:].indirect(entries(idx, h * HALF, HALF)), mixed[:], wgo_sb[:, js], ALU.mult)
+            product(ht, w_w[s], w_s[:, :, s * P : (s + 1) * P], h, (0, 1))
+            product(hv, w_w[s], w_s[:, :, s * P : (s + 1) * P], h, (2,))
+            av[step] = sbuf("av%d" % step, [P, HALF], F32)
+            at[step] = sbuf("at%d" % step, [P, HALF], F32)
+            nc.scalar.activation(at[step][:], ht[:], ACT.Silu, bias=no_bias[:])
+            nc.scalar.activation(av[step][:], hv[:], ACT.Silu, bias=no_bias[:])
+
+        def gate(out, s, h, number):
+            z = bank(number, "z")
+            product(z, z_w[s], z_s[s], h, (0, 1, 2))
+            nc.scalar.activation(out, z[:], ACT.Tanh, bias=half_b[:, s : s + 1], scale=0.5)
+
+        def store_page(step):
+            s, h = STEPS[step]
             if h == HALVES - 1:
-                dma(out=out_0[cols, :], in_=pages[s][:])
+                dma(out=out_0[s * P : (s + 1) * P, :], in_=pages[s][:])
+                if s == 0:
+                    read_back(s)
+
+        gates = {}
+
+        def plain_gate(step):
+            s, h = STEPS[step]
+            gates[step] = sbuf("gate%d" % step, [P, HALF], F32)
+            gate(gates[step][:], s, h, 3 * (step % 2) + 2)
+
+        def subtract(step):
+            nc.vector.tensor_tensor(av[step][:], av[step][:], at[step][:], ALU.subtract)
+
+        def weigh(step):
+            nc.vector.scalar_tensor_tensor(av[step][:], gates[step][:], 1.0, av[step][:], ALU.add, ALU.mult)
+
+        def mix(step, after):
+            mixed[step] = sbuf("mixed%d" % step, [P, HALF], F32, after)
+            nc.vector.scalar_tensor_tensor(mixed[step][:], av[step][:], 0.5, at[step][:], ALU.mult, ALU.add)
+
+        def scatter_product(step):
+            s, h = STEPS[step]
+            js = slice(h * HALF, (h + 1) * HALF)
+            nc.vector.tensor_tensor(pages[s][:].indirect(entries(idx, h * HALF, HALF)), mixed[step][:], wgo_sb[:, js], ALU.mult)
+            store_page(step)
+
+        tanhs, shares = {}, {}
+
+        def pair_gates(h):
+            tanhs[h] = sbuf("tanhs%d" % h, [P, 2, HALF], F32)
+            for e, s in enumerate(PAIR):
+                gate(tanhs[h][:, e], s, h, PAIR_Z_BANKS[h][e])
+
+        def pair_shares(h):
+            shares[h] = [sbuf("share%d_%d" % (h, side), [P, TILES, 2 * P], F32) for side in range(2)]
+            for c2 in range(TILES // 2):
+                turned = bank(6 + c2, "turned")
+                for c in (2 * c2, 2 * c2 + 1):
+                    for e in range(2):
+                        c0 = (c % 2 * 2 + e) * P
+                        nc.tensor.transpose(turned[:, c0 : c0 + P], tanhs[h][:, e, c * P : (c + 1) * P], ident[:])
+                for c in (2 * c2, 2 * c2 + 1):
+                    col = slice(TILES * h + c, TILES * h + c + 1)
+                    for side in range(2):
+                        nc.scalar.activation(
+                            shares[h][side][:, c], turned[:, c % 2 * 2 * P : (c % 2 + 1) * 2 * P], ACT.Identity,
+                            bias=half_w[0][:, col], scale=half_w[side][:, col],
+                        )
+
+        weights = {}
+
+        def turn_shares(step):
+            s, h = STEPS[step]
+            weights[step] = [bank(number, "weights") for number in SHARE_BANKS[step]]
+            for side in range(2):
+                for c in range(TILES):
+                    e = s - PAIR[0]
+                    nc.tensor.transpose(weights[step][side][:, c * P : (c + 1) * P], shares[h][side][:, c, e * P : (e + 1) * P], ident[:])
+
+        def weigh_v(step):
+            nc.vector.tensor_tensor(av[step][:], weights[step][0][:], av[step][:], ALU.mult)
+
+        def weigh_t(step, tile):
+            mixed[step] = tile
+            nc.vector.tensor_tensor(mixed[step][:], weights[step][1][:], at[step][:], ALU.mult)
+
+        def scatter_sum(step):
+            s, h = STEPS[step]
+            nc.vector.tensor_tensor(pages[s][:].indirect(entries(idx, h * HALF, HALF)), av[step][:], mixed[step][:], ALU.add)
+            store_page(step)
+
+        hidden(0, 0)
+        plain_gate(0)
+        make_z(1)
+        subtract(0)
+        weigh(0)
+        mix(0, None)
+        scatter_product(0)
+        hidden(1, 3)
+        plain_gate(1)
+        pages[2] = sbuf("page2", [P, T], F32, "at0")
+        clear_page(2)
+        turned = bank(2, "turned")
+        nc.tensor.transpose(turned[:, 0:P], wgo_rows[:], ident[:])
+        half_w = [sbuf("half_w%d" % side, [P, J // P], F32) for side in range(2)]
+        for side, factor in enumerate((0.5, -0.5)):
+            nc.scalar.mul(half_w[side][:], turned[:, 0 : J // P], factor)
+        subtract(1)
+        weigh(1)
+        hidden(2, 0)
+        subtract(2)
+        make_z(2)
+        make_z(3)
+        plain_gate(2)
+        mix(1, "zt_bf3")
+        pages[3] = sbuf("page3", [P, T], F32, "at1")
+        clear_page(3)
+        weigh(2)
+        scatter_product(1)
+        hidden(3, 3)
+        plain_gate(3)
+        subtract(3)
+        mix(2, None)
+        weigh(3)
+        scatter_product(2)
+        mix(3, None)
+        scatter_product(3)
+        hidden(4, 0)
+        pair_gates(0)
+        hidden(5, 0)
+        pair_shares(0)
+        turn_shares(4)
+        pair_gates(1)
+        pair_shares(1)
+        turn_shares(5)
+        hidden(6, 3)
+        turn_shares(6)
+        hidden(7, 3)
+        turn_shares(7)
+        weigh_v(4)
+        weigh_t(4, sbuf("mixed4", [P, HALF], F32))
+        scatter_sum(4)
+        weigh_v(5)
+        weigh_t(5, sbuf("mixed5", [P, HALF], F32, "share0_0"))
+        weigh_v(6)
+        scatter_sum(5)
+        weigh_t(6, sbuf("mixed6", [P, HALF], F32, "share1_0"))
+        weigh_v(7)
+        scatter_sum(6)
+        weigh_t(7, sbuf("mixed7", [P, HALF], F32))
+        early_ident = sbuf("early_ident", [P, P], F32, "tanhs1")
+        nc.scalar.copy(early_ident[:], ident[:])
+        regroup(1, early_ident, (0, 1, 0, 1), (2, 5))
+        round_dealt(0)
+        mid_ident = sbuf("mid_ident", [P, P], F32, "share1_1")
+        nc.scalar.copy(mid_ident[:], ident[:])
+        regroup(2, mid_ident, TURN_BANKS, BACK_BANKS)
+        scatter_sum(7)
 
         warm = bank(BACK_BANKS[1], "warm")
         for repeat in range(WARM_PASSES):
-            nc.tensor.matmul_mx(warm[:], w_w[s][:, 2].bitcast(FP8X4), w_s[:, 2, cols], fp8, fp8_s, start=True, stop=True)
+            product(warm, w_w[3], w_s[:, :, 3 * P : 4 * P], 1, (2,))
         early_w = sbuf("out_w_early", [P, 2, BANK], U32, "mixed7")
-        quantise(early_w, 0, 2)
+        for s in range(2):
+            for half in range(2):
+                quantise(early_w, s, s, half)
         store_words(early_w, 0, 2, [nc.sync, nc.gpsimd])
         finish_last_page()
         for g in range(QUADS):

@@ -37,7 +37,6 @@ LATE_W_AT = LATE_AT + J
 LATE_Z_AT = LATE_W_AT + 3 * 3 * P
 WGO_ROWS_AT = LATE_Z_AT + 3 * 3 * PACK * P
 HELD = WGO_ROWS_AT + P
-WARM_PASSES = 4
 TURN_BANKS = (0, 1, 2, 5)
 BACK_BANKS = (6, 7)
 LAST_BACK_BANKS = (6, 3, 4, 7)
@@ -475,9 +474,6 @@ def tile_list_gmu_silu_scatP_kernel(
         regroup(2, mid_ident, TURN_BANKS, BACK_BANKS)
         scatter_sum(7)
 
-        warm = bank(BACK_BANKS[1], "warm")
-        for repeat in range(WARM_PASSES):
-            product(warm, w_w[3], w_s[:, :, 3 * P : 4 * P], 1, (2,))
         early_w = sbuf("out_w_early", [P, 2, BANK], U32, "mixed7")
         for s in range(2):
             for half in range(2):

@@ -27,7 +27,6 @@ ROWS_AT = 96
 ODD = T // 2 - 1
 Z_GROUPS = [(0, 1), (1, 2), (2, 4)]
 TILES = HALF // P
-PAIR = (2, 3)
 W_GROUPS = [(0, 1), (1, 4)]
 TAB_AT = 0
 TAB2_AT = TAB_AT + T
@@ -37,11 +36,13 @@ LATE_W_AT = LATE_AT + J
 LATE_Z_AT = LATE_W_AT + 3 * 3 * P
 WGO_ROWS_AT = LATE_Z_AT + 3 * 3 * PACK * P
 HELD = WGO_ROWS_AT + P
-TURN_BANKS = (0, 1, 2, 5)
-BACK_BANKS = (6, 7)
-LAST_BACK_BANKS = (6, 3, 4, 7)
-SHARE_BANKS = {4: (0, 1), 5: (2, 5), 6: (6, 7), 7: (3, 4)}
-PAIR_Z_BANKS = ((6, 7), (2, 5))
+HT_BANK, HV_BANK, Z_BANK, ROWS_BANK = 0, 1, 2, 7
+DIFF_BANKS = (3, 4)
+BASE_BANKS = (5, 6)
+TURN_BANKS = (0, 1, 2, 7)
+BACK_BANKS = (3, 5, 4, 6)
+DEALT_AT = (TAB2_AT, LATE_Z_AT, LATE_Z_AT + T)
+WEIGHED_FROM = 3
 STEPS = [(s, h) for s in range(SLICES) for h in range(HALVES)]
 
 
@@ -195,15 +196,15 @@ def tile_list_gmu_silu_scatP_kernel(
         gather_pairs(0, placed("pairs0", [P, HELD - LATE_AT], U32, LATE_AT))
         part_pairs(0)
         wgo_sb = placed("wgo_sb", [P, J], F32, LATE_AT)
-        dma(out=wgo_sb[:], in_=wgo)
         load_z(1)
+        dma(out=wgo_sb[:], in_=wgo)
         load_w(1)
         load_z(2)
         wgo_rows = placed("wgo_rows", [P, P], F32, WGO_ROWS_AT)
         nc.gpsimd.memset(wgo_rows[:], 0.0)
         dma(out=wgo_rows[0 : J // P, :], in_=wgo[0].rearrange("(c n) -> c n", n=P))
 
-        turned = bank(7, "turned")
+        turned = bank(ROWS_BANK, "turned")
         nc.tensor.transpose(turned[:, 0:P], rows[:], ident[:])
         half_b = sbuf("half_b", [P, SLICES], F32)
         nc.scalar.mul(half_b[:], turned[:, 0:SLICES], 0.5)
@@ -216,64 +217,35 @@ def tile_list_gmu_silu_scatP_kernel(
         clear_page(1)
 
         out_s = sbuf("out_s", [P, SLICES, BANK], U8)
-        grouped = {}
+        dealt, grouped = {}, {}
 
-        def regroup(s, unit, turn_banks, back_banks):
-            blocks = pages[s][:].rearrange("p (g k c) -> p k g c", g=QUADS, c=P)
-            for half in range(2):
-                back = bank(back_banks[half], "back")
-                for k2 in range(2):
-                    k = 2 * half + k2
-                    turned = bank(turn_banks[k], "turned")
-                    for g in range(QUADS):
-                        nc.tensor.transpose(turned[:, g * P : (g + 1) * P], blocks[:, k, g], unit[:])
-                    if (s, k) == (SLICES - 2, QUADS - 1):
-                        rounded = placed("rounded%d_%d" % (s, k), [P, BANK], BF16, LATE_Z_AT)
-                    else:
-                        rounded = sbuf("rounded%d_%d" % (s, k), [P, BANK], BF16)
-                    nc.scalar.copy(
-                        rounded[:].rearrange("p (u m e) -> p u m e", u=2, e=2),
-                        turned[:].rearrange("p (m u e) -> p u m e", u=2, e=2),
-                    )
-                    for u in range(2):
-                        c0 = (2 * k2 + u) * P
-                        nc.tensor.transpose(back[:, c0 : c0 + P], rounded[:].bitcast(F32)[:, u * P : (u + 1) * P], ident[:])
-                late = (s, half) == (SLICES - 2, 1)
-                grouped[s, half] = sbuf("grouped%d_%d" % (s, half), [P, 2 * BANK], BF16, "at7" if late else None)
-                nc.scalar.copy(
-                    grouped[s, half][:].bitcast(F32).rearrange("p (k c u) -> p k c u", k=2, u=2),
-                    back[:].rearrange("p (k u c) -> p k c u", k=2, u=2),
-                )
-
-        dealt = {}
-
-        def read_back(s):
-            dealt[s] = placed("dealt%d" % s, [P, PACK, BANK], F32, LATE_Z_AT + s * T)
-            rows_in = out_0[s * P : (s + 1) * P, :].rearrange("(q i) (g c) -> g q i c", i=PACK, g=QUADS)
+        def deal_page(s):
+            dealt[s] = placed("dealt%d" % s, [P, PACK, BANK], F32, DEALT_AT[s])
             for g in range(QUADS):
-                dma(out=dealt[s][32 * g : 32 * (g + 1)], in_=rows_in[g])
+                dma(out=dealt[s][32 * g : 32 * (g + 1)], in_=pages[s][:, g * BANK : (g + 1) * BANK])
 
-        def round_dealt(s):
-            for half in range(2):
-                grouped[s, half] = sbuf("grouped%d_%d" % (s, half), [P, 2 * BANK], BF16)
-                nc.scalar.copy(
-                    grouped[s, half][:].rearrange("p (c e i) -> p c i e", e=4, i=PACK),
-                    dealt[s][:, :, half * 2 * P : (half + 1) * 2 * P].rearrange("p i (c e) -> p c i e", e=4),
-                )
+        def round_dealt(s, tile):
+            grouped[s] = tile
+            nc.scalar.copy(
+                grouped[s][:].rearrange("p (c e i) -> p c i e", e=4, i=PACK),
+                dealt[s][:].rearrange("p i (c e) -> p c i e", e=4),
+            )
 
         def store_words(out_w, s0, s1, queues):
             rows_out = as_words(out_1[0]).rearrange("(s q) (g c) -> g q s c", s=SLICES, g=QUADS)
             for g in range(QUADS):
                 queues[g % 2].dma_start(out=rows_out[g][:, s0:s1], in_=out_w[32 * g : 32 * (g + 1)].bitcast(I32))
 
+        def quantise(out_w, row, s):
+            nc.vector.quantize_mx(out_w[:, row].bitcast(FP8X4), out_s[:, s], grouped[s][:])
+
         def finish_last_page():
             s = SLICES - 1
-            late_ident = placed("late_ident", [P, P], F32, LATE_Z_AT)
+            late_ident = placed("late_ident", [P, P], F32, DEALT_AT[s - 1])
             nc.scalar.copy(late_ident[:], ident[:])
             blocks = pages[s][:].rearrange("p (g k c) -> p k g c", g=QUADS, c=P)
-            out_w = sbuf("out_w_late", [P, 2, BANK], U32, "av7")
-            for half in range(2):
-                quantise(out_w, 0, s - 1, half)
+            out_w = sbuf("out_w_late", [P, 2, BANK], U32, "gate7")
+            quantise(out_w, 0, s - 1)
             rounded = {}
             for k in range(QUADS):
                 turned = bank(TURN_BANKS[k], "turned")
@@ -286,7 +258,7 @@ def tile_list_gmu_silu_scatP_kernel(
                     turned[:].rearrange("p (m u e) -> p u m e", u=2, e=2),
                 )
             for k in range(QUADS):
-                back = bank(LAST_BACK_BANKS[k], "back")
+                back = bank(BACK_BANKS[k], "back")
                 for u in range(2):
                     nc.tensor.transpose(back[:, u * P : (u + 1) * P], rounded[k][:].bitcast(F32)[:, u * P : (u + 1) * P], ident[:])
                 block = sbuf("block%d" % k, [P, BANK], BF16)
@@ -298,16 +270,17 @@ def tile_list_gmu_silu_scatP_kernel(
                 nc.vector.quantize_mx(out_w[:, 1, ws].bitcast(FP8X4), out_s[:, s, ws], block[:])
             store_words(out_w, s - 1, s + 1, [nc.sync, nc.scalar])
 
-        def quantise(out_w, row, s, half):
-            ws = slice(half * 2 * P, (half + 1) * 2 * P)
-            nc.vector.quantize_mx(out_w[:, row, ws].bitcast(FP8X4), out_s[:, s, ws], grouped[s, half][:])
-
-        av, at, mixed = {}, {}, {}
+        av, at, gates, diff, base, mixed = {}, {}, {}, {}, {}, {}
 
         def operands(h):
             js = slice(h * HALF, (h + 1) * HALF)
             fp4 = [(v2_w[h][:, a, :].bitcast(FP4X4), planes[:, a, 0, js]) for a in range(2)]
             return fp4 + [(v_w[h][:].bitcast(FP8X4), planes[:, 0, 1, js])]
+
+        def tile_operands(h, c):
+            js = slice(h * HALF + c * P, h * HALF + (c + 1) * P)
+            fp4 = [(v2_w[h][:, a, 2 * c * P : 2 * (c + 1) * P].bitcast(FP4X4), planes[:, a, 0, js]) for a in range(2)]
+            return fp4 + [(v_w[h][:, c * P : (c + 1) * P].bitcast(FP8X4), planes[:, 0, 1, js])]
 
         def product(out, words, scales, h, passes):
             for a in passes:
@@ -315,169 +288,123 @@ def tile_list_gmu_silu_scatP_kernel(
                     out[:], words[:, a].bitcast(FP8X4), scales[:, a], *operands(h)[a], start=(a == passes[0]), stop=(a == passes[-1])
                 )
 
-        def hidden(step, first):
+        def turned_product(out, s, h, passes):
+            for c in range(TILES):
+                for a in passes:
+                    nc.tensor.matmul_mx(
+                        out[:, c * P : (c + 1) * P], *tile_operands(h, c)[a],
+                        w_w[s][:, a].bitcast(FP8X4), w_s[:, a, s * P : (s + 1) * P],
+                        start=(a == passes[0]), stop=(a == passes[-1]),
+                    )
+
+        def hidden(step):
             s, h = STEPS[step]
-            ht = bank(first + step // 2 % 2, "ht")
-            hv = bank(first + 1 - step // 2 % 2, "hv")
-            product(ht, w_w[s], w_s[:, :, s * P : (s + 1) * P], h, (0, 1))
-            product(hv, w_w[s], w_s[:, :, s * P : (s + 1) * P], h, (2,))
+            ht = bank(HT_BANK, "ht")
+            hv = bank(HV_BANK, "hv")
+            if step:
+                turned_product(ht, s, h, (0, 1))
+                turned_product(hv, s, h, (2,))
+            else:
+                product(ht, w_w[s], w_s[:, :, s * P : (s + 1) * P], h, (0, 1))
+                product(hv, w_w[s], w_s[:, :, s * P : (s + 1) * P], h, (2,))
             av[step] = sbuf("av%d" % step, [P, HALF], F32)
             at[step] = sbuf("at%d" % step, [P, HALF], F32)
             nc.scalar.activation(at[step][:], ht[:], ACT.Silu, bias=no_bias[:])
             nc.scalar.activation(av[step][:], hv[:], ACT.Silu, bias=no_bias[:])
 
-        def gate(out, s, h, number):
-            z = bank(number, "z")
-            product(z, z_w[s], z_s[s], h, (0, 1, 2))
-            nc.scalar.activation(out, z[:], ACT.Tanh, bias=half_b[:, s : s + 1], scale=0.5)
-
-        def store_page(step):
-            s, h = STEPS[step]
-            if h == HALVES - 1:
-                dma(out=out_0[s * P : (s + 1) * P, :], in_=pages[s][:])
-                if s == 0:
-                    read_back(s)
-
-        gates = {}
-
-        def plain_gate(step):
+        def gate(step):
             s, h = STEPS[step]
             gates[step] = sbuf("gate%d" % step, [P, HALF], F32)
-            gate(gates[step][:], s, h, 3 * (step % 2) + 2)
+            z = bank(Z_BANK, "z")
+            product(z, z_w[s], z_s[s], h, (0, 1, 2))
+            nc.scalar.activation(gates[step][:], z[:], ACT.Tanh, bias=half_b[:, s : s + 1], scale=0.5)
 
-        def subtract(step):
-            nc.vector.tensor_tensor(av[step][:], av[step][:], at[step][:], ALU.subtract)
+        def turn_sum(out, terms):
+            for c in range(TILES):
+                cs = slice(c * P, (c + 1) * P)
+                for number, term in enumerate(terms):
+                    nc.tensor.matmul(
+                        out[:, cs], term[:, cs], ident[:], is_transpose=True, start=(number == 0), stop=(number == len(terms) - 1)
+                    )
+
+        def front(step):
+            s, h = STEPS[step]
+            hidden(step)
+            if step < WEIGHED_FROM:
+                less = sbuf("less%d" % step, [P, HALF], F32)
+                nc.scalar.mul(less[:], at[step][:], -1.0)
+                kept = at[step]
+            else:
+                for side, term in ((1, at[step]), (0, av[step])):
+                    for c in range(TILES):
+                        cs = slice(c * P, (c + 1) * P)
+                        nc.scalar.activation(term[:, cs], term[:, cs], ACT.Copy, scale=half_w[side][:, TILES * h + c : TILES * h + c + 1])
+                less = kept = at[step]
+            gate(step)
+            diff[step] = bank(DIFF_BANKS[step % 2], "diff")
+            turn_sum(diff[step], (less, av[step]))
+            base[step] = bank(BASE_BANKS[step % 2], "base")
+            turn_sum(base[step], (kept,))
 
         def weigh(step):
-            nc.vector.scalar_tensor_tensor(av[step][:], gates[step][:], 1.0, av[step][:], ALU.add, ALU.mult)
+            nc.vector.scalar_tensor_tensor(gates[step][:], gates[step][:], 1.0, diff[step][:], ALU.add, ALU.mult)
 
-        def mix(step, after):
+        def join(step, after):
             mixed[step] = sbuf("mixed%d" % step, [P, HALF], F32, after)
-            nc.vector.scalar_tensor_tensor(mixed[step][:], av[step][:], 0.5, at[step][:], ALU.mult, ALU.add)
+            if step < WEIGHED_FROM:
+                nc.vector.scalar_tensor_tensor(mixed[step][:], gates[step][:], 0.5, base[step][:], ALU.mult, ALU.add)
+            else:
+                nc.scalar.mul(mixed[step][:], base[step][:], -2.0)
 
-        def scatter_product(step):
+        def scatter(step):
             s, h = STEPS[step]
-            js = slice(h * HALF, (h + 1) * HALF)
-            nc.vector.tensor_tensor(pages[s][:].indirect(entries(idx, h * HALF, HALF)), mixed[step][:], wgo_sb[:, js], ALU.mult)
-            store_page(step)
+            window = pages[s][:].indirect(entries(idx, h * HALF, HALF))
+            if step < WEIGHED_FROM:
+                nc.vector.tensor_tensor(window, mixed[step][:], wgo_sb[:, h * HALF : (h + 1) * HALF], ALU.mult)
+            else:
+                nc.vector.tensor_tensor(window, mixed[step][:], gates[step][:], ALU.add)
+            if h == HALVES - 1:
+                if s < SLICES - 1:
+                    deal_page(s)
+                dma(out=out_0[s * P : (s + 1) * P, :], in_=pages[s][:])
 
-        tanhs, shares = {}, {}
-
-        def pair_gates(h):
-            tanhs[h] = sbuf("tanhs%d" % h, [P, 2, HALF], F32)
-            for e, s in enumerate(PAIR):
-                gate(tanhs[h][:, e], s, h, PAIR_Z_BANKS[h][e])
-
-        def pair_shares(h):
-            shares[h] = [sbuf("share%d_%d" % (h, side), [P, TILES, 2 * P], F32) for side in range(2)]
-            for c2 in range(TILES // 2):
-                turned = bank(6 + c2, "turned")
-                for c in (2 * c2, 2 * c2 + 1):
-                    for e in range(2):
-                        c0 = (c % 2 * 2 + e) * P
-                        nc.tensor.transpose(turned[:, c0 : c0 + P], tanhs[h][:, e, c * P : (c + 1) * P], ident[:])
-                for c in (2 * c2, 2 * c2 + 1):
-                    col = slice(TILES * h + c, TILES * h + c + 1)
-                    for side in range(2):
-                        nc.scalar.activation(
-                            shares[h][side][:, c], turned[:, c % 2 * 2 * P : (c % 2 + 1) * 2 * P], ACT.Identity,
-                            bias=half_w[0][:, col], scale=half_w[side][:, col],
-                        )
-
-        weights = {}
-
-        def turn_shares(step):
-            s, h = STEPS[step]
-            weights[step] = [bank(number, "weights") for number in SHARE_BANKS[step]]
-            for side in range(2):
-                for c in range(TILES):
-                    e = s - PAIR[0]
-                    nc.tensor.transpose(weights[step][side][:, c * P : (c + 1) * P], shares[h][side][:, c, e * P : (e + 1) * P], ident[:])
-
-        def weigh_v(step):
-            nc.vector.tensor_tensor(av[step][:], weights[step][0][:], av[step][:], ALU.mult)
-
-        def weigh_t(step, tile):
-            mixed[step] = tile
-            nc.vector.tensor_tensor(mixed[step][:], weights[step][1][:], at[step][:], ALU.mult)
-
-        def scatter_sum(step):
-            s, h = STEPS[step]
-            nc.vector.tensor_tensor(pages[s][:].indirect(entries(idx, h * HALF, HALF)), av[step][:], mixed[step][:], ALU.add)
-            store_page(step)
-
-        hidden(0, 0)
-        plain_gate(0)
+        hidden(0)
+        gate(0)
         make_z(1)
-        subtract(0)
+        diff[0], base[0] = av[0], at[0]
+        nc.vector.tensor_tensor(av[0][:], av[0][:], at[0][:], ALU.subtract)
         weigh(0)
-        mix(0, None)
-        scatter_product(0)
-        hidden(1, 3)
-        plain_gate(1)
+        join(0, None)
+        scatter(0)
         pages[2] = sbuf("page2", [P, T], F32, "at0")
         clear_page(2)
-        turned = bank(2, "turned")
+        front(1)
+        turned = bank(ROWS_BANK, "turned")
         nc.tensor.transpose(turned[:, 0:P], wgo_rows[:], ident[:])
         half_w = [sbuf("half_w%d" % side, [P, J // P], F32) for side in range(2)]
         for side, factor in enumerate((0.5, -0.5)):
             nc.scalar.mul(half_w[side][:], turned[:, 0 : J // P], factor)
-        subtract(1)
         weigh(1)
-        hidden(2, 0)
-        subtract(2)
-        make_z(2)
-        make_z(3)
-        plain_gate(2)
-        mix(1, "zt_bf3")
-        pages[3] = sbuf("page3", [P, T], F32, "at1")
-        clear_page(3)
-        weigh(2)
-        scatter_product(1)
-        hidden(3, 3)
-        plain_gate(3)
-        subtract(3)
-        mix(2, None)
-        weigh(3)
-        scatter_product(2)
-        mix(3, None)
-        scatter_product(3)
-        hidden(4, 0)
-        pair_gates(0)
-        hidden(5, 0)
-        pair_shares(0)
-        turn_shares(4)
-        pair_gates(1)
-        pair_shares(1)
-        turn_shares(5)
-        hidden(6, 3)
-        turn_shares(6)
-        hidden(7, 3)
-        turn_shares(7)
-        weigh_v(4)
-        weigh_t(4, sbuf("mixed4", [P, HALF], F32))
-        scatter_sum(4)
-        weigh_v(5)
-        weigh_t(5, sbuf("mixed5", [P, HALF], F32, "share0_0"))
-        weigh_v(6)
-        scatter_sum(5)
-        weigh_t(6, sbuf("mixed6", [P, HALF], F32, "share1_0"))
-        weigh_v(7)
-        scatter_sum(6)
-        weigh_t(7, sbuf("mixed7", [P, HALF], F32))
-        early_ident = sbuf("early_ident", [P, P], F32, "tanhs1")
-        nc.scalar.copy(early_ident[:], ident[:])
-        regroup(1, early_ident, (0, 1, 0, 1), (2, 5))
-        round_dealt(0)
-        mid_ident = sbuf("mid_ident", [P, P], F32, "share1_1")
-        nc.scalar.copy(mid_ident[:], ident[:])
-        regroup(2, mid_ident, TURN_BANKS, BACK_BANKS)
-        scatter_sum(7)
+        last = len(STEPS) - 1
+        for step in range(1, last):
+            front(step + 1)
+            if step < 3:
+                make_z(step + 1)
+            join(step, "av%d" % (step + 1))
+            if step == 1:
+                pages[3] = sbuf("page3", [P, T], F32, "gate1")
+                clear_page(3)
+            weigh(step + 1)
+            scatter(step)
+        join(last, None)
+        round_dealt(0, sbuf("grouped0", [P, T], BF16, "at7"))
+        round_dealt(1, placed("grouped1", [P, T], BF16, DEALT_AT[0]))
+        round_dealt(2, placed("grouped2", [P, T], BF16, DEALT_AT[1]))
+        scatter(last)
 
         early_w = sbuf("out_w_early", [P, 2, BANK], U32, "mixed7")
         for s in range(2):
-            for half in range(2):
-                quantise(early_w, s, s, half)
+            quantise(early_w, s, s)
         store_words(early_w, 0, 2, [nc.sync, nc.gpsimd])
         finish_last_page()
         for g in range(QUADS):

@@ -41,7 +41,8 @@ DIFF_BANKS = (3, 4)
 BASE_BANKS = (5, 6)
 TURN_BANKS = (0, 1, 2, 7)
 BACK_BANKS = (3, 5, 4, 6)
-DEALT_AT = (TAB2_AT, LATE_Z_AT, LATE_Z_AT + T)
+DEALT_AT = (TAB2_AT, LATE_Z_AT)
+PORT_ORDER = (0, 2, 1, 3)
 WEIGHED_FROM = 3
 STEPS = [(s, h) for s in range(SLICES) for h in range(HALVES)]
 
@@ -216,12 +217,12 @@ def tile_list_gmu_silu_scatP_kernel(
         pages[1] = placed("page1", [P, T], F32, TAB_AT)
         clear_page(1)
 
-        out_s = sbuf("out_s", [P, SLICES, BANK], U8)
+        out_s = sbuf("out_s", [P, BANK], U8)
         dealt, grouped = {}, {}
 
         def deal_page(s):
             dealt[s] = placed("dealt%d" % s, [P, PACK, BANK], F32, DEALT_AT[s])
-            for g in range(QUADS):
+            for g in PORT_ORDER:
                 dma(out=dealt[s][32 * g : 32 * (g + 1)], in_=pages[s][:, g * BANK : (g + 1) * BANK])
 
         def round_dealt(s, tile):
@@ -233,26 +234,21 @@ def tile_list_gmu_silu_scatP_kernel(
 
         def store_words(out_w, s0, s1, queues):
             rows_out = as_words(out_1[0]).rearrange("(s q) (g c) -> g q s c", s=SLICES, g=QUADS)
-            for g in range(QUADS):
-                queues[g % 2].dma_start(out=rows_out[g][:, s0:s1], in_=out_w[32 * g : 32 * (g + 1)].bitcast(I32))
+            for g in PORT_ORDER:
+                queues[g // 2].dma_start(out=rows_out[g][:, s0:s1], in_=out_w[32 * g : 32 * (g + 1)].bitcast(I32))
 
         def quantise(out_w, row, s):
-            nc.vector.quantize_mx(out_w[:, row].bitcast(FP8X4), out_s[:, s], grouped[s][:])
+            nc.vector.quantize_mx(out_w[:, row].bitcast(FP8X4), out_s[4 * s :], grouped[s][:])
 
-        def finish_last_page():
-            s = SLICES - 1
-            late_ident = placed("late_ident", [P, P], F32, DEALT_AT[s - 1])
-            nc.scalar.copy(late_ident[:], ident[:])
+        def regroup(s, unit, vector_block):
             blocks = pages[s][:].rearrange("p (g k c) -> p k g c", g=QUADS, c=P)
-            out_w = sbuf("out_w_late", [P, 2, BANK], U32, "gate7")
-            quantise(out_w, 0, s - 1)
             rounded = {}
             for k in range(QUADS):
                 turned = bank(TURN_BANKS[k], "turned")
                 for g in range(QUADS):
-                    nc.tensor.transpose(turned[:, g * P : (g + 1) * P], blocks[:, k, g], late_ident[:])
+                    nc.tensor.transpose(turned[:, g * P : (g + 1) * P], blocks[:, k, g], unit[:])
                 rounded[k] = sbuf("rounded%d_%d" % (s, k), [P, BANK], BF16)
-                copy = nc.vector.tensor_copy if k == 2 else nc.scalar.copy
+                copy = nc.vector.tensor_copy if k == vector_block else nc.scalar.copy
                 copy(
                     rounded[k][:].rearrange("p (u m e) -> p u m e", u=2, e=2),
                     turned[:].rearrange("p (m u e) -> p u m e", u=2, e=2),
@@ -261,14 +257,10 @@ def tile_list_gmu_silu_scatP_kernel(
                 back = bank(BACK_BANKS[k], "back")
                 for u in range(2):
                     nc.tensor.transpose(back[:, u * P : (u + 1) * P], rounded[k][:].bitcast(F32)[:, u * P : (u + 1) * P], ident[:])
-                block = sbuf("block%d" % k, [P, BANK], BF16)
                 nc.scalar.copy(
-                    block[:].bitcast(F32).rearrange("p (c u) -> p c u", u=2),
+                    grouped[s][:, k * BANK : (k + 1) * BANK].bitcast(F32).rearrange("p (c u) -> p c u", u=2),
                     back[:, 0 : 2 * P].rearrange("p (u c) -> p c u", u=2),
                 )
-                ws = slice(k * P, (k + 1) * P)
-                nc.vector.quantize_mx(out_w[:, 1, ws].bitcast(FP8X4), out_s[:, s, ws], block[:])
-            store_words(out_w, s - 1, s + 1, [nc.sync, nc.scalar])
 
         av, at, gates, diff, base, mixed = {}, {}, {}, {}, {}, {}
 
@@ -364,7 +356,7 @@ def tile_list_gmu_silu_scatP_kernel(
             else:
                 nc.vector.tensor_tensor(window, mixed[step][:], gates[step][:], ALU.add)
             if h == HALVES - 1:
-                if s < SLICES - 1:
+                if s < len(DEALT_AT):
                     deal_page(s)
                 dma(out=out_0[s * P : (s + 1) * P, :], in_=pages[s][:])
 
@@ -398,18 +390,27 @@ def tile_list_gmu_silu_scatP_kernel(
             scatter(step)
         join(last, None)
         round_dealt(0, sbuf("grouped0", [P, T], BF16, "at7"))
-        round_dealt(1, placed("grouped1", [P, T], BF16, DEALT_AT[0]))
-        round_dealt(2, placed("grouped2", [P, T], BF16, DEALT_AT[1]))
+        mid_ident = placed("mid_ident", [P, P], F32, DEALT_AT[0])
+        nc.scalar.copy(mid_ident[:], ident[:])
+        round_dealt(1, placed("grouped1", [P, T], BF16, DEALT_AT[0] + P))
+        grouped[2] = sbuf("grouped2", [P, T], BF16)
+        regroup(2, mid_ident, None)
         scatter(last)
 
-        early_w = sbuf("out_w_early", [P, 2, BANK], U32, "mixed7")
-        for s in range(2):
+        early_w = sbuf("out_w_early", [P, SLICES - 1, BANK], U32, "mixed7")
+        for s in range(SLICES - 1):
             quantise(early_w, s, s)
-        store_words(early_w, 0, 2, [nc.sync, nc.gpsimd])
-        finish_last_page()
-        for g in range(QUADS):
-            queue = nc.scalar if g % 2 else nc.sync
-            queue.dma_start(
-                out=out_2[0].rearrange("(s r) (g c) -> g r s c", r=4, g=QUADS)[g].bitcast(I32),
-                in_=out_s[32 * g : 32 * g + 4].bitcast(I32),
-            )
+        store_words(early_w, 0, SLICES - 1, [nc.sync, nc.gpsimd])
+        s = SLICES - 1
+        grouped[s] = sbuf("grouped3", [P, T], BF16)
+        late_ident = sbuf("late_ident", [P, P], F32, "rounded2_3")
+        nc.scalar.copy(late_ident[:], ident[:])
+        regroup(s, late_ident, 2)
+        late_w = sbuf("out_w_late", [P, 1, BANK], U32)
+        for k in range(QUADS):
+            ws = slice(k * P, (k + 1) * P)
+            nc.vector.quantize_mx(late_w[:, 0, ws].bitcast(FP8X4), out_s[4 * s :, ws], grouped[s][:, k * BANK : (k + 1) * BANK])
+        store_words(late_w, s, s + 1, [nc.sync, nc.scalar])
+        for g in PORT_ORDER:
+            queue = nc.scalar if g // 2 else nc.sync
+            queue.dma_start(out=out_2[0][:, g * BANK : (g + 1) * BANK].bitcast(I32), in_=out_s[32 * g : 32 * g + 16].bitcast(I32))

@@ -43,7 +43,7 @@ TURN_BANKS = (0, 1, 2, 7)
 BACK_BANKS = (3, 5, 4, 6)
 DEALT_AT = (TAB2_AT, LATE_Z_AT)
 PORT_ORDER = (0, 2, 1, 3)
-WEIGHED_FROM = 3
+WEIGHED_FROM = 4
 STEPS = [(s, h) for s in range(SLICES) for h in range(HALVES)]
 
 
@@ -188,7 +188,7 @@ def tile_list_gmu_silu_scatP_kernel(
 
         nc.vector.tensor_copy(picked_s[:, 0], tab2_s[:].indirect(idx2[:]))
         nc.vector.tensor_copy(picked_s[:, 1], tab_s[:].indirect(idx[:]))
-        for q in range(QUADS):
+        for q in PORT_ORDER:
             dma(
                 out=planes[32 * q : 32 * q + 4].rearrange("p a g n -> p a (g n)").bitcast(I32),
                 in_=picked_s[ROWS_AT + 8 * q : ROWS_AT + 8 * q + 8].rearrange("p g n -> p (g n)").bitcast(I32),
@@ -227,10 +227,11 @@ def tile_list_gmu_silu_scatP_kernel(
 
         def round_dealt(s, tile):
             grouped[s] = tile
-            nc.scalar.copy(
-                grouped[s][:].rearrange("p (c e i) -> p c i e", e=4, i=PACK),
-                dealt[s][:].rearrange("p i (c e) -> p c i e", e=4),
-            )
+            for k in range(QUADS):
+                nc.scalar.copy(
+                    grouped[s][:, k * BANK : (k + 1) * BANK].rearrange("p (c e i) -> p c i e", e=4, i=PACK),
+                    dealt[s][:, :, k * P : (k + 1) * P].rearrange("p i (c e) -> p c i e", e=4),
+                )
 
         def store_words(out_w, s0, s1, queues):
             rows_out = as_words(out_1[0]).rearrange("(s q) (g c) -> g q s c", s=SLICES, g=QUADS)
@@ -392,9 +393,9 @@ def tile_list_gmu_silu_scatP_kernel(
         round_dealt(0, sbuf("grouped0", [P, T], BF16, "at7"))
         mid_ident = placed("mid_ident", [P, P], F32, DEALT_AT[0])
         nc.scalar.copy(mid_ident[:], ident[:])
-        round_dealt(1, placed("grouped1", [P, T], BF16, DEALT_AT[0] + P))
         grouped[2] = sbuf("grouped2", [P, T], BF16)
         regroup(2, mid_ident, None)
+        round_dealt(1, placed("grouped1", [P, T], BF16, DEALT_AT[0] + P))
         scatter(last)
 
         early_w = sbuf("out_w_early", [P, SLICES - 1, BANK], U32, "mixed7")

@@ -40,7 +40,8 @@ HT_BANK, HV_BANK, Z_BANK, ROWS_BANK = 0, 1, 2, 7
 DIFF_BANKS = (3, 4)
 BASE_BANKS = (5, 6)
 TURN_BANKS = (0, 1, 2, 7)
-BACK_BANKS = (3, 5, 4, 6)
+BACK_BANKS = (3, 5, 6, 3)
+LAST_BACK_BANKS = (3, 5, 6, 4)
 DEALT_AT = (TAB2_AT, LATE_Z_AT)
 PORT_ORDER = (0, 2, 1, 3)
 WEIGHED_FROM = 4
@@ -241,21 +242,24 @@ def tile_list_gmu_silu_scatP_kernel(
         def quantise(out_w, row, s):
             nc.vector.quantize_mx(out_w[:, row].bitcast(FP8X4), out_s[4 * s :], grouped[s][:])
 
-        def regroup(s, unit, vector_block):
+        def regroup(s, unit, back_banks, vector_blocks):
             blocks = pages[s][:].rearrange("p (g k c) -> p k g c", g=QUADS, c=P)
             rounded = {}
             for k in range(QUADS):
                 turned = bank(TURN_BANKS[k], "turned")
                 for g in range(QUADS):
                     nc.tensor.transpose(turned[:, g * P : (g + 1) * P], blocks[:, k, g], unit[:])
-                rounded[k] = sbuf("rounded%d_%d" % (s, k), [P, BANK], BF16)
-                copy = nc.vector.tensor_copy if k == vector_block else nc.scalar.copy
+                if s == len(DEALT_AT):
+                    rounded[k] = placed("rounded%d_%d" % (s, k), [P, BANK], BF16, DEALT_AT[-1] + k * BANK)
+                else:
+                    rounded[k] = sbuf("rounded%d_%d" % (s, k), [P, BANK], BF16)
+                copy = nc.vector.tensor_copy if k in vector_blocks else nc.scalar.copy
                 copy(
                     rounded[k][:].rearrange("p (u m e) -> p u m e", u=2, e=2),
                     turned[:].rearrange("p (m u e) -> p u m e", u=2, e=2),
                 )
             for k in range(QUADS):
-                back = bank(BACK_BANKS[k], "back")
+                back = bank(back_banks[k], "back")
                 for u in range(2):
                     nc.tensor.transpose(back[:, u * P : (u + 1) * P], rounded[k][:].bitcast(F32)[:, u * P : (u + 1) * P], ident[:])
                 nc.scalar.copy(
@@ -301,7 +305,10 @@ def tile_list_gmu_silu_scatP_kernel(
                 product(ht, w_w[s], w_s[:, :, s * P : (s + 1) * P], h, (0, 1))
                 product(hv, w_w[s], w_s[:, :, s * P : (s + 1) * P], h, (2,))
             av[step] = sbuf("av%d" % step, [P, HALF], F32)
-            at[step] = sbuf("at%d" % step, [P, HALF], F32)
+            if step + 1 < len(STEPS):
+                at[step] = sbuf("at%d" % step, [P, HALF], F32)
+            else:
+                at[step] = placed("at%d" % step, [P, HALF], F32, LATE_AT)
             nc.scalar.activation(at[step][:], ht[:], ACT.Silu, bias=no_bias[:])
             nc.scalar.activation(av[step][:], hv[:], ACT.Silu, bias=no_bias[:])
 
@@ -339,8 +346,10 @@ def tile_list_gmu_silu_scatP_kernel(
             base[step] = bank(BASE_BANKS[step % 2], "base")
             turn_sum(base[step], (kept,))
 
-        def weigh(step):
-            nc.vector.scalar_tensor_tensor(gates[step][:], gates[step][:], 1.0, diff[step][:], ALU.add, ALU.mult)
+        def weigh(step, tile=None):
+            tanh = gates[step]
+            gates[step] = tile or tanh
+            nc.vector.scalar_tensor_tensor(gates[step][:], tanh[:], 1.0, diff[step][:], ALU.add, ALU.mult)
 
         def join(step, after):
             mixed[step] = sbuf("mixed%d" % step, [P, HALF], F32, after)
@@ -387,31 +396,36 @@ def tile_list_gmu_silu_scatP_kernel(
             if step == 1:
                 pages[3] = sbuf("page3", [P, T], F32, "gate1")
                 clear_page(3)
-            weigh(step + 1)
+            if step + 1 < last:
+                weigh(step + 1)
+            else:
+                quantise(early_w, 0, 0)
             scatter(step)
+            if step + 2 == last:
+                round_dealt(0, sbuf("grouped0", [P, T], BF16, "at6"))
+                early_w = sbuf("out_w_early", [P, 2, BANK], U32)
         join(last, None)
-        round_dealt(0, sbuf("grouped0", [P, T], BF16, "at7"))
-        mid_ident = placed("mid_ident", [P, P], F32, DEALT_AT[0])
+        mid_ident = placed("mid_ident", [P, P], F32, LATE_AT)
         nc.scalar.copy(mid_ident[:], ident[:])
+        round_dealt(1, placed("grouped1", [P, T], BF16, LATE_AT + P))
         grouped[2] = sbuf("grouped2", [P, T], BF16)
-        regroup(2, mid_ident, None)
-        round_dealt(1, placed("grouped1", [P, T], BF16, DEALT_AT[0] + P))
+        regroup(2, mid_ident, BACK_BANKS, ())
+        quantise(early_w, 1, 1)
+        store_words(early_w, 0, 2, [nc.sync, nc.sync])
+        weigh(last, placed("weighed7", [P, HALF], F32, LATE_AT + P))
         scatter(last)
 
-        early_w = sbuf("out_w_early", [P, SLICES - 1, BANK], U32, "mixed7")
-        for s in range(SLICES - 1):
-            quantise(early_w, s, s)
-        store_words(early_w, 0, SLICES - 1, [nc.sync, nc.gpsimd])
+        late_w = sbuf("out_w_late", [P, 2, BANK], U32, "mixed7")
+        quantise(late_w, 0, 2)
         s = SLICES - 1
         grouped[s] = sbuf("grouped3", [P, T], BF16)
-        late_ident = sbuf("late_ident", [P, P], F32, "rounded2_3")
+        late_ident = placed("late_ident", [P, P], F32, DEALT_AT[-1] + (QUADS - 1) * BANK)
         nc.scalar.copy(late_ident[:], ident[:])
-        regroup(s, late_ident, 2)
-        late_w = sbuf("out_w_late", [P, 1, BANK], U32)
+        regroup(s, late_ident, LAST_BACK_BANKS, (1, 3))
         for k in range(QUADS):
             ws = slice(k * P, (k + 1) * P)
-            nc.vector.quantize_mx(late_w[:, 0, ws].bitcast(FP8X4), out_s[4 * s :, ws], grouped[s][:, k * BANK : (k + 1) * BANK])
-        store_words(late_w, s, s + 1, [nc.sync, nc.scalar])
+            nc.vector.quantize_mx(late_w[:, 1, ws].bitcast(FP8X4), out_s[4 * s :, ws], grouped[s][:, k * BANK : (k + 1) * BANK])
+        store_words(late_w, s - 1, s + 1, [nc.sync, nc.scalar])
         for g in PORT_ORDER:
             queue = nc.scalar if g // 2 else nc.sync
             queue.dma_start(out=out_2[0][:, g * BANK : (g + 1) * BANK].bitcast(I32), in_=out_s[32 * g : 32 * g + 16].bitcast(I32))

@@ -44,7 +44,7 @@ BACK_BANKS = (3, 5, 6, 3)
 LAST_BACK_BANKS = (3, 5, 6, 4)
 DEALT_AT = (TAB2_AT, LATE_Z_AT)
 PORT_ORDER = (0, 2, 1, 3)
-WEIGHED_FROM = 4
+WEIGHED_FROM = 3
 STEPS = [(s, h) for s in range(SLICES) for h in range(HALVES)]
 
 
@@ -215,8 +215,6 @@ def tile_list_gmu_silu_scatP_kernel(
         gather_v_words(1)
         gather_pairs(1, placed("pairs1", [P, HALF], U32, TAB_AT))
         part_pairs(1)
-        pages[1] = placed("page1", [P, T], F32, TAB_AT)
-        clear_page(1)
 
         out_s = sbuf("out_s", [P, BANK], U8)
         dealt, grouped = {}, {}
@@ -378,8 +376,6 @@ def tile_list_gmu_silu_scatP_kernel(
         weigh(0)
         join(0, None)
         scatter(0)
-        pages[2] = sbuf("page2", [P, T], F32, "at0")
-        clear_page(2)
         front(1)
         turned = bank(ROWS_BANK, "turned")
         nc.tensor.transpose(turned[:, 0:P], wgo_rows[:], ident[:])
@@ -393,10 +389,11 @@ def tile_list_gmu_silu_scatP_kernel(
             if step < 3:
                 make_z(step + 1)
             join(step, "av%d" % (step + 1))
-            if step == 1:
-                pages[3] = sbuf("page3", [P, T], F32, "gate1")
-                clear_page(3)
-            if step + 1 < last:
+            if step < SLICES:
+                weigh(step + 1, sbuf("weighed%d" % (step + 1), [P, HALF], F32))
+                pages[step] = sbuf("page%d" % step, [P, T], F32, "gate%d" % (step + 1))
+                clear_page(step)
+            elif step + 1 < last:
                 weigh(step + 1)
             else:
                 quantise(early_w, 0, 0)

@@ -45,6 +45,7 @@ LAST_BACK_BANKS = (3, 5, 6, 4)
 DEALT_AT = (TAB2_AT, LATE_Z_AT)
 PORT_ORDER = (0, 2, 1, 3)
 WEIGHED_FROM = 3
+WARM_PASSES = 4
 STEPS = [(s, h) for s in range(SLICES) for h in range(HALVES)]
 
 
@@ -410,6 +411,9 @@ def tile_list_gmu_silu_scatP_kernel(
         quantise(early_w, 1, 1)
         store_words(early_w, 0, 2, [nc.sync, nc.sync])
         weigh(last, placed("weighed7", [P, HALF], F32, LATE_AT + P))
+        warm = bank(DIFF_BANKS[last % 2], "warm")
+        for repeat in range(WARM_PASSES):
+            product(warm, z_w[SLICES - 1], z_s[SLICES - 1], HALVES - 1, (2,))
         scatter(last)
 
         late_w = sbuf("out_w_late", [P, 2, BANK], U32, "mixed7")

@@ -46,6 +46,7 @@ DEALT_AT = (TAB2_AT, LATE_Z_AT)
 PORT_ORDER = (0, 2, 1, 3)
 WEIGHED_FROM = 3
 WARM_PASSES = 4
+HELD_FROM = 3
 STEPS = [(s, h) for s in range(SLICES) for h in range(HALVES)]
 
 
@@ -377,6 +378,8 @@ def tile_list_gmu_silu_scatP_kernel(
         weigh(0)
         join(0, None)
         scatter(0)
+        pages[1] = sbuf("page1", [P, T], F32, "at0")
+        clear_page(1)
         front(1)
         turned = bank(ROWS_BANK, "turned")
         nc.tensor.transpose(turned[:, 0:P], wgo_rows[:], ident[:])
@@ -389,8 +392,8 @@ def tile_list_gmu_silu_scatP_kernel(
             front(step + 1)
             if step < 3:
                 make_z(step + 1)
-            join(step, "av%d" % (step + 1))
-            if step < SLICES:
+            join(step, "av%d" % (step + 1) if HELD_FROM <= step < last - 1 else None)
+            if step in (2, 3):
                 weigh(step + 1, sbuf("weighed%d" % (step + 1), [P, HALF], F32))
                 pages[step] = sbuf("page%d" % step, [P, T], F32, "gate%d" % (step + 1))
                 clear_page(step)

@@ -242,7 +242,7 @@ def tile_list_gmu_silu_scatP_kernel(
         def quantise(out_w, row, s):
             nc.vector.quantize_mx(out_w[:, row].bitcast(FP8X4), out_s[4 * s :], grouped[s][:])
 
-        def regroup(s, unit, back_banks, vector_blocks):
+        def regroup(s, unit, back_banks, vector_blocks, vector_backs):
             blocks = pages[s][:].rearrange("p (g k c) -> p k g c", g=QUADS, c=P)
             rounded = {}
             for k in range(QUADS):
@@ -262,7 +262,8 @@ def tile_list_gmu_silu_scatP_kernel(
                 back = bank(back_banks[k], "back")
                 for u in range(2):
                     nc.tensor.transpose(back[:, u * P : (u + 1) * P], rounded[k][:].bitcast(F32)[:, u * P : (u + 1) * P], ident[:])
-                nc.scalar.copy(
+                copy = nc.vector.tensor_copy if k in vector_backs else nc.scalar.copy
+                copy(
                     grouped[s][:, k * BANK : (k + 1) * BANK].bitcast(F32).rearrange("p (c u) -> p c u", u=2),
                     back[:, 0 : 2 * P].rearrange("p (u c) -> p c u", u=2),
                 )
@@ -410,7 +411,7 @@ def tile_list_gmu_silu_scatP_kernel(
         nc.scalar.copy(mid_ident[:], ident[:])
         round_dealt(1, placed("grouped1", [P, T], BF16, LATE_AT + P))
         grouped[2] = sbuf("grouped2", [P, T], BF16)
-        regroup(2, mid_ident, BACK_BANKS, ())
+        regroup(2, mid_ident, BACK_BANKS, (), (2, 3))
         quantise(early_w, 1, 1)
         store_words(early_w, 0, 2, [nc.sync, nc.sync])
         weigh(last, placed("weighed7", [P, HALF], F32, LATE_AT + P))
@@ -423,9 +424,9 @@ def tile_list_gmu_silu_scatP_kernel(
         quantise(late_w, 0, 2)
         s = SLICES - 1
         grouped[s] = sbuf("grouped3", [P, T], BF16)
-        late_ident = placed("late_ident", [P, P], F32, DEALT_AT[-1] + (QUADS - 1) * BANK)
+        late_ident = placed("late_ident", [P, P], F32, LATE_AT)
         nc.scalar.copy(late_ident[:], ident[:])
-        regroup(s, late_ident, LAST_BACK_BANKS, (1, 3))
+        regroup(s, late_ident, LAST_BACK_BANKS, (1, 3), ())
         for k in range(QUADS):
             ws = slice(k * P, (k + 1) * P)
             nc.vector.quantize_mx(late_w[:, 1, ws].bitcast(FP8X4), out_s[4 * s :, ws], grouped[s][:, k * BANK : (k + 1) * BANK])

from contextlib import ExitStack

import concourse.mybir as mybir

K, L, N, T, J = 512, 1024, 512, 2048, 1024
FLOPS = 2 * 2 * (K + L) * N * J

F32 = mybir.dt.float32
BF16 = mybir.dt.bfloat16
I32 = mybir.dt.int32
U32 = mybir.dt.uint32
U16 = mybir.dt.uint16
U8 = mybir.dt.uint8
FP8X4 = mybir.dt.float8_e4m3fn_x4
FP4X4 = mybir.dt.float4_e2m1fn_x4
ACT = mybir.ActivationFunctionType
ALU = mybir.AluOpType

P = 128
PACK = 4
QUADS = 4
SLICES = N // P
HALF = 512
HALVES = J // HALF
BANK = 512
ROWS_AT = 96
ODD = T // 2 - 1
Z_GROUPS = [(0, 1), (1, 2), (2, 4)]
TILES = HALF // P
W_GROUPS = [(0, 1), (1, 4)]
TAB_AT = 0
TAB2_AT = TAB_AT + T
W_AT = TAB2_AT + T
LATE_AT = W_AT + 3 * P
LATE_W_AT = LATE_AT + J
LATE_Z_AT = LATE_W_AT + 3 * 3 * P
WGO_ROWS_AT = LATE_Z_AT + 3 * 3 * PACK * P
HELD = WGO_ROWS_AT + P
HT_BANK, HV_BANK, Z_BANK, ROWS_BANK = 0, 1, 2, 7
DIFF_BANKS = (3, 4)
BASE_BANKS = (5, 6)
TURN_BANKS = (0, 1, 2, 7)
BACK_BANKS = (3, 5, 6, 3)
LAST_BACK_BANKS = (3, 5, 6, 4)
DEALT_AT = (TAB2_AT, LATE_Z_AT)
PORT_ORDER = (0, 2, 1, 3)
WEIGHED_FROM = 3
WARM_PASSES = 4
HELD_FROM = 3
STEPS = [(s, h) for s in range(SLICES) for h in range(HALVES)]


def tile_list_gmu_silu_scatP_kernel(
    tc, tab_words, tab_scales, tab2_words, tab2_scales, zv, zt, b, wv_words, wv_scales, wt_words, wt_scales,
    wgo, offs, offs2, out_0, out_1, out_2,
):
    nc = tc.nc
    with ExitStack() as ctx:
        keep = ctx.enter_context(tc.tile_pool(name="keep", bufs=1))
        psum = ctx.enter_context(tc.psum_pool(name="psum", bufs=1))

        def sbuf(name, shape, dtype, after=None, pool=keep):
            return pool.tile(shape, dtype, name=name, tag=after or name, align_bytes=64)

        def bank(number, name):
            return psum.tile([P, BANK], F32, name=name, tag="bank%d" % number)

        def as_words(ap):
            return ap.rearrange("p n i -> p (n i)").bitcast(I32)

        def by_partition(ap):
            return ap.rearrange("(p i) n -> p i n", i=PACK)

        def entries(list_tile, j0, count):
            return list_tile[:, j0 // 16 : (j0 + count) // 16]

        dma = nc.sync.dma_start

        idx = keep.tile([P, J // 16], U16, name="idx")
        idx2 = keep.tile([P, J // 16], U16, name="idx2")
        tab_s = sbuf("tab_s", [P, T], U8)
        tab2_s = sbuf("tab2_s", [P, T], U8)
        planes = sbuf("planes", [P, 2, 2, J], U8)
        pages = {0: sbuf("page0", [P, T], F32)}
        zero = sbuf("zero", [P, 1], F32)
        ident = sbuf("ident", [P, P], F32)
        no_bias = sbuf("no_bias", [P, 1], F32)

        zeros = sbuf("zeros", [P, P], F32)
        w_s = sbuf("w_s", [P, 3, N], U8)
        rows = sbuf("rows", [P, P], F32)

        def clear_page(t):
            for c in range(0, T, BANK):
                nc.gpsimd.memset(pages[t][:, c : c + BANK], 0.0)

        nc.gpsimd.memset(tab_s[:].bitcast(I32), 0)
        nc.gpsimd.memset(tab2_s[0:ROWS_AT].bitcast(I32), 0)
        nc.gpsimd.memset(w_s[:].rearrange("p a n -> p (a n)").bitcast(I32), 0)
        nc.gpsimd.memset(planes[:].rearrange("p a g n -> p (a g n)").bitcast(I32), 0)
        nc.gpsimd.memset(rows[:], 0.0)
        nc.gpsimd.memset(zeros[:], 0.0)
        nc.gpsimd.affine_select(
            out=ident[:], in_=zeros[:], pattern=[[-1, P]], compare_op=ALU.not_equal, fill=1.0, base=0, channel_multiplier=1
        )
        with tc.tile_pool(name="early", bufs=1) as early:
            seed = sbuf("seed", [P, HELD], F32, pool=early)
            nc.vector.memset(seed[:, 0:1], 0.0)
            nc.vector.tensor_copy(zero[:], seed[:, 0:1])
        nc.scalar.activation(no_bias[:], zero[:], ACT.Silu)
        w_pool = ctx.enter_context(tc.tile_pool(name="w_pool", bufs=1))
        nc.vector.memset(pages[0][:, 0:ODD], 0.0)
        nc.vector.memset(pages[0][:, ODD:T], 0.0)

        def placed(name, shape, dtype, word):
            return w_pool.tile(shape, dtype, name=name, align_bytes=64, offset=4 * word)

        tab_w = placed("tab_w", [P, T], U32, TAB_AT)
        tab2_w = placed("tab2_w", [P, T], U32, TAB2_AT)
        z_src = [by_partition(zt[0:512, :]), by_partition(zt[512:1024, :]), by_partition(zv)]
        z_raw, w_w = {}, {}

        def load_z(group):
            s0, s1 = Z_GROUPS[group]
            for a in range(3):
                shape = [P, PACK, (s1 - s0) * P]
                name = "z_raw%d_%d" % (group, a)
                if group:
                    raw = placed(name, shape, F32, LATE_Z_AT + (3 * (s0 - 1) + a * (s1 - s0)) * PACK * P)
                else:
                    raw = sbuf(name, shape, F32)
                dma(out=raw[:], in_=z_src[a][:, :, s0 * P : s1 * P])
                for s in range(s0, s1):
                    z_raw[s, a] = raw[:, :, (s - s0) * P : (s - s0 + 1) * P]

        def load_w(group):
            s0, s1 = W_GROUPS[group]
            cs = slice(s0 * P, s1 * P)
            words = placed("w_w%d" % group, [P, 3, (s1 - s0) * P], U32, LATE_W_AT if group else W_AT)
            dma(out=words[:, 0:2].bitcast(I32), in_=wt_words.rearrange("a p n i -> p a (n i)").bitcast(I32)[:, :, cs])
            dma(out=words[:, 2].bitcast(I32), in_=as_words(wv_words[0])[:, cs])
            for s in range(s0, s1):
                w_w[s] = words[:, :, (s - s0) * P : (s - s0 + 1) * P]

        dma(out=idx2[:], in_=offs2)
        dma(out=tab2_s[ROWS_AT:P].bitcast(I32), in_=tab2_scales.bitcast(I32).rearrange("a q n -> q a n"))
        dma(out=idx[:], in_=offs)
        load_z(0)
        dma(out=tab_s[ROWS_AT:P:2].bitcast(I32), in_=tab_scales[0].bitcast(I32))
        dma(out=tab2_w[:].bitcast(I32), in_=as_words(tab2_words[0]))
        dma(out=w_s[0:16, 0:2].bitcast(I32), in_=wt_scales.bitcast(I32).rearrange("a q n -> q a n"))
        dma(out=w_s[0:16, 2].bitcast(I32), in_=wv_scales[0].bitcast(I32))
        dma(out=rows[0:SLICES, :], in_=b.rearrange("(s n) -> s n", n=P))
        load_w(0)
        dma(out=tab_w[:].bitcast(I32), in_=as_words(tab_words[0]))
        for q in range(1, QUADS):
            dma(out=w_s[32 * q : 32 * q + 4].bitcast(I32), in_=w_s[4 * q : 4 * q + 4].bitcast(I32))

        v_w, v2_w, pairs = {}, {}, {}
        picked_s = sbuf("picked_s", [P, 2, J], U8)

        def gather_pairs(h, tile):
            pairs[h] = tile[:, 0:HALF]
            nc.vector.tensor_copy(pairs[h], tab2_w[:].indirect(entries(idx2, h * HALF, HALF)))

        def part_pairs(h):
            v2_w[h] = sbuf("v2_w%d" % h, [P, 2, 2 * HALF], U8)
            nc.vector.tensor_copy(v2_w[h][:].bitcast(U16), pairs[h].bitcast(U16).rearrange("p (j d) -> p d j", d=2))

        def gather_v_words(h):
            v_w[h] = sbuf("v_w%d" % h, [P, HALF], U32)
            nc.vector.tensor_copy(v_w[h][:], tab_w[:].indirect(entries(idx, h * HALF, HALF)))

        z_w, z_s = {}, {}

        def make_z(s):
            z_w[s] = sbuf("z_w%d" % s, [P, 3, P], U32)
            z_s[s] = sbuf("z_s%d" % s, [P, 3, P], U8)
            for name, a0, a1 in (("zt", 0, 2), ("zv", 2, 3)):
                rounded = sbuf("%s_bf%d" % (name, s), [P, a1 - a0, PACK * P], BF16)
                for a in range(a0, a1):
                    nc.scalar.copy(
                        rounded[:, a - a0].rearrange("p (c e i) -> p c i e", e=4, i=PACK),
                        z_raw[s, a].rearrange("p i (c e) -> p c i e", e=4),
                    )
                nc.vector.quantize_mx(
                    z_w[s][:, a0:a1].rearrange("p a n -> p (a n)").bitcast(FP8X4),
                    z_s[s][:, a0:a1].rearrange("p a n -> p (a n)"),
                    rounded[:].rearrange("p a n -> p (a n)"),
                )

        nc.vector.tensor_copy(picked_s[:, 0], tab2_s[:].indirect(idx2[:]))
        nc.vector.tensor_copy(picked_s[:, 1], tab_s[:].indirect(idx[:]))
        for q in PORT_ORDER:
            dma(
                out=planes[32 * q : 32 * q + 4].rearrange("p a g n -> p a (g n)").bitcast(I32),
                in_=picked_s[ROWS_AT + 8 * q : ROWS_AT + 8 * q + 8].rearrange("p g n -> p (g n)").bitcast(I32),
            )
        make_z(0)
        gather_pairs(0, placed("pairs0", [P, HELD - LATE_AT], U32, LATE_AT))
        part_pairs(0)
        wgo_sb = placed("wgo_sb", [P, J], F32, LATE_AT)
        load_z(1)
        dma(out=wgo_sb[:], in_=wgo)
        load_w(1)
        load_z(2)
        wgo_rows = placed("wgo_rows", [P, P], F32, WGO_ROWS_AT)
        nc.gpsimd.memset(wgo_rows[:], 0.0)
        dma(out=wgo_rows[0 : J // P, :], in_=wgo[0].rearrange("(c n) -> c n", n=P))

        turned = bank(ROWS_BANK, "turned")
        nc.tensor.transpose(turned[:, 0:P], rows[:], ident[:])
        half_b = sbuf("half_b", [P, SLICES], F32)
        nc.scalar.mul(half_b[:], turned[:, 0:SLICES], 0.5)

        gather_v_words(0)
        gather_v_words(1)
        gather_pairs(1, placed("pairs1", [P, HALF], U32, TAB_AT))
        part_pairs(1)

        out_s = sbuf("out_s", [P, BANK], U8)
        dealt, grouped = {}, {}

        def deal_page(s):
            dealt[s] = placed("dealt%d" % s, [P, PACK, BANK], F32, DEALT_AT[s])
            for g in PORT_ORDER:
                dma(out=dealt[s][32 * g : 32 * (g + 1)], in_=pages[s][:, g * BANK : (g + 1) * BANK])

        def round_dealt(s, tile):
            grouped[s] = tile
            for k in range(QUADS):
                nc.scalar.copy(
                    grouped[s][:, k * BANK : (k + 1) * BANK].rearrange("p (c e i) -> p c i e", e=4, i=PACK),
                    dealt[s][:, :, k * P : (k + 1) * P].rearrange("p i (c e) -> p c i e", e=4),
                )

        def store_words(out_w, s0, s1, queues):
            rows_out = as_words(out_1[0]).rearrange("(s q) (g c) -> g q s c", s=SLICES, g=QUADS)
            for g in PORT_ORDER:
                queues[g // 2].dma_start(out=rows_out[g][:, s0:s1], in_=out_w[32 * g : 32 * (g + 1)].bitcast(I32))

        def quantise(out_w, row, s):
            nc.vector.quantize_mx(out_w[:, row].bitcast(FP8X4), out_s[4 * s :], grouped[s][:])

        def regroup(s, unit, back_banks, vector_blocks, vector_backs):
            blocks = pages[s][:].rearrange("p (g k c) -> p k g c", g=QUADS, c=P)
            rounded = {}
            for k in range(QUADS):
                turned = bank(TURN_BANKS[k], "turned")
                for g in range(QUADS):
                    nc.tensor.transpose(turned[:, g * P : (g + 1) * P], blocks[:, k, g], unit[:])
                if s == len(DEALT_AT):
                    rounded[k] = placed("rounded%d_%d" % (s, k), [P, BANK], BF16, DEALT_AT[-1] + k * BANK)
                else:
                    rounded[k] = sbuf("rounded%d_%d" % (s, k), [P, BANK], BF16)
                copy = nc.vector.tensor_copy if k in vector_blocks else nc.scalar.copy
                copy(
                    rounded[k][:].rearrange("p (u m e) -> p u m e", u=2, e=2),
                    turned[:].rearrange("p (m u e) -> p u m e", u=2, e=2),
                )
            for k in range(QUADS):
                back = bank(back_banks[k], "back")
                for u in range(2):
                    nc.tensor.transpose(back[:, u * P : (u + 1) * P], rounded[k][:].bitcast(F32)[:, u * P : (u + 1) * P], ident[:])
                copy = nc.vector.tensor_copy if k in vector_backs else nc.scalar.copy
                copy(
                    grouped[s][:, k * BANK : (k + 1) * BANK].bitcast(F32).rearrange("p (c u) -> p c u", u=2),
                    back[:, 0 : 2 * P].rearrange("p (u c) -> p c u", u=2),
                )

        av, at, gates, diff, base, mixed = {}, {}, {}, {}, {}, {}

        def operands(h):
            js = slice(h * HALF, (h + 1) * HALF)
            fp4 = [(v2_w[h][:, a, :].bitcast(FP4X4), planes[:, a, 0, js]) for a in range(2)]
            return fp4 + [(v_w[h][:].bitcast(FP8X4), planes[:, 0, 1, js])]

        def tile_operands(h, c):
            js = slice(h * HALF + c * P, h * HALF + (c + 1) * P)
            fp4 = [(v2_w[h][:, a, 2 * c * P : 2 * (c + 1) * P].bitcast(FP4X4), planes[:, a, 0, js]) for a in range(2)]
            return fp4 + [(v_w[h][:, c * P : (c + 1) * P].bitcast(FP8X4), planes[:, 0, 1, js])]

        def product(out, words, scales, h, passes):
            for a in passes:
                nc.tensor.matmul_mx(
                    out[:], words[:, a].bitcast(FP8X4), scales[:, a], *operands(h)[a], start=(a == passes[0]), stop=(a == passes[-1])
                )

        def turned_product(out, s, h, passes):
            for c in range(TILES):
                for a in passes:
                    nc.tensor.matmul_mx(
                        out[:, c * P : (c + 1) * P], *tile_operands(h, c)[a],
                        w_w[s][:, a].bitcast(FP8X4), w_s[:, a, s * P : (s + 1) * P],
                        start=(a == passes[0]), stop=(a == passes[-1]),
                    )

        def hidden(step):
            s, h = STEPS[step]
            ht = bank(HT_BANK, "ht")
            hv = bank(HV_BANK, "hv")
            if step:
                turned_product(ht, s, h, (0, 1))
                turned_product(hv, s, h, (2,))
            else:
                product(ht, w_w[s], w_s[:, :, s * P : (s + 1) * P], h, (0, 1))
                product(hv, w_w[s], w_s[:, :, s * P : (s + 1) * P], h, (2,))
            av[step] = sbuf("av%d" % step, [P, HALF], F32)
            if step + 1 < len(STEPS):
                at[step] = sbuf("at%d" % step, [P, HALF], F32)
            else:
                at[step] = placed("at%d" % step, [P, HALF], F32, LATE_AT)
            nc.scalar.activation(at[step][:], ht[:], ACT.Silu, bias=no_bias[:])
            nc.scalar.activation(av[step][:], hv[:], ACT.Silu, bias=no_bias[:])

        def gate(step):
            s, h = STEPS[step]
            gates[step] = sbuf("gate%d" % step, [P, HALF], F32)
            z = bank(Z_BANK, "z")
            product(z, z_w[s], z_s[s], h, (0, 1, 2))
            nc.scalar.activation(gates[step][:], z[:], ACT.Tanh, bias=half_b[:, s : s + 1], scale=0.5)

        def turn_sum(out, terms):
            for c in range(TILES):
                cs = slice(c * P, (c + 1) * P)
                for number, term in enumerate(terms):
                    nc.tensor.matmul(
                        out[:, cs], term[:, cs], ident[:], is_transpose=True, start=(number == 0), stop=(number == len(terms) - 1)
                    )

        def front(step):
            s, h = STEPS[step]
            hidden(step)
            if step < WEIGHED_FROM:
                less = sbuf("less%d" % step, [P, HALF], F32)
                nc.scalar.mul(less[:], at[step][:], -1.0)
                kept = at[step]
            else:
                for side, term in ((1, at[step]), (0, av[step])):
                    for c in range(TILES):
                        cs = slice(c * P, (c + 1) * P)
                        nc.scalar.activation(term[:, cs], term[:, cs], ACT.Copy, scale=half_w[side][:, TILES * h + c : TILES * h + c + 1])
                less = kept = at[step]
            gate(step)
            diff[step] = bank(DIFF_BANKS[step % 2], "diff")
            turn_sum(diff[step], (less, av[step]))
            base[step] = bank(BASE_BANKS[step % 2], "base")
            turn_sum(base[step], (kept,))

        def weigh(step, tile=None):
            tanh = gates[step]
            gates[step] = tile or tanh
            nc.vector.scalar_tensor_tensor(gates[step][:], tanh[:], 1.0, diff[step][:], ALU.add, ALU.mult)

        def join(step, after):
            mixed[step] = sbuf("mixed%d" % step, [P, HALF], F32, after)
            if step < WEIGHED_FROM:
                nc.vector.scalar_tensor_tensor(mixed[step][:], gates[step][:], 0.5, base[step][:], ALU.mult, ALU.add)
            else:
                nc.scalar.mul(mixed[step][:], base[step][:], -2.0)

        def scatter(step):
            s, h = STEPS[step]
            window = pages[s][:].indirect(entries(idx, h * HALF, HALF))
            if step < WEIGHED_FROM:
                nc.vector.tensor_tensor(window, mixed[step][:], wgo_sb[:, h * HALF : (h + 1) * HALF], ALU.mult)
            else:
                nc.vector.tensor_tensor(window, mixed[step][:], gates[step][:], ALU.add)
            if h == HALVES - 1:
                if s < len(DEALT_AT):
                    deal_page(s)
                dma(out=out_0[s * P : (s + 1) * P, :], in_=pages[s][:])

        hidden(0)
        gate(0)
        make_z(1)
        diff[0], base[0] = av[0], at[0]
        nc.vector.tensor_tensor(av[0][:], av[0][:], at[0][:], ALU.subtract)
        weigh(0)
        join(0, None)
        scatter(0)
        pages[1] = sbuf("page1", [P, T], F32, "at0")
        clear_page(1)
        front(1)
        turned = bank(ROWS_BANK, "turned")
        nc.tensor.transpose(turned[:, 0:P], wgo_rows[:], ident[:])
        half_w = [sbuf("half_w%d" % side, [P, J // P], F32) for side in range(2)]
        for side, factor in enumerate((0.5, -0.5)):
            nc.scalar.mul(half_w[side][:], turned[:, 0 : J // P], factor)
        weigh(1)
        last = len(STEPS) - 1
        for step in range(1, last):
            front(step + 1)
            if step < 3:
                make_z(step + 1)
            join(step, "av%d" % (step + 1) if HELD_FROM <= step < last - 1 else None)
            if step in (2, 3):
                weigh(step + 1, sbuf("weighed%d" % (step + 1), [P, HALF], F32))
                pages[step] = sbuf("page%d" % step, [P, T], F32, "gate%d" % (step + 1))
                clear_page(step)
            elif step + 1 < last:
                weigh(step + 1)
            else:
                quantise(early_w, 0, 0)
            scatter(step)
            if step + 2 == last:
                round_dealt(0, sbuf("grouped0", [P, T], BF16, "at6"))
                early_w = sbuf("out_w_early", [P, 2, BANK], U32)
        join(last, None)
        mid_ident = placed("mid_ident", [P, P], F32, LATE_AT)
        nc.scalar.copy(mid_ident[:], ident[:])
        round_dealt(1, placed("grouped1", [P, T], BF16, LATE_AT + P))
        grouped[2] = sbuf("grouped2", [P, T], BF16)
        regroup(2, mid_ident, BACK_BANKS, (), (2, 3))
        quantise(early_w, 1, 1)
        store_words(early_w, 0, 2, [nc.sync, nc.sync])
        weigh(last, placed("weighed7", [P, HALF], F32, LATE_AT + P))
        warm = bank(DIFF_BANKS[last % 2], "warm")
        for repeat in range(WARM_PASSES):
            product(warm, z_w[SLICES - 1], z_s[SLICES - 1], HALVES - 1, (2,))
        scatter(last)

        late_w = sbuf("out_w_late", [P, 2, BANK], U32, "mixed7")
        quantise(late_w, 0, 2)
        s = SLICES - 1
        grouped[s] = sbuf("grouped3", [P, T], BF16)
        late_ident = placed("late_ident", [P, P], F32, LATE_AT)
        nc.scalar.copy(late_ident[:], ident[:])
        regroup(s, late_ident, LAST_BACK_BANKS, (1, 3), ())
        for k in range(QUADS):
            ws = slice(k * P, (k + 1) * P)
            nc.vector.quantize_mx(late_w[:, 1, ws].bitcast(FP8X4), out_s[4 * s :, ws], grouped[s][:, k * BANK : (k + 1) * BANK])
        store_words(late_w, s - 1, s + 1, [nc.sync, nc.scalar])
        for g in PORT_ORDER:
            queue = nc.scalar if g // 2 else nc.sync
            queue.dma_start(out=out_2[0][:, g * BANK : (g + 1) * BANK].bitcast(I32), in_=out_s[32 * g : 32 * g + 16].bitcast(I32))
